import numpy as np
import ml_dtypes


def mxq(x, axis, fmt="e4m3"):
    dtype, down = {"e4m3": (ml_dtypes.float8_e4m3fn, 7), "e5m2": (ml_dtypes.float8_e5m2, 14)}[fmt]
    v = np.moveaxis(np.asarray(x, np.float32).astype(ml_dtypes.bfloat16).astype(np.float64), axis, -1)
    blocks = v.reshape(v.shape[:-1] + (-1, 32))
    amax = np.abs(blocks).max(-1, keepdims=True)
    byte = np.maximum(np.where(amax > 0, np.frexp(amax)[1] - 1 + 127, 0) - down, 1)
    scale = np.exp2(byte - 127.0)
    codes = (blocks / scale).astype(np.float32).astype(dtype).astype(np.float64)
    return np.moveaxis((codes * scale).reshape(v.shape), -1, axis)


WIDE = False


def mx_kscale(k):
    if not WIDE:
        return np.ones(k)
    levels = np.array([10, -10, 5, -5, 0])
    if k % 512:
        return np.exp2(np.random.permutation(np.resize(levels, k // 32))).repeat(32)
    a = np.empty((k // 512, 16))
    for p in range(k // 512):
        a[p, :8] = np.random.permutation(np.resize(levels, 8))
        for g in range(8):
            far = levels[np.abs(levels - a[p, g]) >= 10]
            a[p, g + 8] = far[np.random.randint(len(far))]
    return np.exp2(a.ravel()).repeat(32)


def f64(x):
    return np.asarray(x).astype(np.float64)


def striped8(idx):
    return np.concatenate([v.reshape(-1, 16).T for v in idx]).astype(np.uint16)


def unstriped8(offs):
    return np.stack([offs[16 * g:16 * g + 16].T.reshape(-1) for g in range(8)]).astype(np.int64)


E2M1 = np.array([0.0, 0.5, 1.0, 1.5, 2.0, 3.0, 4.0, 6.0, -0.0, -0.5, -1.0, -1.5, -2.0, -3.0, -4.0, -6.0])


def pack_weight(w, fmt):
    k, n = w.shape
    w = f64(np.asarray(w, np.float32).astype(ml_dtypes.bfloat16)).reshape(k // 32, 32, n)
    amax = np.abs(w).max(1)
    if fmt == "e4m3":
        byte = np.frexp(amax)[1] - 1 + 127 - 7
    else:
        mant, ex = np.frexp(amax / 6.0)
        byte = np.where(mant > 0.5, ex, ex - 1) + 127
    byte = np.clip(np.where(amax > 0, byte, 1), 1, 254)
    scaled = (w * np.exp2(127.0 - byte)[:, None, :]).reshape(k, n).astype(np.float32)
    by_word = np.ascontiguousarray(scaled.reshape(k // 512, 128, 4, n).transpose(0, 1, 3, 2))
    if fmt == "e4m3":
        words = by_word.astype(ml_dtypes.float8_e4m3fn).view(np.uint8)
    else:
        c = by_word.astype(ml_dtypes.float4_e2m1fn).view(np.uint8) & 0xF
        words = (c[..., 0::2] | (c[..., 1::2] << 4)).reshape(k // 512, 128, 2 * n)
    return np.ascontiguousarray(words), np.ascontiguousarray(byte.astype(np.uint8).reshape(k // 512, 16, n))


def unpack_weight(words, scales, fmt):
    g, _, n = scales.shape
    words = np.ascontiguousarray(words).reshape(g, 128, n, -1)
    if fmt == "e4m3":
        vals = words.view(ml_dtypes.float8_e4m3fn).astype(np.float64)
    else:
        nib = np.empty((g, 128, n, 4), np.uint8)
        nib[..., 0::2] = words & 0xF
        nib[..., 1::2] = words >> 4
        vals = E2M1[nib]
    vals = vals * np.repeat(np.exp2(scales.astype(np.float64) - 127.0), 8, axis=1)[..., None]
    return vals.transpose(0, 1, 3, 2).reshape(g * 512, n)


K, H, M, T, S = 512, 1024, 512, 2048, 1024


def setup_inputs():
    n = np.random.standard_normal
    s = mx_kscale(K)[:, None]
    u = mx_kscale(H)[:, None]
    p_w2 = pack_weight(1.4 * n((H, M)) / np.sqrt(H) / u, "e2m1")
    return {
        "xT": (n((K, T)) * s).astype(np.float32),
        "w1": (n((K, H)) / np.sqrt(K) / s * u.T).astype(np.float32),
        "w2_words": p_w2[0],
        "w2_scales": p_w2[1],
        "wgt": np.repeat(np.random.uniform(0.5, 2.0, (8, S)), 16, axis=0).astype(np.float32),
        "offs": striped8(np.stack([np.random.permutation(T)[:S] for _ in range(8)])),
    }


def reference(xT, w1, w2_words, w2_scales, wgt, offs):
    idx = unstriped8(offs)
    group = np.arange(K) % 512 // 64
    xg = f64(wgt)[np.arange(K) // 4 % 128] * f64(xT)[np.arange(K)[:, None], idx[group]]
    xT_ = mxq(xg, 0, "e4m3")
    w1_ = mxq(f64(w1), 0, "e4m3")
    w2_ = unpack_weight(w2_words, w2_scales, "e2m1")
    h_ = mxq(np.maximum(w1_.T @ xT_, 0.0), 0, "e4m3")
    y = h_.T @ w2_
    return y

@@ -1,0 +1,190 @@
+from contextlib import ExitStack
+
+import concourse.mybir as mybir
+
+K, H, M, T, S = 512, 1024, 512, 2048, 1024
+FLOPS = 2 * K * H * S + 2 * H * M * S
+
+F32 = mybir.dt.float32
+BF16 = mybir.dt.bfloat16
+I32 = mybir.dt.int32
+U32 = mybir.dt.uint32
+U16 = mybir.dt.uint16
+U8 = mybir.dt.uint8
+FP8X4 = mybir.dt.float8_e4m3fn_x4
+FP4X4 = mybir.dt.float4_e2m1fn_x4
+MULT = mybir.AluOpType.mult
+MAX = mybir.AluOpType.max
+RELU = mybir.ActivationFunctionType.Relu
+COPY = mybir.ActivationFunctionType.Copy
+
+P = 128
+PACK = 4
+PASS = P * PACK
+PASSES = H // PASS
+TILE = 128
+TILES = S // TILE
+CHUNK = 256
+CHUNKS = S // CHUNK
+HALF = 512
+
+
+def tile_list_hmlp_tm_none_kernel(tc, xT, w1, w2_words, w2_scales, wgt, offs, out):
+    nc = tc.nc
+    with ExitStack() as ctx:
+        keep = ctx.enter_context(tc.tile_pool(name="keep", bufs=1))
+        ring = ctx.enter_context(tc.tile_pool(name="ring", bufs=4))
+        h_psum = ctx.enter_context(tc.psum_pool(name="h_psum", bufs=5))
+        y_psum = ctx.enter_context(tc.psum_pool(name="y_psum", bufs=3))
+
+        offsets = keep.tile([P, S // 16], U16, name="offsets")
+        nc.sync.dma_start(offsets[:], offs)
+        weights = keep.tile([P, S], F32, name="weights")
+        nc.sync.dma_start(weights[:, :HALF], wgt[:, :HALF])
+        x_rows = xT.rearrange("(p i) t -> p i t", i=PACK)
+        planes = []
+        for i in range(PACK):
+            plane = keep.tile([P, T], F32, name=f"plane{i}")
+            nc.sync.dma_start(plane[:], x_rows[:, i, :])
+            planes.append(plane)
+            if i == 0:
+                nc.sync.dma_start(weights[:, HALF:], wgt[:, HALF:])
+        w1_rows = w1.rearrange("(p i) r -> p i r", i=PACK)
+        w1_raw = []
+        for a in range(PASSES):
+            raw = keep.tile([P, PACK, PASS], F32, name=f"w1_raw{a}")
+            nc.sync.dma_start(raw[:], w1_rows[:, :, a * PASS : (a + 1) * PASS])
+            w1_raw.append(raw)
+        w2_codes = keep.tile([P, PASSES, 2 * M], U8, name="w2_codes", align_bytes=64)
+        nc.sync.dma_start(w2_codes[:].bitcast(I32), w2_words.bitcast(I32).rearrange("a p n -> p a n"))
+        w2_plane = keep.tile([P, PASSES, M], U8, name="w2_plane", align_bytes=64)
+        nc.gpsimd.memset(w2_plane[:].bitcast(I32), 0)
+        scale_rows = w2_scales.bitcast(I32).rearrange("a q n -> q a n")
+        for quad in range(4):
+            nc.gpsimd.dma_start(w2_plane[32 * quad : 32 * quad + 4, :, :].bitcast(I32), scale_rows[4 * quad : 4 * quad + 4, :, :])
+
+        warm = keep.tile([P, 8], F32, name="warm")
+        nc.vector.memset(warm[:], 0.0)
+        nc.scalar.activation(warm[:, 0:1], warm[:, 1:2], RELU)
+
+        picked = [keep.tile([P, PACK, HALF], F32, name=f"picked{u}") for u in range(S // HALF)]
+
+        def gather(i, j0, n):
+            nc.vector.tensor_tensor(
+                picked[j0 // HALF][:, i, j0 % HALF : j0 % HALF + n],
+                planes[i][:].indirect(offsets[:, j0 // 16 : (j0 + n) // 16]),
+                weights[:, j0 : j0 + n],
+                MULT,
+            )
+
+        x_bf = [keep.tile([P, HALF * PACK], BF16, name=f"x_bf{u}", align_bytes=64) for u in range(S // HALF)]
+        x_codes = [keep.tile([P, CHUNK], U32, name=f"x_codes{c}", align_bytes=64) for c in range(CHUNKS)]
+        x_scales = [keep.tile([P, CHUNK], U8, name=f"x_scales{c}", align_bytes=64) for c in range(CHUNKS)]
+
+        def round_x(j0, n, i0, on_scalar):
+            u, lo = divmod(j0, HALF)
+            src = picked[u][:, i0 : i0 + 2, lo : lo + n].rearrange("p i n -> p n i")
+            dst = x_bf[u][:].rearrange("p (n i) -> p n i", i=PACK)[:, lo : lo + n, i0 : i0 + 2]
+            if on_scalar:
+                nc.scalar.activation(dst, src, COPY)
+            else:
+                nc.vector.tensor_copy(dst, src)
+
+        def quantize_x(c):
+            u, lo = divmod(c * CHUNK, HALF)
+            nc.vector.quantize_mx(x_codes[c][:].bitcast(FP8X4), x_scales[c][:], x_bf[u][:, lo * PACK : (lo + CHUNK) * PACK])
+
+        w1_bf = [keep.tile([P, PASS * PACK], BF16, name=f"w1_bf{a}", align_bytes=64) for a in range(PASSES)]
+        w1_codes = [keep.tile([P, PASS], U32, name=f"w1_codes{a}", align_bytes=64) for a in range(PASSES)]
+        w1_scales = [keep.tile([P, PASS], U8, name=f"w1_scales{a}", align_bytes=64) for a in range(PASSES)]
+
+        def round_w1(a, m0, m1, on_scalar):
+            src = w1_raw[a][:].rearrange("p i (m t) -> p m i t", t=PACK)[:, m0:m1, :, :]
+            dst = w1_bf[a][:].rearrange("p (t m i) -> p m i t", t=PACK, i=PACK)[:, m0:m1, :, :]
+            if on_scalar:
+                nc.scalar.activation(dst, src, COPY)
+            else:
+                nc.vector.tensor_copy(dst, src)
+
+        def quantize_w1(a):
+            nc.vector.quantize_mx(w1_codes[a][:].bitcast(FP8X4), w1_scales[a][:], w1_bf[a][:])
+
+        h_codes = {}
+        h_scales = {}
+        h_bf = {}
+
+        def first_layer(a, b, on_scalar):
+            c, n0 = divmod(b * TILE, CHUNK)
+            acc = h_psum.tile([P, PACK, TILE], F32, name="h_acc")
+            for t in range(PACK):
+                nc.tensor.matmul_mx(
+                    out=acc[:, t, :],
+                    lhsT=w1_codes[a][:, t * P : (t + 1) * P].bitcast(FP8X4),
+                    lhsT_scale=w1_scales[a][:, t * P : (t + 1) * P],
+                    rhs=x_codes[c][:, n0 : n0 + TILE].bitcast(FP8X4),
+                    rhs_scale=x_scales[c][:, n0 : n0 + TILE],
+                    start=True,
+                    stop=True,
+                )
+            h_bf[a, b] = ring.tile([P, TILE * PACK], BF16, name="h_bf", align_bytes=64)
+            dst = h_bf[a, b][:].rearrange("p (n t) -> p n t", t=PACK)
+            src = acc[:].rearrange("p t n -> p n t")
+            if on_scalar:
+                nc.scalar.activation(dst, src, RELU)
+            else:
+                nc.vector.tensor_scalar(dst, src, 0.0, None, MAX)
+
+        def quantize_h(a, b):
+            h_codes[a, b] = keep.tile([P, TILE], U32, name=f"h_codes{a}_{b}", align_bytes=64)
+            h_scales[a, b] = keep.tile([P, TILE], U8, name=f"h_scales{a}_{b}", align_bytes=64)
+            nc.vector.quantize_mx(h_codes[a, b][:].bitcast(FP8X4), h_scales[a, b][:], h_bf[a, b][:])
+
+        def second_layer(b, on_scalar):
+            acc = y_psum.tile([P, M], F32, name="y_acc")
+            for a in range(PASSES):
+                nc.tensor.matmul_mx(
+                    out=acc[:],
+                    lhsT=h_codes[a, b][:].bitcast(FP8X4),
+                    lhsT_scale=h_scales[a, b][:],
+                    rhs=w2_codes[:, a, :].bitcast(FP4X4),
+                    rhs_scale=w2_plane[:, a, :],
+                    start=(a == 0),
+                    stop=(a == PASSES - 1),
+                )
+            y = ring.tile([P, M], F32, name="y")
+            if on_scalar:
+                nc.scalar.copy(y[:], acc[:])
+            else:
+                nc.vector.tensor_copy(y[:], acc[:])
+            nc.sync.dma_start(out[b * TILE : (b + 1) * TILE, :], y[:])
+
+        def finish_chunk(c):
+            gather(PACK - 1, c * CHUNK, CHUNK)
+            round_x(c * CHUNK, CHUNK, 2, c < 2)
+            quantize_x(c)
+
+        for i in range(2):
+            for u in range(S // HALF):
+                gather(i, u * HALF, HALF)
+        for u in range(S // HALF):
+            round_x(u * HALF, HALF, 0, True)
+        for u in range(S // HALF):
+            gather(2, u * HALF, HALF)
+        for a in range(PASSES):
+            round_w1(a, 0, 48, True)
+            round_w1(a, 48, 128, False)
+            quantize_w1(a)
+        finish_chunk(0)
+        finish_chunk(1)
+        lead = 2
+        for step in range(TILES + lead):
+            if step < TILES:
+                if step in (2, 4):
+                    finish_chunk(step // 2 + 1)
+                first_layer(0, step, True)
+                quantize_h(0, step)
+            if step >= lead:
+                b = step - lead
+                first_layer(1, b, b % 2 == 1)
+                quantize_h(1, b)
+                second_layer(b, b % 2 == 0)

@@ -33,29 +33,27 @@ def tile_list_hmlp_tm_none_kernel(tc, xT, w1, w2_words, w2_scales, wgt, offs, ou
     nc = tc.nc
     with ExitStack() as ctx:
         keep = ctx.enter_context(tc.tile_pool(name="keep", bufs=1))
-        ring = ctx.enter_context(tc.tile_pool(name="ring", bufs=4))
-        h_psum = ctx.enter_context(tc.psum_pool(name="h_psum", bufs=5))
-        y_psum = ctx.enter_context(tc.psum_pool(name="y_psum", bufs=3))
+        h_psum = ctx.enter_context(tc.psum_pool(name="psum", bufs=8))
+        y_psum = h_psum
+        H_TAG = "bank"
+        Y_TAG = "bank"
 
         offsets = keep.tile([P, S // 16], U16, name="offsets")
-        nc.sync.dma_start(offsets[:], offs)
         weights = keep.tile([P, S], F32, name="weights")
-        nc.sync.dma_start(weights[:, :HALF], wgt[:, :HALF])
         x_rows = xT.rearrange("(p i) t -> p i t", i=PACK)
-        planes = []
-        for i in range(PACK):
-            plane = keep.tile([P, T], F32, name=f"plane{i}")
-            nc.sync.dma_start(plane[:], x_rows[:, i, :])
-            planes.append(plane)
-            if i == 0:
-                nc.sync.dma_start(weights[:, HALF:], wgt[:, HALF:])
+        planes = [keep.tile([P, T], F32, name=f"plane{i}") for i in range(PACK)]
         w1_rows = w1.rearrange("(p i) r -> p i r", i=PACK)
-        w1_raw = []
-        for a in range(PASSES):
-            raw = keep.tile([P, PACK, PASS], F32, name=f"w1_raw{a}")
-            nc.sync.dma_start(raw[:], w1_rows[:, :, a * PASS : (a + 1) * PASS])
-            w1_raw.append(raw)
+        w1_raw = [keep.tile([P, PACK, PASS], F32, name=f"w1_raw{a}") for a in range(PASSES)]
         w2_codes = keep.tile([P, PASSES, 2 * M], U8, name="w2_codes", align_bytes=64)
+        nc.sync.dma_start(offsets[:], offs)
+        nc.sync.dma_start(planes[0][:], x_rows[:, 0, :])
+        nc.sync.dma_start(weights[:, 512:1024], wgt[:, 512:1024])
+        nc.sync.dma_start(weights[:, 0:512], wgt[:, 0:512])
+        nc.sync.dma_start(planes[1][:], x_rows[:, 1, :])
+        nc.sync.dma_start(planes[2][:], x_rows[:, 2, :])
+        nc.sync.dma_start(w1_raw[0][:, :, 0:512], w1_rows[:, :, 0:512])
+        nc.sync.dma_start(planes[3][:], x_rows[:, 3, :])
+        nc.sync.dma_start(w1_raw[1][:, :, 0:512], w1_rows[:, :, 512:1024])
         nc.sync.dma_start(w2_codes[:].bitcast(I32), w2_words.bitcast(I32).rearrange("a p n -> p a n"))
         w2_plane = keep.tile([P, PASSES, M], U8, name="w2_plane", align_bytes=64)
         nc.gpsimd.memset(w2_plane[:].bitcast(I32), 0)
@@ -68,6 +66,24 @@ def tile_list_hmlp_tm_none_kernel(tc, xT, w1, w2_words, w2_scales, wgt, offs, ou
         nc.scalar.activation(warm[:, 0:1], warm[:, 1:2], RELU)
 
         picked = [keep.tile([P, PACK, HALF], F32, name=f"picked{u}") for u in range(S // HALF)]
+        x_bf = [keep.tile([P, HALF * PACK], BF16, name=f"x_bf{u}", align_bytes=64) for u in range(S // HALF)]
+        x_codes = keep.tile([P, S], U32, name="x_codes", align_bytes=64)
+        x_scales = keep.tile([P, S], U8, name="x_scales", align_bytes=64)
+        w1_bf = [keep.tile([P, PASS * PACK], BF16, name=f"w1_bf{a}", align_bytes=64) for a in range(PASSES)]
+        w1_codes = [keep.tile([P, PASS], U32, name=f"w1_codes{a}", align_bytes=64) for a in range(PASSES)]
+        w1_scales = [keep.tile([P, PASS], U8, name=f"w1_scales{a}", align_bytes=64) for a in range(PASSES)]
+        h_bf = [keep.tile([P, PASSES, TILE * PACK], BF16, name=f"h_bf{b}", align_bytes=64) for b in range(TILES)]
+        h_codes = [keep.tile([P, PASSES, TILE], U32, name=f"h_codes{b}", align_bytes=64) for b in range(TILES)]
+        h_scales = [keep.tile([P, PASSES, TILE], U8, name=f"h_scales{b}", align_bytes=64) for b in range(TILES)]
+        y = [keep.tile([P, M], F32, name=f"y{b}") for b in range(TILES)]
+        h_acc = {}
+        y_acc = {}
+
+        def cast(dst, src, on_scalar):
+            if on_scalar:
+                nc.scalar.activation(dst, src, COPY)
+            else:
+                nc.vector.tensor_copy(dst, src)
 
         def gather(i, j0, n):
             nc.vector.tensor_tensor(
@@ -77,114 +93,169 @@ def tile_list_hmlp_tm_none_kernel(tc, xT, w1, w2_words, w2_scales, wgt, offs, ou
                 MULT,
             )
 
-        x_bf = [keep.tile([P, HALF * PACK], BF16, name=f"x_bf{u}", align_bytes=64) for u in range(S // HALF)]
-        x_codes = [keep.tile([P, CHUNK], U32, name=f"x_codes{c}", align_bytes=64) for c in range(CHUNKS)]
-        x_scales = [keep.tile([P, CHUNK], U8, name=f"x_scales{c}", align_bytes=64) for c in range(CHUNKS)]
-
-        def round_x(j0, n, i0, on_scalar):
+        def round_x(j0, n, i0, count, on_scalar):
             u, lo = divmod(j0, HALF)
-            src = picked[u][:, i0 : i0 + 2, lo : lo + n].rearrange("p i n -> p n i")
-            dst = x_bf[u][:].rearrange("p (n i) -> p n i", i=PACK)[:, lo : lo + n, i0 : i0 + 2]
-            if on_scalar:
-                nc.scalar.activation(dst, src, COPY)
+            if count == 2:
+                src = picked[u][:, i0 : i0 + 2, lo : lo + n].rearrange("p i n -> p n i")
+                dst = x_bf[u][:].rearrange("p (n i) -> p n i", i=PACK)[:, lo : lo + n, i0 : i0 + 2]
             else:
-                nc.vector.tensor_copy(dst, src)
+                src = picked[u][:, :, lo : lo + n].rearrange("p i (c e) -> p c i e", e=4)
+                dst = x_bf[u][:, lo * PACK : (lo + n) * PACK].rearrange("p (c e i) -> p c i e", e=4, i=PACK)
+            cast(dst, src, on_scalar)
 
-        def quantize_x(c):
-            u, lo = divmod(c * CHUNK, HALF)
-            nc.vector.quantize_mx(x_codes[c][:].bitcast(FP8X4), x_scales[c][:], x_bf[u][:, lo * PACK : (lo + CHUNK) * PACK])
+        def quantize_x(j0, n):
+            u, lo = divmod(j0, HALF)
+            nc.vector.quantize_mx(x_codes[:, j0 : j0 + n].bitcast(FP8X4), x_scales[:, j0 : j0 + n], x_bf[u][:, lo * PACK : (lo + n) * PACK])
 
-        w1_bf = [keep.tile([P, PASS * PACK], BF16, name=f"w1_bf{a}", align_bytes=64) for a in range(PASSES)]
-        w1_codes = [keep.tile([P, PASS], U32, name=f"w1_codes{a}", align_bytes=64) for a in range(PASSES)]
-        w1_scales = [keep.tile([P, PASS], U8, name=f"w1_scales{a}", align_bytes=64) for a in range(PASSES)]
+        def round_w1(a, t0, m0, n, on_scalar):
+            src = w1_raw[a][:].rearrange("p i (m t) -> p m i t", t=PACK)[:, m0 : m0 + n, :, t0 : t0 + 2]
+            dst = w1_bf[a][:].rearrange("p (t m i) -> p m i t", t=PACK, i=PACK)[:, m0 : m0 + n, :, t0 : t0 + 2]
+            cast(dst, src, on_scalar)
 
-        def round_w1(a, m0, m1, on_scalar):
-            src = w1_raw[a][:].rearrange("p i (m t) -> p m i t", t=PACK)[:, m0:m1, :, :]
-            dst = w1_bf[a][:].rearrange("p (t m i) -> p m i t", t=PACK, i=PACK)[:, m0:m1, :, :]
-            if on_scalar:
-                nc.scalar.activation(dst, src, COPY)
-            else:
-                nc.vector.tensor_copy(dst, src)
+        def quantize_w1(a, t0, n):
+            cols = slice(t0 * P, (t0 + n) * P)
+            nc.vector.quantize_mx(w1_codes[a][:, cols].bitcast(FP8X4), w1_scales[a][:, cols], w1_bf[a][:, t0 * PASS : (t0 + n) * PASS])
 
-        def quantize_w1(a):
-            nc.vector.quantize_mx(w1_codes[a][:].bitcast(FP8X4), w1_scales[a][:], w1_bf[a][:])
-
-        h_codes = {}
-        h_scales = {}
-        h_bf = {}
-
-        def first_layer(a, b, on_scalar):
-            c, n0 = divmod(b * TILE, CHUNK)
-            acc = h_psum.tile([P, PACK, TILE], F32, name="h_acc")
+        def first_layer(a, b):
+            h_acc[a, b] = h_psum.tile([P, PACK, TILE], F32, name="h_acc", tag=H_TAG)
+            tokens = slice(b * TILE, (b + 1) * TILE)
             for t in range(PACK):
                 nc.tensor.matmul_mx(
-                    out=acc[:, t, :],
+                    out=h_acc[a, b][:, t, :],
                     lhsT=w1_codes[a][:, t * P : (t + 1) * P].bitcast(FP8X4),
                     lhsT_scale=w1_scales[a][:, t * P : (t + 1) * P],
-                    rhs=x_codes[c][:, n0 : n0 + TILE].bitcast(FP8X4),
-                    rhs_scale=x_scales[c][:, n0 : n0 + TILE],
+                    rhs=x_codes[:, tokens].bitcast(FP8X4),
+                    rhs_scale=x_scales[:, tokens],
                     start=True,
                     stop=True,
                 )
-            h_bf[a, b] = ring.tile([P, TILE * PACK], BF16, name="h_bf", align_bytes=64)
-            dst = h_bf[a, b][:].rearrange("p (n t) -> p n t", t=PACK)
-            src = acc[:].rearrange("p t n -> p n t")
+
+        def relu(a, b, on_scalar):
+            dst = h_bf[b][:, a, :].rearrange("p (n t) -> p n t", t=PACK)
+            src = h_acc[a, b][:].rearrange("p t n -> p n t")
             if on_scalar:
                 nc.scalar.activation(dst, src, RELU)
             else:
                 nc.vector.tensor_scalar(dst, src, 0.0, None, MAX)
 
-        def quantize_h(a, b):
-            h_codes[a, b] = keep.tile([P, TILE], U32, name=f"h_codes{a}_{b}", align_bytes=64)
-            h_scales[a, b] = keep.tile([P, TILE], U8, name=f"h_scales{a}_{b}", align_bytes=64)
-            nc.vector.quantize_mx(h_codes[a, b][:].bitcast(FP8X4), h_scales[a, b][:], h_bf[a, b][:])
+        def quantize_h(a, b, n):
+            nc.vector.quantize_mx(
+                h_codes[b][:, a : a + n, :].rearrange("p a n -> p (a n)").bitcast(FP8X4),
+                h_scales[b][:, a : a + n, :].rearrange("p a n -> p (a n)"),
+                h_bf[b][:, a : a + n, :].rearrange("p a n -> p (a n)"),
+            )
 
-        def second_layer(b, on_scalar):
-            acc = y_psum.tile([P, M], F32, name="y_acc")
+        def second_layer(b):
+            y_acc[b] = y_psum.tile([P, M], F32, name="y_acc", tag=Y_TAG)
             for a in range(PASSES):
                 nc.tensor.matmul_mx(
-                    out=acc[:],
-                    lhsT=h_codes[a, b][:].bitcast(FP8X4),
-                    lhsT_scale=h_scales[a, b][:],
+                    out=y_acc[b][:],
+                    lhsT=h_codes[b][:, a, :].bitcast(FP8X4),
+                    lhsT_scale=h_scales[b][:, a, :],
                     rhs=w2_codes[:, a, :].bitcast(FP4X4),
                     rhs_scale=w2_plane[:, a, :],
                     start=(a == 0),
                     stop=(a == PASSES - 1),
                 )
-            y = ring.tile([P, M], F32, name="y")
+
+        def store(b, on_scalar):
             if on_scalar:
-                nc.scalar.copy(y[:], acc[:])
+                nc.scalar.copy(y[b][:], y_acc[b][:])
             else:
-                nc.vector.tensor_copy(y[:], acc[:])
-            nc.sync.dma_start(out[b * TILE : (b + 1) * TILE, :], y[:])
+                nc.vector.tensor_copy(y[b][:], y_acc[b][:])
+            nc.sync.dma_start(out[b * TILE : (b + 1) * TILE, :], y[b][:])
 
-        def finish_chunk(c):
-            gather(PACK - 1, c * CHUNK, CHUNK)
-            round_x(c * CHUNK, CHUNK, 2, c < 2)
-            quantize_x(c)
-
-        for i in range(2):
-            for u in range(S // HALF):
-                gather(i, u * HALF, HALF)
-        for u in range(S // HALF):
-            round_x(u * HALF, HALF, 0, True)
-        for u in range(S // HALF):
-            gather(2, u * HALF, HALF)
-        for a in range(PASSES):
-            round_w1(a, 0, 48, True)
-            round_w1(a, 48, 128, False)
-            quantize_w1(a)
-        finish_chunk(0)
-        finish_chunk(1)
-        lead = 2
-        for step in range(TILES + lead):
-            if step < TILES:
-                if step in (2, 4):
-                    finish_chunk(step // 2 + 1)
-                first_layer(0, step, True)
-                quantize_h(0, step)
-            if step >= lead:
-                b = step - lead
-                first_layer(1, b, b % 2 == 1)
-                quantize_h(1, b)
-                second_layer(b, b % 2 == 0)
+        round_w1(0, 2, 0, 64, True)
+        gather(2, 0, 512)
+        round_w1(1, 0, 0, 128, False)
+        round_w1(0, 0, 0, 128, False)
+        quantize_w1(0, 0, 2)
+        gather(3, 0, 256)
+        quantize_w1(1, 0, 2)
+        gather(3, 512, 256)
+        round_w1(1, 2, 64, 64, False)
+        round_x(0, 256, 2, 2, True)
+        gather(1, 0, 512)
+        gather(0, 0, 512)
+        gather(3, 256, 256)
+        gather(1, 512, 512)
+        round_x(256, 256, 2, 2, False)
+        round_x(0, 512, 0, 2, True)
+        quantize_x(256, 256)
+        round_w1(0, 2, 64, 64, False)
+        quantize_x(0, 256)
+        quantize_w1(0, 2, 2)
+        first_layer(0, 2)
+        first_layer(0, 0)
+        round_w1(1, 2, 0, 64, True)
+        first_layer(0, 1)
+        quantize_w1(1, 2, 2)
+        first_layer(1, 1)
+        relu(1, 1, True)
+        gather(0, 512, 512)
+        first_layer(0, 3)
+        relu(0, 1, True)
+        gather(2, 512, 512)
+        relu(0, 3, True)
+        round_x(512, 256, 2, 2, True)
+        round_x(512, 512, 0, 2, True)
+        first_layer(1, 0)
+        quantize_x(512, 256)
+        quantize_h(0, 1, 1)
+        relu(1, 0, True)
+        first_layer(1, 3)
+        relu(0, 0, True)
+        gather(3, 768, 256)
+        round_x(768, 256, 2, 2, False)
+        first_layer(0, 4)
+        relu(0, 2, True)
+        relu(0, 4, False)
+        first_layer(1, 2)
+        quantize_h(0, 0, 1)
+        first_layer(0, 5)
+        quantize_x(768, 256)
+        quantize_h(0, 2, 1)
+        relu(1, 2, True)
+        first_layer(0, 6)
+        relu(1, 3, False)
+        first_layer(1, 6)
+        quantize_h(1, 1, 1)
+        first_layer(1, 4)
+        quantize_h(1, 0, 1)
+        quantize_h(1, 2, 1)
+        relu(1, 4, False)
+        quantize_h(0, 4, 1)
+        relu(0, 5, True)
+        second_layer(0)
+        second_layer(1)
+        quantize_h(0, 5, 1)
+        relu(1, 6, False)
+        quantize_h(1, 3, 1)
+        second_layer(2)
+        store(0, True)
+        store(1, True)
+        store(2, True)
+        quantize_h(1, 4, 1)
+        relu(0, 6, True)
+        quantize_h(0, 3, 1)
+        first_layer(0, 7)
+        quantize_h(1, 6, 1)
+        first_layer(1, 5)
+        relu(0, 7, False)
+        relu(1, 5, True)
+        first_layer(1, 7)
+        quantize_h(1, 5, 1)
+        quantize_h(0, 6, 1)
+        second_layer(4)
+        second_layer(3)
+        second_layer(6)
+        store(4, False)
+        relu(1, 7, True)
+        second_layer(5)
+        quantize_h(1, 7, 1)
+        quantize_h(0, 7, 1)
+        store(3, True)
+        store(5, False)
+        store(6, False)
+        second_layer(7)
+        store(7, True)

@@ -1,6 +1,7 @@
 from contextlib import ExitStack
 
 import concourse.mybir as mybir
+from concourse.masks import make_identity
 
 K, H, M, T, S = 512, 1024, 512, 2048, 1024
 FLOPS = 2 * K * H * S + 2 * H * M * S
@@ -43,23 +44,23 @@ def tile_list_hmlp_tm_none_kernel(tc, xT, w1, w2_words, w2_scales, wgt, offs, ou
         x_rows = xT.rearrange("(p i) t -> p i t", i=PACK)
         planes = [keep.tile([P, T], F32, name=f"plane{i}") for i in range(PACK)]
         w1_rows = w1.rearrange("(p i) r -> p i r", i=PACK)
-        w1_raw = [keep.tile([P, PACK, PASS], F32, name=f"w1_raw{a}") for a in range(PASSES)]
+        w1_raw = [keep.tile([P, PACK, PASS], F32, name=f"w1_raw{a}", tag=f"w1_raw{a}", align_bytes=64) for a in range(PASSES)]
         w2_codes = keep.tile([P, PASSES, 2 * M], U8, name="w2_codes", align_bytes=64)
-        nc.sync.dma_start(offsets[:], offs)
-        nc.sync.dma_start(planes[0][:], x_rows[:, 0, :])
         nc.sync.dma_start(weights[:, 512:1024], wgt[:, 512:1024])
+        nc.sync.dma_start(planes[0][:], x_rows[:, 0, :])
+        nc.sync.dma_start(offsets[:], offs)
         nc.sync.dma_start(weights[:, 0:512], wgt[:, 0:512])
         nc.sync.dma_start(planes[1][:], x_rows[:, 1, :])
         nc.sync.dma_start(planes[2][:], x_rows[:, 2, :])
-        nc.sync.dma_start(w1_raw[0][:, :, 0:512], w1_rows[:, :, 0:512])
         nc.sync.dma_start(planes[3][:], x_rows[:, 3, :])
+        nc.sync.dma_start(w1_raw[0][:, :, 0:512], w1_rows[:, :, 0:512])
         nc.sync.dma_start(w1_raw[1][:, :, 0:512], w1_rows[:, :, 512:1024])
         nc.sync.dma_start(w2_codes[:].bitcast(I32), w2_words.bitcast(I32).rearrange("a p n -> p a n"))
         w2_plane = keep.tile([P, PASSES, M], U8, name="w2_plane", align_bytes=64)
-        nc.gpsimd.memset(w2_plane[:].bitcast(I32), 0)
+        nc.vector.memset(w2_plane[:].bitcast(I32), 0)
         scale_rows = w2_scales.bitcast(I32).rearrange("a q n -> q a n")
         for quad in range(4):
-            nc.gpsimd.dma_start(w2_plane[32 * quad : 32 * quad + 4, :, :].bitcast(I32), scale_rows[4 * quad : 4 * quad + 4, :, :])
+            nc.sync.dma_start(w2_plane[32 * quad : 32 * quad + 4, :, :].bitcast(I32), scale_rows[4 * quad : 4 * quad + 4, :, :])
 
         warm = keep.tile([P, 8], F32, name="warm")
         nc.vector.memset(warm[:], 0.0)
@@ -72,7 +73,7 @@ def tile_list_hmlp_tm_none_kernel(tc, xT, w1, w2_words, w2_scales, wgt, offs, ou
         w1_bf = [keep.tile([P, PASS * PACK], BF16, name=f"w1_bf{a}", align_bytes=64) for a in range(PASSES)]
         w1_codes = [keep.tile([P, PASS], U32, name=f"w1_codes{a}", align_bytes=64) for a in range(PASSES)]
         w1_scales = [keep.tile([P, PASS], U8, name=f"w1_scales{a}", align_bytes=64) for a in range(PASSES)]
-        h_bf = [keep.tile([P, PASSES, TILE * PACK], BF16, name=f"h_bf{b}", align_bytes=64) for b in range(TILES)]
+        h_bf = []
         h_codes = [keep.tile([P, PASSES, TILE], U32, name=f"h_codes{b}", align_bytes=64) for b in range(TILES)]
         h_scales = [keep.tile([P, PASSES, TILE], U8, name=f"h_scales{b}", align_bytes=64) for b in range(TILES)]
         y = [keep.tile([P, M], F32, name=f"y{b}") for b in range(TILES)]
@@ -131,6 +132,9 @@ def tile_list_hmlp_tm_none_kernel(tc, xT, w1, w2_words, w2_scales, wgt, offs, ou
                 )
 
         def relu(a, b, on_scalar):
+            if not h_bf:
+                h_all = keep.tile([P, TILES, PASSES, TILE * PACK], BF16, name="h_all", tag="w1_raw1", align_bytes=64)
+                h_bf.extend(h_all[:, t, :, :] for t in range(TILES))
             dst = h_bf[b][:, a, :].rearrange("p (n t) -> p n t", t=PACK)
             src = h_acc[a, b][:].rearrange("p t n -> p n t")
             if on_scalar:
@@ -165,97 +169,144 @@ def tile_list_hmlp_tm_none_kernel(tc, xT, w1, w2_words, w2_scales, wgt, offs, ou
                 nc.vector.tensor_copy(y[b][:], y_acc[b][:])
             nc.sync.dma_start(out[b * TILE : (b + 1) * TILE, :], y[b][:])
 
-        round_w1(0, 2, 0, 64, True)
+        def warm_up(j0, count):
+            scratch = h_psum.tile([P, CHUNK], F32, name="scratch", tag=H_TAG)
+            for r in range(count):
+                nc.tensor.matmul_mx(
+                    out=scratch[:],
+                    lhsT=x_codes[:, j0 : j0 + P].bitcast(FP8X4),
+                    lhsT_scale=x_scales[:, j0 : j0 + P],
+                    rhs=x_codes[:, j0 : j0 + CHUNK].bitcast(FP8X4),
+                    rhs_scale=x_scales[:, j0 : j0 + CHUNK],
+                    start=True,
+                    stop=True,
+                )
+
+        def warm_up_w(a):
+            scratch = h_psum.tile([P, CHUNK], F32, name="scratch", tag=H_TAG)
+            for r in range(6):
+                nc.tensor.matmul_mx(
+                    out=scratch[:],
+                    lhsT=w1_codes[a][:, 0:P].bitcast(FP8X4),
+                    lhsT_scale=w1_scales[a][:, 0:P],
+                    rhs=w1_codes[a][:, CHUNK:PASS].bitcast(FP8X4),
+                    rhs_scale=w1_scales[a][:, CHUNK:PASS],
+                    start=True,
+                    stop=True,
+                )
+
+        def second_layer_split(b):
+            for u in range(2):
+                y_acc[b, u] = y_psum.tile([P, 2, P], F32, name="y_half", tag=Y_TAG)
+                for q in range(2):
+                    n0 = (2 * u + q) * P
+                    for a in range(PASSES):
+                        nc.tensor.matmul_mx(
+                            out=y_acc[b, u][:, q, :],
+                            lhsT=h_codes[b][:, a, :].bitcast(FP8X4),
+                            lhsT_scale=h_scales[b][:, a, :],
+                            rhs=w2_codes[:, a, 2 * n0 : 2 * (n0 + P)].bitcast(FP4X4),
+                            rhs_scale=w2_plane[:, a, n0 : n0 + P],
+                            start=(a == 0),
+                            stop=(a == PASSES - 1),
+                        )
+
+        def store_half(b, u, on_scalar):
+            cols = slice(u * 2 * P, (u + 1) * 2 * P)
+            src = y_acc[b, u][:].rearrange("p q n -> p (q n)")
+            if on_scalar:
+                nc.scalar.copy(y[b][:, cols], src)
+            else:
+                nc.vector.tensor_copy(y[b][:, cols], src)
+            nc.sync.dma_start(out[b * TILE : (b + 1) * TILE, cols], y[b][:, cols])
+
+        gather(1, 0, 512)
         gather(2, 0, 512)
-        round_w1(1, 0, 0, 128, False)
+        gather(0, 0, 512)
+        round_x(0, 512, 0, 2, True)
         round_w1(0, 0, 0, 128, False)
-        quantize_w1(0, 0, 2)
         gather(3, 0, 256)
-        quantize_w1(1, 0, 2)
-        gather(3, 512, 256)
+        gather(3, 256, 256)
+        round_w1(0, 2, 64, 64, True)
+        gather(2, 512, 512)
         round_w1(1, 2, 64, 64, False)
         round_x(0, 256, 2, 2, True)
-        gather(1, 0, 512)
-        gather(0, 0, 512)
-        gather(3, 256, 256)
-        gather(1, 512, 512)
-        round_x(256, 256, 2, 2, False)
-        round_x(0, 512, 0, 2, True)
-        quantize_x(256, 256)
-        round_w1(0, 2, 64, 64, False)
+        round_w1(0, 2, 0, 64, True)
         quantize_x(0, 256)
-        quantize_w1(0, 2, 2)
-        first_layer(0, 2)
-        first_layer(0, 0)
-        round_w1(1, 2, 0, 64, True)
-        first_layer(0, 1)
-        quantize_w1(1, 2, 2)
-        first_layer(1, 1)
-        relu(1, 1, True)
-        gather(0, 512, 512)
-        first_layer(0, 3)
-        relu(0, 1, True)
-        gather(2, 512, 512)
-        relu(0, 3, True)
-        round_x(512, 256, 2, 2, True)
-        round_x(512, 512, 0, 2, True)
-        first_layer(1, 0)
-        quantize_x(512, 256)
-        quantize_h(0, 1, 1)
-        relu(1, 0, True)
-        first_layer(1, 3)
-        relu(0, 0, True)
+        warm_up(0, 6)
         gather(3, 768, 256)
+        quantize_w1(0, 2, 2)
+        gather(3, 512, 256)
+        round_x(256, 256, 2, 2, True)
+        round_w1(1, 0, 0, 128, True)
+        quantize_x(256, 256)
         round_x(768, 256, 2, 2, False)
-        first_layer(0, 4)
-        relu(0, 2, True)
-        relu(0, 4, False)
+        round_w1(1, 2, 0, 64, True)
+        round_x(512, 256, 2, 2, False)
+        quantize_w1(1, 0, 2)
+        quantize_w1(0, 0, 2)
+        first_layer(0, 3)
+        relu(0, 3, True)
+        first_layer(0, 1)
+        gather(0, 512, 256)
+        quantize_w1(1, 2, 2)
+        first_layer(0, 0)
+        first_layer(0, 2)
         first_layer(1, 2)
-        quantize_h(0, 0, 1)
-        first_layer(0, 5)
-        quantize_x(768, 256)
-        quantize_h(0, 2, 1)
+        first_layer(1, 0)
+        relu(1, 0, False)
+        gather(0, 768, 256)
         relu(1, 2, True)
-        first_layer(0, 6)
-        relu(1, 3, False)
-        first_layer(1, 6)
-        quantize_h(1, 1, 1)
-        first_layer(1, 4)
+        gather(1, 512, 512)
+        relu(0, 0, False)
+        first_layer(1, 1)
+        round_x(512, 512, 0, 2, True)
+        quantize_h(0, 0, 1)
+        relu(0, 1, True)
+        quantize_x(512, 256)
+        first_layer(0, 4)
+        quantize_x(768, 256)
         quantize_h(1, 0, 1)
-        quantize_h(1, 2, 1)
+        relu(0, 2, False)
+        first_layer(1, 6)
+        first_layer(1, 4)
+        relu(1, 1, True)
+        relu(0, 4, False)
+        quantize_h(0, 1, 2)
+        quantize_h(0, 2, 2)
+        relu(1, 6, True)
         relu(1, 4, False)
-        quantize_h(0, 4, 1)
-        relu(0, 5, True)
+        first_layer(0, 6)
+        first_layer(1, 3)
+        relu(1, 3, False)
         second_layer(0)
-        second_layer(1)
-        quantize_h(0, 5, 1)
-        relu(1, 6, False)
-        quantize_h(1, 3, 1)
-        second_layer(2)
-        store(0, True)
-        store(1, True)
-        store(2, True)
-        quantize_h(1, 4, 1)
-        relu(0, 6, True)
-        quantize_h(0, 3, 1)
-        first_layer(0, 7)
-        quantize_h(1, 6, 1)
         first_layer(1, 5)
-        relu(0, 7, False)
-        relu(1, 5, True)
-        first_layer(1, 7)
-        quantize_h(1, 5, 1)
-        quantize_h(0, 6, 1)
+        first_layer(0, 5)
+        quantize_h(0, 4, 2)
+        first_layer(0, 7)
+        quantize_h(0, 3, 2)
+        relu(0, 5, False)
+        store(0, True)
+        relu(0, 6, True)
+        second_layer(2)
+        store(2, True)
+        second_layer(1)
         second_layer(4)
+        relu(1, 5, True)
+        quantize_h(0, 5, 2)
         second_layer(3)
+        store(4, True)
+        quantize_h(0, 6, 2)
+        first_layer(1, 7)
+        relu(0, 7, False)
+        relu(1, 7, False)
         second_layer(6)
-        store(4, False)
-        relu(1, 7, True)
+        quantize_h(0, 7, 2)
+        store(6, True)
+        store(1, True)
         second_layer(5)
-        quantize_h(1, 7, 1)
-        quantize_h(0, 7, 1)
+        second_layer_split(7)
+        store(5, True)
+        store_half(7, 0, False)
+        store_half(7, 1, False)
         store(3, True)
-        store(5, False)
-        store(6, False)
-        second_layer(7)
-        store(7, True)

@@ -40,16 +40,20 @@ def tile_list_hmlp_tm_none_kernel(tc, xT, w1, w2_words, w2_scales, wgt, offs, ou
         Y_TAG = "bank"
 
         offsets = keep.tile([P, S // 16], U16, name="offsets")
-        weights = keep.tile([P, S], F32, name="weights")
+        weights = keep.tile([P, S], F32, name="weights", align_bytes=64)
         x_rows = xT.rearrange("(p i) t -> p i t", i=PACK)
         planes = [keep.tile([P, T], F32, name=f"plane{i}") for i in range(PACK)]
         w1_rows = w1.rearrange("(p i) r -> p i r", i=PACK)
         w1_raw = [keep.tile([P, PACK, PASS], F32, name=f"w1_raw{a}", tag=f"w1_raw{a}", align_bytes=64) for a in range(PASSES)]
         w2_codes = keep.tile([P, PASSES, 2 * M], U8, name="w2_codes", align_bytes=64)
-        nc.sync.dma_start(weights[:, 512:1024], wgt[:, 512:1024])
+        seeds = keep.tile([P, 64], F32, name="seeds", align_bytes=64)
+        wgt_flat = wgt.rearrange("p s -> (p s)")
+        for quad in range(4):
+            base = (32 * quad + 1) * S
+            rows = wgt_flat[base : base + 32 * (S - 64)].rearrange("(r x) -> r x", x=S - 64)
+            (nc.sync if quad % 2 == 0 else nc.scalar).dma_start(seeds[32 * quad : 32 * quad + 32, :], rows[:, 0:64])
         nc.sync.dma_start(planes[0][:], x_rows[:, 0, :])
         nc.sync.dma_start(offsets[:], offs)
-        nc.sync.dma_start(weights[:, 0:512], wgt[:, 0:512])
         nc.sync.dma_start(planes[1][:], x_rows[:, 1, :])
         nc.sync.dma_start(planes[2][:], x_rows[:, 2, :])
         nc.sync.dma_start(planes[3][:], x_rows[:, 3, :])
@@ -65,6 +69,18 @@ def tile_list_hmlp_tm_none_kernel(tc, xT, w1, w2_words, w2_scales, wgt, offs, ou
         warm = keep.tile([P, 8], F32, name="warm")
         nc.vector.memset(warm[:], 0.0)
         nc.scalar.activation(warm[:, 0:1], warm[:, 1:2], RELU)
+
+        turned = keep.tile([P, 2, 32], F32, name="turned", align_bytes=64)
+        spread = keep.tile([P, S], F32, name="spread", align_bytes=64)
+        for half in range(2):
+            nc.vector.transpose(turned[:, half, :], seeds[:, 32 * half : 32 * half + 32])
+        by_run = turned[:].rearrange("p b (g u) -> p u b g", u=16)
+        spread_v = spread[:].rearrange("p (u b g r) -> p u b g r", b=2, g=2, r=16)
+        nc.vector.tensor_copy(spread_v[:, 8:16], by_run[:, 8:0:-1].unsqueeze(4).to_broadcast([P, 8, 2, 2, 16]))
+        nc.vector.tensor_copy(spread_v[:, 0:1], by_run[:, 0:1].unsqueeze(4).to_broadcast([P, 1, 2, 2, 16]))
+        nc.vector.tensor_copy(spread_v[:, 1:8], by_run[:, 15:8:-1].unsqueeze(4).to_broadcast([P, 7, 2, 2, 16]))
+        nc.vector.transpose(weights[:, 512:1024], spread[:, 512:1024])
+        nc.vector.transpose(weights[:, 0:512], spread[:, 0:512])
 
         picked = [keep.tile([P, PACK, HALF], F32, name=f"picked{u}") for u in range(S // HALF)]
         x_bf = [keep.tile([P, HALF * PACK], BF16, name=f"x_bf{u}", align_bytes=64) for u in range(S // HALF)]

@@ -1,7 +1,6 @@
 from contextlib import ExitStack
 
 import concourse.mybir as mybir
-from concourse.masks import make_identity
 
 K, H, M, T, S = 512, 1024, 512, 2048, 1024
 FLOPS = 2 * K * H * S + 2 * H * M * S
@@ -26,40 +25,31 @@ PASSES = H // PASS
 TILE = 128
 TILES = S // TILE
 CHUNK = 256
-CHUNKS = S // CHUNK
-HALF = 512
+RUN = 64
+FIRST = 256
 
 
 def tile_list_hmlp_tm_none_kernel(tc, xT, w1, w2_words, w2_scales, wgt, offs, out):
     nc = tc.nc
     with ExitStack() as ctx:
         keep = ctx.enter_context(tc.tile_pool(name="keep", bufs=1))
-        h_psum = ctx.enter_context(tc.psum_pool(name="psum", bufs=8))
-        y_psum = h_psum
-        H_TAG = "bank"
-        Y_TAG = "bank"
+        shared = ctx.enter_context(tc.tile_pool(name="shared", bufs=1))
+        psum = ctx.enter_context(tc.psum_pool(name="psum", bufs=8))
 
         offsets = keep.tile([P, S // 16], U16, name="offsets")
         weights = keep.tile([P, S], F32, name="weights", align_bytes=64)
         x_rows = xT.rearrange("(p i) t -> p i t", i=PACK)
-        planes = [keep.tile([P, T], F32, name=f"plane{i}") for i in range(PACK)]
-        w1_rows = w1.rearrange("(p i) r -> p i r", i=PACK)
-        w1_raw = [keep.tile([P, PACK, PASS], F32, name=f"w1_raw{a}", tag=f"w1_raw{a}", align_bytes=64) for a in range(PASSES)]
-        w2_codes = keep.tile([P, PASSES, 2 * M], U8, name="w2_codes", align_bytes=64)
-        seeds = keep.tile([P, 64], F32, name="seeds", align_bytes=64)
+        planes = [keep.tile([P, T], F32, name=f"plane{i}", tag=f"plane{i}", align_bytes=64) for i in range(PACK)]
+        seeds = keep.tile([P, RUN], F32, name="seeds", align_bytes=64)
         wgt_flat = wgt.rearrange("p s -> (p s)")
         for quad in range(4):
             base = (32 * quad + 1) * S
-            rows = wgt_flat[base : base + 32 * (S - 64)].rearrange("(r x) -> r x", x=S - 64)
-            (nc.sync if quad % 2 == 0 else nc.scalar).dma_start(seeds[32 * quad : 32 * quad + 32, :], rows[:, 0:64])
+            rows = wgt_flat[base : base + 32 * (S - RUN)].rearrange("(r x) -> r x", x=S - RUN)
+            (nc.sync if quad % 2 == 0 else nc.scalar).dma_start(seeds[32 * quad : 32 * quad + 32, :], rows[:, 0:RUN])
         nc.sync.dma_start(planes[0][:], x_rows[:, 0, :])
         nc.sync.dma_start(offsets[:], offs)
-        nc.sync.dma_start(planes[1][:], x_rows[:, 1, :])
-        nc.sync.dma_start(planes[2][:], x_rows[:, 2, :])
-        nc.sync.dma_start(planes[3][:], x_rows[:, 3, :])
-        nc.sync.dma_start(w1_raw[0][:, :, 0:512], w1_rows[:, :, 0:512])
-        nc.sync.dma_start(w1_raw[1][:, :, 0:512], w1_rows[:, :, 512:1024])
-        nc.sync.dma_start(w2_codes[:].bitcast(I32), w2_words.bitcast(I32).rearrange("a p n -> p a n"))
+        for i in range(1, PACK):
+            nc.sync.dma_start(planes[i][:], x_rows[:, i, :])
         w2_plane = keep.tile([P, PASSES, M], U8, name="w2_plane", align_bytes=64)
         nc.vector.memset(w2_plane[:].bitcast(I32), 0)
         scale_rows = w2_scales.bitcast(I32).rearrange("a q n -> q a n")
@@ -76,20 +66,23 @@ def tile_list_hmlp_tm_none_kernel(tc, xT, w1, w2_words, w2_scales, wgt, offs, ou
             nc.vector.transpose(turned[:, half, :], seeds[:, 32 * half : 32 * half + 32])
         by_run = turned[:].rearrange("p b (g u) -> p u b g", u=16)
         spread_v = spread[:].rearrange("p (u b g r) -> p u b g r", b=2, g=2, r=16)
-        nc.vector.tensor_copy(spread_v[:, 8:16], by_run[:, 8:0:-1].unsqueeze(4).to_broadcast([P, 8, 2, 2, 16]))
         nc.vector.tensor_copy(spread_v[:, 0:1], by_run[:, 0:1].unsqueeze(4).to_broadcast([P, 1, 2, 2, 16]))
         nc.vector.tensor_copy(spread_v[:, 1:8], by_run[:, 15:8:-1].unsqueeze(4).to_broadcast([P, 7, 2, 2, 16]))
-        nc.vector.transpose(weights[:, 512:1024], spread[:, 512:1024])
+        nc.vector.tensor_copy(spread_v[:, 8:16], by_run[:, 8:0:-1].unsqueeze(4).to_broadcast([P, 8, 2, 2, 16]))
         nc.vector.transpose(weights[:, 0:512], spread[:, 0:512])
+        nc.vector.transpose(weights[:, 512:1024], spread[:, 512:1024])
 
-        picked = [keep.tile([P, PACK, HALF], F32, name=f"picked{u}") for u in range(S // HALF)]
-        x_bf = [keep.tile([P, HALF * PACK], BF16, name=f"x_bf{u}", align_bytes=64) for u in range(S // HALF)]
+        raw_bytes = PACK * PASS * 4
+        early_first = shared.tile([P, 2, FIRST], F32, name="early_first", align_bytes=64, offset=raw_bytes - 64)
+        early_rest = keep.tile([P, 2, S - FIRST], F32, name="early_rest")
+        late = keep.tile([P, 2, S], F32, name="late")
+        x_bf = keep.tile([P, S * PACK], BF16, name="x_bf", align_bytes=64)
         x_codes = keep.tile([P, S], U32, name="x_codes", align_bytes=64)
         x_scales = keep.tile([P, S], U8, name="x_scales", align_bytes=64)
         w1_bf = [keep.tile([P, PASS * PACK], BF16, name=f"w1_bf{a}", align_bytes=64) for a in range(PASSES)]
         w1_codes = [keep.tile([P, PASS], U32, name=f"w1_codes{a}", align_bytes=64) for a in range(PASSES)]
         w1_scales = [keep.tile([P, PASS], U8, name=f"w1_scales{a}", align_bytes=64) for a in range(PASSES)]
-        h_bf = []
+        h_bf = [keep.tile([P, PASSES, TILE * PACK], BF16, name=f"h_bf{b}", align_bytes=64) for b in range(TILES)]
         h_codes = [keep.tile([P, PASSES, TILE], U32, name=f"h_codes{b}", align_bytes=64) for b in range(TILES)]
         h_scales = [keep.tile([P, PASSES, TILE], U8, name=f"h_scales{b}", align_bytes=64) for b in range(TILES)]
         y = [keep.tile([P, M], F32, name=f"y{b}") for b in range(TILES)]
@@ -102,31 +95,25 @@ def tile_list_hmlp_tm_none_kernel(tc, xT, w1, w2_words, w2_scales, wgt, offs, ou
             else:
                 nc.vector.tensor_copy(dst, src)
 
-        def gather(i, j0, n):
-            nc.vector.tensor_tensor(
-                picked[j0 // HALF][:, i, j0 % HALF : j0 % HALF + n],
-                planes[i][:].indirect(offsets[:, j0 // 16 : (j0 + n) // 16]),
-                weights[:, j0 : j0 + n],
-                MULT,
-            )
+        def gather(i, j0, n, dst):
+            nc.vector.tensor_tensor(dst, planes[i][:].indirect(offsets[:, j0 // 16 : (j0 + n) // 16]), weights[:, j0 : j0 + n], MULT)
 
-        def round_x(j0, n, i0, count, on_scalar):
-            u, lo = divmod(j0, HALF)
-            if count == 2:
-                src = picked[u][:, i0 : i0 + 2, lo : lo + n].rearrange("p i n -> p n i")
-                dst = x_bf[u][:].rearrange("p (n i) -> p n i", i=PACK)[:, lo : lo + n, i0 : i0 + 2]
-            else:
-                src = picked[u][:, :, lo : lo + n].rearrange("p i (c e) -> p c i e", e=4)
-                dst = x_bf[u][:, lo * PACK : (lo + n) * PACK].rearrange("p (c e i) -> p c i e", e=4, i=PACK)
-            cast(dst, src, on_scalar)
+        def round_x(src, j0, n, i0, on_scalar):
+            dst = x_bf[:].rearrange("p (n i) -> p n i", i=PACK)[:, j0 : j0 + n, i0 : i0 + 2]
+            cast(dst, src.rearrange("p i n -> p n i"), on_scalar)
+
+        def gather_late(i, j0, n):
+            gather(i, j0, n, late[:, i - 2, j0 : j0 + n])
+
+        def round_late(j0, n, on_scalar):
+            round_x(late[:, :, j0 : j0 + n], j0, n, 2, on_scalar)
 
         def quantize_x(j0, n):
-            u, lo = divmod(j0, HALF)
-            nc.vector.quantize_mx(x_codes[:, j0 : j0 + n].bitcast(FP8X4), x_scales[:, j0 : j0 + n], x_bf[u][:, lo * PACK : (lo + n) * PACK])
+            nc.vector.quantize_mx(x_codes[:, j0 : j0 + n].bitcast(FP8X4), x_scales[:, j0 : j0 + n], x_bf[:, j0 * PACK : (j0 + n) * PACK])
 
-        def round_w1(a, t0, m0, n, on_scalar):
-            src = w1_raw[a][:].rearrange("p i (m t) -> p m i t", t=PACK)[:, m0 : m0 + n, :, t0 : t0 + 2]
-            dst = w1_bf[a][:].rearrange("p (t m i) -> p m i t", t=PACK, i=PACK)[:, m0 : m0 + n, :, t0 : t0 + 2]
+        def round_w1(a, t0, on_scalar):
+            src = w1_raw[a][:].rearrange("p i (m t) -> p m i t", t=PACK)[:, :, :, t0 : t0 + 2]
+            dst = w1_bf[a][:].rearrange("p (t m i) -> p m i t", t=PACK, i=PACK)[:, :, :, t0 : t0 + 2]
             cast(dst, src, on_scalar)
 
         def quantize_w1(a, t0, n):
@@ -134,7 +121,7 @@ def tile_list_hmlp_tm_none_kernel(tc, xT, w1, w2_words, w2_scales, wgt, offs, ou
             nc.vector.quantize_mx(w1_codes[a][:, cols].bitcast(FP8X4), w1_scales[a][:, cols], w1_bf[a][:, t0 * PASS : (t0 + n) * PASS])
 
         def first_layer(a, b):
-            h_acc[a, b] = h_psum.tile([P, PACK, TILE], F32, name="h_acc", tag=H_TAG)
+            h_acc[a, b] = psum.tile([P, PACK, TILE], F32, name="h_acc", tag="bank")
             tokens = slice(b * TILE, (b + 1) * TILE)
             for t in range(PACK):
                 nc.tensor.matmul_mx(
@@ -148,9 +135,6 @@ def tile_list_hmlp_tm_none_kernel(tc, xT, w1, w2_words, w2_scales, wgt, offs, ou
                 )
 
         def relu(a, b, on_scalar):
-            if not h_bf:
-                h_all = keep.tile([P, TILES, PASSES, TILE * PACK], BF16, name="h_all", tag="w1_raw1", align_bytes=64)
-                h_bf.extend(h_all[:, t, :, :] for t in range(TILES))
             dst = h_bf[b][:, a, :].rearrange("p (n t) -> p n t", t=PACK)
             src = h_acc[a, b][:].rearrange("p t n -> p n t")
             if on_scalar:
@@ -166,7 +150,7 @@ def tile_list_hmlp_tm_none_kernel(tc, xT, w1, w2_words, w2_scales, wgt, offs, ou
             )
 
         def second_layer(b):
-            y_acc[b] = y_psum.tile([P, M], F32, name="y_acc", tag=Y_TAG)
+            y_acc[b] = psum.tile([P, M], F32, name="y_acc", tag="bank")
             for a in range(PASSES):
                 nc.tensor.matmul_mx(
                     out=y_acc[b][:],
@@ -185,47 +169,33 @@ def tile_list_hmlp_tm_none_kernel(tc, xT, w1, w2_words, w2_scales, wgt, offs, ou
                 nc.vector.tensor_copy(y[b][:], y_acc[b][:])
             nc.sync.dma_start(out[b * TILE : (b + 1) * TILE, :], y[b][:])
 
-        def warm_up(j0, count):
-            scratch = h_psum.tile([P, CHUNK], F32, name="scratch", tag=H_TAG)
+        def warm_up(codes, scales, count):
+            scratch = psum.tile([P, CHUNK], F32, name="scratch", tag="bank")
             for r in range(count):
                 nc.tensor.matmul_mx(
                     out=scratch[:],
-                    lhsT=x_codes[:, j0 : j0 + P].bitcast(FP8X4),
-                    lhsT_scale=x_scales[:, j0 : j0 + P],
-                    rhs=x_codes[:, j0 : j0 + CHUNK].bitcast(FP8X4),
-                    rhs_scale=x_scales[:, j0 : j0 + CHUNK],
+                    lhsT=codes[:, 0:P].bitcast(FP8X4),
+                    lhsT_scale=scales[:, 0:P],
+                    rhs=codes[:, 0:CHUNK].bitcast(FP8X4),
+                    rhs_scale=scales[:, 0:CHUNK],
                     start=True,
                     stop=True,
                 )
 
-        def warm_up_w(a):
-            scratch = h_psum.tile([P, CHUNK], F32, name="scratch", tag=H_TAG)
-            for r in range(6):
-                nc.tensor.matmul_mx(
-                    out=scratch[:],
-                    lhsT=w1_codes[a][:, 0:P].bitcast(FP8X4),
-                    lhsT_scale=w1_scales[a][:, 0:P],
-                    rhs=w1_codes[a][:, CHUNK:PASS].bitcast(FP8X4),
-                    rhs_scale=w1_scales[a][:, CHUNK:PASS],
-                    start=True,
-                    stop=True,
-                )
-
-        def second_layer_split(b):
-            for u in range(2):
-                y_acc[b, u] = y_psum.tile([P, 2, P], F32, name="y_half", tag=Y_TAG)
-                for q in range(2):
-                    n0 = (2 * u + q) * P
-                    for a in range(PASSES):
-                        nc.tensor.matmul_mx(
-                            out=y_acc[b, u][:, q, :],
-                            lhsT=h_codes[b][:, a, :].bitcast(FP8X4),
-                            lhsT_scale=h_scales[b][:, a, :],
-                            rhs=w2_codes[:, a, 2 * n0 : 2 * (n0 + P)].bitcast(FP4X4),
-                            rhs_scale=w2_plane[:, a, n0 : n0 + P],
-                            start=(a == 0),
-                            stop=(a == PASSES - 1),
-                        )
+        def second_layer_half(b, u):
+            y_acc[b, u] = psum.tile([P, 2, P], F32, name="y_half", tag="bank")
+            for q in range(2):
+                n0 = (2 * u + q) * P
+                for a in range(PASSES):
+                    nc.tensor.matmul_mx(
+                        out=y_acc[b, u][:, q, :],
+                        lhsT=h_codes[b][:, a, :].bitcast(FP8X4),
+                        lhsT_scale=h_scales[b][:, a, :],
+                        rhs=w2_codes[:, a, 2 * n0 : 2 * (n0 + P)].bitcast(FP4X4),
+                        rhs_scale=w2_plane[:, a, n0 : n0 + P],
+                        start=(a == 0),
+                        stop=(a == PASSES - 1),
+                    )
 
         def store_half(b, u, on_scalar):
             cols = slice(u * 2 * P, (u + 1) * 2 * P)
@@ -236,93 +206,94 @@ def tile_list_hmlp_tm_none_kernel(tc, xT, w1, w2_words, w2_scales, wgt, offs, ou
                 nc.vector.tensor_copy(y[b][:, cols], src)
             nc.sync.dma_start(out[b * TILE : (b + 1) * TILE, cols], y[b][:, cols])
 
-        gather(1, 0, 512)
-        gather(2, 0, 512)
-        gather(0, 0, 512)
-        round_x(0, 512, 0, 2, True)
-        round_w1(0, 0, 0, 128, False)
-        gather(3, 0, 256)
-        gather(3, 256, 256)
-        round_w1(0, 2, 64, 64, True)
-        gather(2, 512, 512)
-        round_w1(1, 2, 64, 64, False)
-        round_x(0, 256, 2, 2, True)
-        round_w1(0, 2, 0, 64, True)
-        quantize_x(0, 256)
-        warm_up(0, 6)
-        gather(3, 768, 256)
-        quantize_w1(0, 2, 2)
-        gather(3, 512, 256)
-        round_x(256, 256, 2, 2, True)
-        round_w1(1, 0, 0, 128, True)
-        quantize_x(256, 256)
-        round_x(768, 256, 2, 2, False)
-        round_w1(1, 2, 0, 64, True)
-        round_x(512, 256, 2, 2, False)
+        for i in range(2):
+            gather(i, 0, FIRST, early_first[:, i, :])
+            gather(i, FIRST, S - FIRST, early_rest[:, i, :])
+        round_x(early_first[:], 0, FIRST, 0, True)
+        w1_rows = w1.rearrange("(p i) r -> p i r", i=PACK)
+        w1_raw = [shared.tile([P, PACK, PASS], F32, name=f"w1_raw{a}", align_bytes=64, offset=a * raw_bytes) for a in range(PASSES)]
+        for a in range(PASSES):
+            nc.gpsimd.dma_start(w1_raw[a][:], w1_rows[:, :, a * PASS : (a + 1) * PASS])
+        round_x(early_rest[:], FIRST, S - FIRST, 0, True)
+        gather_late(2, 0, S)
+        gather_late(3, 0, 256)
+        round_w1(1, 0, False)
+        round_w1(1, 2, False)
         quantize_w1(1, 0, 2)
+        round_w1(0, 2, True)
+        round_late(0, 256, False)
+        gather_late(3, 512, 256)
+        round_late(512, 256, True)
+        quantize_x(0, 256)
+        quantize_w1(1, 2, 2)
+        round_w1(0, 0, False)
         quantize_w1(0, 0, 2)
+        gather_late(3, 256, 256)
+        gather_late(3, 768, 256)
+        w2_codes = keep.tile([P, PASSES, 2 * M], U8, name="w2_codes", tag="plane3", align_bytes=64)
+        nc.sync.dma_start(w2_codes[:].bitcast(I32), w2_words.bitcast(I32).rearrange("a p n -> p a n"))
+        round_late(768, 256, True)
+        quantize_w1(0, 2, 2)
+        round_late(256, 256, True)
+        quantize_x(768, 256)
+        quantize_x(256, 256)
+        quantize_x(512, 256)
+        warm_up(x_codes, x_scales, 4)
+        first_layer(0, 0)
+        relu(0, 0, True)
+        first_layer(0, 1)
+        relu(0, 1, True)
+        first_layer(0, 2)
+        relu(0, 2, True)
         first_layer(0, 3)
         relu(0, 3, True)
-        first_layer(0, 1)
-        gather(0, 512, 256)
-        quantize_w1(1, 2, 2)
-        first_layer(0, 0)
-        first_layer(0, 2)
-        first_layer(1, 2)
+        first_layer(0, 4)
+        relu(0, 4, True)
+        first_layer(0, 5)
+        relu(0, 5, False)
         first_layer(1, 0)
         relu(1, 0, False)
-        gather(0, 768, 256)
-        relu(1, 2, True)
-        gather(1, 512, 512)
-        relu(0, 0, False)
         first_layer(1, 1)
-        round_x(512, 512, 0, 2, True)
-        quantize_h(0, 0, 1)
-        relu(0, 1, True)
-        quantize_x(512, 256)
-        first_layer(0, 4)
-        quantize_x(768, 256)
-        quantize_h(1, 0, 1)
-        relu(0, 2, False)
-        first_layer(1, 6)
-        first_layer(1, 4)
-        relu(1, 1, True)
-        relu(0, 4, False)
+        relu(1, 1, False)
+        quantize_h(0, 0, 2)
+        first_layer(1, 2)
+        relu(1, 2, True)
         quantize_h(0, 1, 2)
-        quantize_h(0, 2, 2)
-        relu(1, 6, True)
-        relu(1, 4, False)
-        first_layer(0, 6)
         first_layer(1, 3)
-        relu(1, 3, False)
-        second_layer(0)
-        first_layer(1, 5)
-        first_layer(0, 5)
-        quantize_h(0, 4, 2)
-        first_layer(0, 7)
+        relu(1, 3, True)
+        quantize_h(0, 2, 2)
+        first_layer(1, 4)
+        relu(1, 4, True)
         quantize_h(0, 3, 2)
-        relu(0, 5, False)
-        store(0, True)
+        first_layer(1, 5)
+        relu(1, 5, False)
+        quantize_h(0, 4, 2)
+        first_layer(0, 6)
         relu(0, 6, True)
-        second_layer(2)
-        store(2, True)
-        second_layer(1)
-        second_layer(4)
-        relu(1, 5, True)
         quantize_h(0, 5, 2)
-        second_layer(3)
-        store(4, True)
+        first_layer(1, 6)
+        relu(1, 6, False)
+        first_layer(0, 7)
+        relu(0, 7, False)
         quantize_h(0, 6, 2)
         first_layer(1, 7)
-        relu(0, 7, False)
         relu(1, 7, False)
-        second_layer(6)
         quantize_h(0, 7, 2)
-        store(6, True)
+        second_layer(0)
+        store(0, True)
+        second_layer(1)
         store(1, True)
-        second_layer(5)
-        second_layer_split(7)
-        store(5, True)
-        store_half(7, 0, False)
-        store_half(7, 1, False)
+        second_layer(2)
+        store(2, True)
+        second_layer(3)
         store(3, True)
+        second_layer(4)
+        store(4, True)
+        second_layer(5)
+        store(5, True)
+        second_layer(6)
+        store(6, False)
+        second_layer_half(7, 0)
+        second_layer_half(7, 1)
+        store_half(7, 0, False)
+        store_half(7, 1, True)

@@ -212,35 +212,35 @@ def tile_list_hmlp_tm_none_kernel(tc, xT, w1, w2_words, w2_scales, wgt, offs, ou
         round_x(early_first[:], 0, FIRST, 0, True)
         w1_rows = w1.rearrange("(p i) r -> p i r", i=PACK)
         w1_raw = [shared.tile([P, PACK, PASS], F32, name=f"w1_raw{a}", align_bytes=64, offset=a * raw_bytes) for a in range(PASSES)]
-        for a in range(PASSES):
-            nc.gpsimd.dma_start(w1_raw[a][:], w1_rows[:, :, a * PASS : (a + 1) * PASS])
+        nc.scalar.dma_start(w1_raw[0][:], w1_rows[:, :, 0:PASS])
         round_x(early_rest[:], FIRST, S - FIRST, 0, True)
+        nc.scalar.dma_start(w1_raw[1][:], w1_rows[:, :, PASS : 2 * PASS])
         gather_late(2, 0, S)
-        gather_late(3, 0, 256)
-        round_w1(1, 0, False)
-        round_w1(1, 2, False)
-        quantize_w1(1, 0, 2)
-        round_w1(0, 2, True)
-        round_late(0, 256, False)
-        gather_late(3, 512, 256)
-        round_late(512, 256, True)
-        quantize_x(0, 256)
-        quantize_w1(1, 2, 2)
-        round_w1(0, 0, False)
-        quantize_w1(0, 0, 2)
         gather_late(3, 256, 256)
+        gather_late(3, 512, 256)
         gather_late(3, 768, 256)
+        gather_late(3, 0, 256)
         w2_codes = keep.tile([P, PASSES, 2 * M], U8, name="w2_codes", tag="plane3", align_bytes=64)
         nc.sync.dma_start(w2_codes[:].bitcast(I32), w2_words.bitcast(I32).rearrange("a p n -> p a n"))
-        round_late(768, 256, True)
-        quantize_w1(0, 2, 2)
+        round_w1(0, 0, False)
+        round_late(0, 256, False)
+        quantize_w1(0, 0, 2)
+        quantize_x(0, 256)
+        warm_up(w1_codes[0], w1_scales[0], 2)
         round_late(256, 256, True)
-        quantize_x(768, 256)
+        round_w1(0, 2, True)
+        round_late(512, 256, True)
+        round_late(768, 256, True)
+        round_w1(1, 2, True)
         quantize_x(256, 256)
+        quantize_w1(0, 2, 2)
+        round_w1(1, 0, False)
         quantize_x(512, 256)
-        warm_up(x_codes, x_scales, 4)
+        quantize_w1(1, 0, 2)
+        quantize_x(768, 256)
+        quantize_w1(1, 2, 2)
         first_layer(0, 0)
-        relu(0, 0, True)
+        relu(0, 0, False)
         first_layer(0, 1)
         relu(0, 1, True)
         first_layer(0, 2)
@@ -253,29 +253,29 @@ def tile_list_hmlp_tm_none_kernel(tc, xT, w1, w2_words, w2_scales, wgt, offs, ou
         relu(0, 5, False)
         first_layer(1, 0)
         relu(1, 0, False)
+        quantize_h(0, 0, 2)
         first_layer(1, 1)
         relu(1, 1, False)
-        quantize_h(0, 0, 2)
+        quantize_h(0, 1, 2)
         first_layer(1, 2)
         relu(1, 2, True)
-        quantize_h(0, 1, 2)
+        quantize_h(0, 2, 2)
         first_layer(1, 3)
         relu(1, 3, True)
-        quantize_h(0, 2, 2)
+        quantize_h(0, 3, 2)
         first_layer(1, 4)
         relu(1, 4, True)
-        quantize_h(0, 3, 2)
-        first_layer(1, 5)
-        relu(1, 5, False)
         quantize_h(0, 4, 2)
-        first_layer(0, 6)
-        relu(0, 6, True)
+        first_layer(1, 5)
+        relu(1, 5, True)
         quantize_h(0, 5, 2)
+        first_layer(0, 6)
+        relu(0, 6, False)
         first_layer(1, 6)
         relu(1, 6, False)
+        quantize_h(0, 6, 2)
         first_layer(0, 7)
         relu(0, 7, False)
-        quantize_h(0, 6, 2)
         first_layer(1, 7)
         relu(1, 7, False)
         quantize_h(0, 7, 2)

@@ -68,7 +68,7 @@ def tile_list_hmlp_tm_none_kernel(tc, xT, w1, w2_words, w2_scales, wgt, offs, ou
         spread_v = spread[:].rearrange("p (u b g r) -> p u b g r", b=2, g=2, r=16)
         nc.vector.tensor_copy(spread_v[:, 0:1], by_run[:, 0:1].unsqueeze(4).to_broadcast([P, 1, 2, 2, 16]))
         nc.vector.tensor_copy(spread_v[:, 1:8], by_run[:, 15:8:-1].unsqueeze(4).to_broadcast([P, 7, 2, 2, 16]))
-        nc.vector.tensor_copy(spread_v[:, 8:16], by_run[:, 8:0:-1].unsqueeze(4).to_broadcast([P, 8, 2, 2, 16]))
+        nc.scalar.copy(spread_v[:, 8:16], by_run[:, 8:0:-1].unsqueeze(4).to_broadcast([P, 8, 2, 2, 16]))
         nc.vector.transpose(weights[:, 0:512], spread[:, 0:512])
         nc.vector.transpose(weights[:, 512:1024], spread[:, 512:1024])
 
@@ -216,29 +216,29 @@ def tile_list_hmlp_tm_none_kernel(tc, xT, w1, w2_words, w2_scales, wgt, offs, ou
         round_x(early_rest[:], FIRST, S - FIRST, 0, True)
         nc.scalar.dma_start(w1_raw[1][:], w1_rows[:, :, PASS : 2 * PASS])
         gather_late(2, 0, S)
-        gather_late(3, 256, 256)
-        gather_late(3, 512, 256)
-        gather_late(3, 768, 256)
         gather_late(3, 0, 256)
+        gather_late(3, 256, 256)
+        round_late(0, 256, False)
+        gather_late(3, 512, 256)
+        quantize_x(0, 256)
+        warm_up(x_codes, x_scales, 6)
+        round_w1(0, 0, False)
+        gather_late(3, 768, 256)
         w2_codes = keep.tile([P, PASSES, 2 * M], U8, name="w2_codes", tag="plane3", align_bytes=64)
         nc.sync.dma_start(w2_codes[:].bitcast(I32), w2_words.bitcast(I32).rearrange("a p n -> p a n"))
-        round_w1(0, 0, False)
-        round_late(0, 256, False)
-        quantize_w1(0, 0, 2)
-        quantize_x(0, 256)
-        warm_up(w1_codes[0], w1_scales[0], 2)
         round_late(256, 256, True)
         round_w1(0, 2, True)
         round_late(512, 256, True)
-        round_late(768, 256, True)
         round_w1(1, 2, True)
+        round_late(768, 256, True)
+        quantize_w1(0, 0, 2)
         quantize_x(256, 256)
         quantize_w1(0, 2, 2)
         round_w1(1, 0, False)
         quantize_x(512, 256)
         quantize_w1(1, 0, 2)
-        quantize_x(768, 256)
         quantize_w1(1, 2, 2)
+        quantize_x(768, 256)
         first_layer(0, 0)
         relu(0, 0, False)
         first_layer(0, 1)
@@ -274,15 +274,15 @@ def tile_list_hmlp_tm_none_kernel(tc, xT, w1, w2_words, w2_scales, wgt, offs, ou
         first_layer(1, 6)
         relu(1, 6, False)
         quantize_h(0, 6, 2)
+        second_layer(0)
+        store(0, True)
         first_layer(0, 7)
         relu(0, 7, False)
+        second_layer(1)
+        store(1, True)
         first_layer(1, 7)
         relu(1, 7, False)
         quantize_h(0, 7, 2)
-        second_layer(0)
-        store(0, True)
-        second_layer(1)
-        store(1, True)
         second_layer(2)
         store(2, True)
         second_layer(3)

@@ -19,14 +19,21 @@ RELU = mybir.ActivationFunctionType.Relu
 COPY = mybir.ActivationFunctionType.Copy
 
 P = 128
+QUAD = 32
+GROUP = 16
 PACK = 4
+PAIR = 2
 PASS = P * PACK
 PASSES = H // PASS
 TILE = 128
 TILES = S // TILE
 CHUNK = 256
-RUN = 64
-FIRST = 256
+CHUNKS = S // CHUNK
+RUN = S // GROUP
+HALF = S // 2
+RAW_BYTES = PACK * PASS * 4
+WARM_PASSES = 6
+SCALAR_TILES = range(1, 5)
 
 
 def tile_list_hmlp_tm_none_kernel(tc, xT, w1, w2_words, w2_scales, wgt, offs, out):
@@ -36,46 +43,52 @@ def tile_list_hmlp_tm_none_kernel(tc, xT, w1, w2_words, w2_scales, wgt, offs, ou
         shared = ctx.enter_context(tc.tile_pool(name="shared", bufs=1))
         psum = ctx.enter_context(tc.psum_pool(name="psum", bufs=8))
 
-        offsets = keep.tile([P, S // 16], U16, name="offsets")
-        weights = keep.tile([P, S], F32, name="weights", align_bytes=64)
-        x_rows = xT.rearrange("(p i) t -> p i t", i=PACK)
-        planes = [keep.tile([P, T], F32, name=f"plane{i}", tag=f"plane{i}", align_bytes=64) for i in range(PACK)]
         seeds = keep.tile([P, RUN], F32, name="seeds", align_bytes=64)
         wgt_flat = wgt.rearrange("p s -> (p s)")
-        for quad in range(4):
-            base = (32 * quad + 1) * S
-            rows = wgt_flat[base : base + 32 * (S - RUN)].rearrange("(r x) -> r x", x=S - RUN)
-            (nc.sync if quad % 2 == 0 else nc.scalar).dma_start(seeds[32 * quad : 32 * quad + 32, :], rows[:, 0:RUN])
+        for quad in range(P // QUAD):
+            first = (QUAD * quad + 1) * S
+            rows = wgt_flat[first : first + QUAD * (S - RUN)].rearrange("(r x) -> r x", x=S - RUN)
+            queue = nc.sync if quad % 2 == 0 else nc.scalar
+            queue.dma_start(seeds[QUAD * quad : QUAD * (quad + 1), :], rows[:, 0:RUN])
+
+        offsets = keep.tile([P, S // GROUP], U16, name="offsets")
+        x_rows = xT.rearrange("(p i) t -> p i t", i=PACK)
+        planes = [keep.tile([P, T], F32, name=f"plane{i}", tag=f"plane{i}", align_bytes=64) for i in range(PACK)]
         nc.sync.dma_start(planes[0][:], x_rows[:, 0, :])
         nc.sync.dma_start(offsets[:], offs)
         for i in range(1, PACK):
             nc.sync.dma_start(planes[i][:], x_rows[:, i, :])
+
         w2_plane = keep.tile([P, PASSES, M], U8, name="w2_plane", align_bytes=64)
         nc.vector.memset(w2_plane[:].bitcast(I32), 0)
         scale_rows = w2_scales.bitcast(I32).rearrange("a q n -> q a n")
-        for quad in range(4):
-            nc.sync.dma_start(w2_plane[32 * quad : 32 * quad + 4, :, :].bitcast(I32), scale_rows[4 * quad : 4 * quad + 4, :, :])
+        for quad in range(P // QUAD):
+            nc.sync.dma_start(w2_plane[QUAD * quad : QUAD * quad + 4, :, :].bitcast(I32), scale_rows[4 * quad : 4 * quad + 4, :, :])
 
         warm = keep.tile([P, 8], F32, name="warm")
         nc.vector.memset(warm[:], 0.0)
         nc.scalar.activation(warm[:, 0:1], warm[:, 1:2], RELU)
 
-        turned = keep.tile([P, 2, 32], F32, name="turned", align_bytes=64)
+        turned = keep.tile([P, RUN // QUAD, QUAD], F32, name="turned", align_bytes=64)
         spread = keep.tile([P, S], F32, name="spread", align_bytes=64)
-        for half in range(2):
-            nc.vector.transpose(turned[:, half, :], seeds[:, 32 * half : 32 * half + 32])
-        by_run = turned[:].rearrange("p b (g u) -> p u b g", u=16)
-        spread_v = spread[:].rearrange("p (u b g r) -> p u b g r", b=2, g=2, r=16)
-        nc.vector.tensor_copy(spread_v[:, 0:1], by_run[:, 0:1].unsqueeze(4).to_broadcast([P, 1, 2, 2, 16]))
-        nc.vector.tensor_copy(spread_v[:, 1:8], by_run[:, 15:8:-1].unsqueeze(4).to_broadcast([P, 7, 2, 2, 16]))
-        nc.scalar.copy(spread_v[:, 8:16], by_run[:, 8:0:-1].unsqueeze(4).to_broadcast([P, 8, 2, 2, 16]))
-        nc.vector.transpose(weights[:, 0:512], spread[:, 0:512])
-        nc.vector.transpose(weights[:, 512:1024], spread[:, 512:1024])
+        weights = keep.tile([P, S], F32, name="weights", align_bytes=64)
+        for b in range(RUN // QUAD):
+            nc.vector.transpose(turned[:, b, :], seeds[:, QUAD * b : QUAD * (b + 1)])
+        by_source = turned[:].rearrange("p b (g u) -> p u b g", u=GROUP)
+        by_run = spread[:].rearrange("p (v b g r) -> p v b g r", b=RUN // QUAD, g=QUAD // GROUP, r=GROUP)
 
-        raw_bytes = PACK * PASS * 4
-        early_first = shared.tile([P, 2, FIRST], F32, name="early_first", align_bytes=64, offset=raw_bytes - 64)
-        early_rest = keep.tile([P, 2, S - FIRST], F32, name="early_rest")
-        late = keep.tile([P, 2, S], F32, name="late")
+        def repeated(sources, count):
+            return by_source[:, sources].unsqueeze(4).to_broadcast([P, count, RUN // QUAD, QUAD // GROUP, GROUP])
+
+        nc.vector.tensor_copy(by_run[:, 0:1], repeated(slice(0, 1), 1))
+        nc.vector.tensor_copy(by_run[:, 1:8], repeated(slice(15, 8, -1), 7))
+        nc.scalar.copy(by_run[:, 8:16], repeated(slice(8, 0, -1), 8))
+        nc.vector.transpose(weights[:, 0:HALF], spread[:, 0:HALF])
+        nc.vector.transpose(weights[:, HALF:S], spread[:, HALF:S])
+
+        early_first = shared.tile([P, PAIR, CHUNK], F32, name="early_first", align_bytes=64, offset=RAW_BYTES - 64)
+        early_rest = keep.tile([P, PAIR, S - CHUNK], F32, name="early_rest")
+        late = keep.tile([P, PAIR, S], F32, name="late")
         x_bf = keep.tile([P, S * PACK], BF16, name="x_bf", align_bytes=64)
         x_codes = keep.tile([P, S], U32, name="x_codes", align_bytes=64)
         x_scales = keep.tile([P, S], U8, name="x_scales", align_bytes=64)
@@ -86,8 +99,6 @@ def tile_list_hmlp_tm_none_kernel(tc, xT, w1, w2_words, w2_scales, wgt, offs, ou
         h_codes = [keep.tile([P, PASSES, TILE], U32, name=f"h_codes{b}", align_bytes=64) for b in range(TILES)]
         h_scales = [keep.tile([P, PASSES, TILE], U8, name=f"h_scales{b}", align_bytes=64) for b in range(TILES)]
         y = [keep.tile([P, M], F32, name=f"y{b}") for b in range(TILES)]
-        h_acc = {}
-        y_acc = {}
 
         def cast(dst, src, on_scalar):
             if on_scalar:
@@ -96,36 +107,38 @@ def tile_list_hmlp_tm_none_kernel(tc, xT, w1, w2_words, w2_scales, wgt, offs, ou
                 nc.vector.tensor_copy(dst, src)
 
         def gather(i, j0, n, dst):
-            nc.vector.tensor_tensor(dst, planes[i][:].indirect(offsets[:, j0 // 16 : (j0 + n) // 16]), weights[:, j0 : j0 + n], MULT)
+            window = planes[i][:].indirect(offsets[:, j0 // GROUP : (j0 + n) // GROUP])
+            nc.vector.tensor_tensor(dst, window, weights[:, j0 : j0 + n], MULT)
 
         def round_x(src, j0, n, i0, on_scalar):
-            dst = x_bf[:].rearrange("p (n i) -> p n i", i=PACK)[:, j0 : j0 + n, i0 : i0 + 2]
+            dst = x_bf[:].rearrange("p (n i) -> p n i", i=PACK)[:, j0 : j0 + n, i0 : i0 + PAIR]
             cast(dst, src.rearrange("p i n -> p n i"), on_scalar)
 
-        def gather_late(i, j0, n):
-            gather(i, j0, n, late[:, i - 2, j0 : j0 + n])
+        def gather_last_plane(c):
+            gather(PACK - 1, c * CHUNK, CHUNK, late[:, PAIR - 1, c * CHUNK : (c + 1) * CHUNK])
 
-        def round_late(j0, n, on_scalar):
-            round_x(late[:, :, j0 : j0 + n], j0, n, 2, on_scalar)
+        def round_late(c, on_scalar):
+            round_x(late[:, :, c * CHUNK : (c + 1) * CHUNK], c * CHUNK, CHUNK, PAIR, on_scalar)
 
-        def quantize_x(j0, n):
-            nc.vector.quantize_mx(x_codes[:, j0 : j0 + n].bitcast(FP8X4), x_scales[:, j0 : j0 + n], x_bf[:, j0 * PACK : (j0 + n) * PACK])
+        def quantize_x(c):
+            cols = slice(c * CHUNK, (c + 1) * CHUNK)
+            nc.vector.quantize_mx(x_codes[:, cols].bitcast(FP8X4), x_scales[:, cols], x_bf[:, c * CHUNK * PACK : (c + 1) * CHUNK * PACK])
 
         def round_w1(a, t0, on_scalar):
-            src = w1_raw[a][:].rearrange("p i (m t) -> p m i t", t=PACK)[:, :, :, t0 : t0 + 2]
-            dst = w1_bf[a][:].rearrange("p (t m i) -> p m i t", t=PACK, i=PACK)[:, :, :, t0 : t0 + 2]
+            src = w1_raw[a][:].rearrange("p i (m t) -> p m i t", t=PACK)[:, :, :, t0 : t0 + PAIR]
+            dst = w1_bf[a][:].rearrange("p (t m i) -> p m i t", t=PACK, i=PACK)[:, :, :, t0 : t0 + PAIR]
             cast(dst, src, on_scalar)
 
-        def quantize_w1(a, t0, n):
-            cols = slice(t0 * P, (t0 + n) * P)
-            nc.vector.quantize_mx(w1_codes[a][:, cols].bitcast(FP8X4), w1_scales[a][:, cols], w1_bf[a][:, t0 * PASS : (t0 + n) * PASS])
+        def quantize_w1(a, t0):
+            cols = slice(t0 * P, (t0 + PAIR) * P)
+            nc.vector.quantize_mx(w1_codes[a][:, cols].bitcast(FP8X4), w1_scales[a][:, cols], w1_bf[a][:, t0 * PASS : (t0 + PAIR) * PASS])
 
         def first_layer(a, b):
-            h_acc[a, b] = psum.tile([P, PACK, TILE], F32, name="h_acc", tag="bank")
+            acc = psum.tile([P, PACK, TILE], F32, name="h_acc", tag="bank")
             tokens = slice(b * TILE, (b + 1) * TILE)
             for t in range(PACK):
                 nc.tensor.matmul_mx(
-                    out=h_acc[a, b][:, t, :],
+                    out=acc[:, t, :],
                     lhsT=w1_codes[a][:, t * P : (t + 1) * P].bitcast(FP8X4),
                     lhsT_scale=w1_scales[a][:, t * P : (t + 1) * P],
                     rhs=x_codes[:, tokens].bitcast(FP8X4),
@@ -133,167 +146,104 @@ def tile_list_hmlp_tm_none_kernel(tc, xT, w1, w2_words, w2_scales, wgt, offs, ou
                     start=True,
                     stop=True,
                 )
-
-        def relu(a, b, on_scalar):
             dst = h_bf[b][:, a, :].rearrange("p (n t) -> p n t", t=PACK)
-            src = h_acc[a, b][:].rearrange("p t n -> p n t")
-            if on_scalar:
+            src = acc[:].rearrange("p t n -> p n t")
+            if b in SCALAR_TILES:
                 nc.scalar.activation(dst, src, RELU)
             else:
                 nc.vector.tensor_scalar(dst, src, 0.0, None, MAX)
-
-        def quantize_h(a, b, n):
-            nc.vector.quantize_mx(
-                h_codes[b][:, a : a + n, :].rearrange("p a n -> p (a n)").bitcast(FP8X4),
-                h_scales[b][:, a : a + n, :].rearrange("p a n -> p (a n)"),
-                h_bf[b][:, a : a + n, :].rearrange("p a n -> p (a n)"),
-            )
-
-        def second_layer(b):
-            y_acc[b] = psum.tile([P, M], F32, name="y_acc", tag="bank")
-            for a in range(PASSES):
-                nc.tensor.matmul_mx(
-                    out=y_acc[b][:],
-                    lhsT=h_codes[b][:, a, :].bitcast(FP8X4),
-                    lhsT_scale=h_scales[b][:, a, :],
-                    rhs=w2_codes[:, a, :].bitcast(FP4X4),
-                    rhs_scale=w2_plane[:, a, :],
-                    start=(a == 0),
-                    stop=(a == PASSES - 1),
+            if a == PASSES - 1:
+                nc.vector.quantize_mx(
+                    h_codes[b][:].rearrange("p a n -> p (a n)").bitcast(FP8X4),
+                    h_scales[b][:].rearrange("p a n -> p (a n)"),
+                    h_bf[b][:].rearrange("p a n -> p (a n)"),
                 )
 
-        def store(b, on_scalar):
-            if on_scalar:
-                nc.scalar.copy(y[b][:], y_acc[b][:])
-            else:
-                nc.vector.tensor_copy(y[b][:], y_acc[b][:])
-            nc.sync.dma_start(out[b * TILE : (b + 1) * TILE, :], y[b][:])
-
-        def warm_up(codes, scales, count):
-            scratch = psum.tile([P, CHUNK], F32, name="scratch", tag="bank")
-            for r in range(count):
-                nc.tensor.matmul_mx(
-                    out=scratch[:],
-                    lhsT=codes[:, 0:P].bitcast(FP8X4),
-                    lhsT_scale=scales[:, 0:P],
-                    rhs=codes[:, 0:CHUNK].bitcast(FP8X4),
-                    rhs_scale=scales[:, 0:CHUNK],
-                    start=True,
-                    stop=True,
-                )
-
-        def second_layer_half(b, u):
-            y_acc[b, u] = psum.tile([P, 2, P], F32, name="y_half", tag="bank")
-            for q in range(2):
-                n0 = (2 * u + q) * P
+        def second_layer(b, n0, width, step):
+            acc = psum.tile([P, width], F32, name="y_acc", tag="bank")
+            for lo in range(0, width, step):
                 for a in range(PASSES):
                     nc.tensor.matmul_mx(
-                        out=y_acc[b, u][:, q, :],
+                        out=acc[:, lo : lo + step],
                         lhsT=h_codes[b][:, a, :].bitcast(FP8X4),
                         lhsT_scale=h_scales[b][:, a, :],
-                        rhs=w2_codes[:, a, 2 * n0 : 2 * (n0 + P)].bitcast(FP4X4),
-                        rhs_scale=w2_plane[:, a, n0 : n0 + P],
+                        rhs=w2_codes[:, a, 2 * (n0 + lo) : 2 * (n0 + lo + step)].bitcast(FP4X4),
+                        rhs_scale=w2_plane[:, a, n0 + lo : n0 + lo + step],
                         start=(a == 0),
                         stop=(a == PASSES - 1),
                     )
+            return acc
 
-        def store_half(b, u, on_scalar):
-            cols = slice(u * 2 * P, (u + 1) * 2 * P)
-            src = y_acc[b, u][:].rearrange("p q n -> p (q n)")
+        def copy_out(dst, acc, on_scalar):
             if on_scalar:
-                nc.scalar.copy(y[b][:, cols], src)
+                nc.scalar.copy(dst, acc[:])
             else:
-                nc.vector.tensor_copy(y[b][:, cols], src)
-            nc.sync.dma_start(out[b * TILE : (b + 1) * TILE, cols], y[b][:, cols])
+                nc.vector.tensor_copy(dst, acc[:])
 
-        for i in range(2):
-            gather(i, 0, FIRST, early_first[:, i, :])
-            gather(i, FIRST, S - FIRST, early_rest[:, i, :])
-        round_x(early_first[:], 0, FIRST, 0, True)
+        def store(b):
+            nc.sync.dma_start(out[b * TILE : (b + 1) * TILE, :], y[b][:])
+
+        def output_tile(b, on_scalar):
+            copy_out(y[b][:], second_layer(b, 0, M, M), on_scalar)
+            store(b)
+
+        for i in range(PAIR):
+            gather(i, 0, CHUNK, early_first[:, i, :])
+            gather(i, CHUNK, S - CHUNK, early_rest[:, i, :])
+        round_x(early_first[:], 0, CHUNK, 0, True)
         w1_rows = w1.rearrange("(p i) r -> p i r", i=PACK)
-        w1_raw = [shared.tile([P, PACK, PASS], F32, name=f"w1_raw{a}", align_bytes=64, offset=a * raw_bytes) for a in range(PASSES)]
+        w1_raw = [shared.tile([P, PACK, PASS], F32, name=f"w1_raw{a}", align_bytes=64, offset=a * RAW_BYTES) for a in range(PASSES)]
         nc.scalar.dma_start(w1_raw[0][:], w1_rows[:, :, 0:PASS])
-        round_x(early_rest[:], FIRST, S - FIRST, 0, True)
+        round_x(early_rest[:], CHUNK, S - CHUNK, 0, True)
         nc.scalar.dma_start(w1_raw[1][:], w1_rows[:, :, PASS : 2 * PASS])
-        gather_late(2, 0, S)
-        gather_late(3, 0, 256)
-        gather_late(3, 256, 256)
-        round_late(0, 256, False)
-        gather_late(3, 512, 256)
-        quantize_x(0, 256)
-        warm_up(x_codes, x_scales, 6)
+        gather(PAIR, 0, S, late[:, 0, :])
+
+        gather_last_plane(0)
+        gather_last_plane(1)
+        round_late(0, False)
+        gather_last_plane(2)
+        quantize_x(0)
+        scratch = psum.tile([P, CHUNK], F32, name="scratch", tag="bank")
+        for r in range(WARM_PASSES):
+            nc.tensor.matmul_mx(
+                out=scratch[:],
+                lhsT=x_codes[:, 0:P].bitcast(FP8X4),
+                lhsT_scale=x_scales[:, 0:P],
+                rhs=x_codes[:, 0:CHUNK].bitcast(FP8X4),
+                rhs_scale=x_scales[:, 0:CHUNK],
+                start=True,
+                stop=True,
+            )
         round_w1(0, 0, False)
-        gather_late(3, 768, 256)
-        w2_codes = keep.tile([P, PASSES, 2 * M], U8, name="w2_codes", tag="plane3", align_bytes=64)
+        gather_last_plane(CHUNKS - 1)
+
+        w2_codes = keep.tile([P, PASSES, 2 * M], U8, name="w2_codes", tag=f"plane{PACK - 1}", align_bytes=64)
         nc.sync.dma_start(w2_codes[:].bitcast(I32), w2_words.bitcast(I32).rearrange("a p n -> p a n"))
-        round_late(256, 256, True)
-        round_w1(0, 2, True)
-        round_late(512, 256, True)
-        round_w1(1, 2, True)
-        round_late(768, 256, True)
-        quantize_w1(0, 0, 2)
-        quantize_x(256, 256)
-        quantize_w1(0, 2, 2)
+
+        for a in range(PASSES):
+            round_late(a + 1, True)
+            round_w1(a, PAIR, True)
+        round_late(CHUNKS - 1, True)
+        quantize_w1(0, 0)
+        quantize_x(1)
+        quantize_w1(0, PAIR)
         round_w1(1, 0, False)
-        quantize_x(512, 256)
-        quantize_w1(1, 0, 2)
-        quantize_w1(1, 2, 2)
-        quantize_x(768, 256)
-        first_layer(0, 0)
-        relu(0, 0, False)
-        first_layer(0, 1)
-        relu(0, 1, True)
-        first_layer(0, 2)
-        relu(0, 2, True)
-        first_layer(0, 3)
-        relu(0, 3, True)
-        first_layer(0, 4)
-        relu(0, 4, True)
-        first_layer(0, 5)
-        relu(0, 5, False)
-        first_layer(1, 0)
-        relu(1, 0, False)
-        quantize_h(0, 0, 2)
-        first_layer(1, 1)
-        relu(1, 1, False)
-        quantize_h(0, 1, 2)
-        first_layer(1, 2)
-        relu(1, 2, True)
-        quantize_h(0, 2, 2)
-        first_layer(1, 3)
-        relu(1, 3, True)
-        quantize_h(0, 3, 2)
-        first_layer(1, 4)
-        relu(1, 4, True)
-        quantize_h(0, 4, 2)
-        first_layer(1, 5)
-        relu(1, 5, True)
-        quantize_h(0, 5, 2)
-        first_layer(0, 6)
-        relu(0, 6, False)
-        first_layer(1, 6)
-        relu(1, 6, False)
-        quantize_h(0, 6, 2)
-        second_layer(0)
-        store(0, True)
-        first_layer(0, 7)
-        relu(0, 7, False)
-        second_layer(1)
-        store(1, True)
-        first_layer(1, 7)
-        relu(1, 7, False)
-        quantize_h(0, 7, 2)
-        second_layer(2)
-        store(2, True)
-        second_layer(3)
-        store(3, True)
-        second_layer(4)
-        store(4, True)
-        second_layer(5)
-        store(5, True)
-        second_layer(6)
-        store(6, False)
-        second_layer_half(7, 0)
-        second_layer_half(7, 1)
-        store_half(7, 0, False)
-        store_half(7, 1, True)
+        quantize_x(2)
+        quantize_w1(1, 0)
+        quantize_w1(1, PAIR)
+        quantize_x(CHUNKS - 1)
+
+        last = TILES - 1
+        for a in range(PASSES):
+            for b in range(last):
+                first_layer(a, b)
+        first_layer(0, last)
+        output_tile(0, True)
+        first_layer(1, last)
+
+        for b in range(1, last):
+            output_tile(b, b < last - 1)
+        halves = [second_layer(last, u * M // 2, M // 2, P) for u in range(2)]
+        for u in range(2):
+            copy_out(y[last][:, u * M // 2 : (u + 1) * M // 2], halves[u], u == 1)
+        store(last)

@@ -53,21 +53,12 @@ def tile_list_hmlp_tm_none_kernel(tc, xT, w1, w2_words, w2_scales, wgt, offs, ou
 
         offsets = keep.tile([P, S // GROUP], U16, name="offsets")
         x_rows = xT.rearrange("(p i) t -> p i t", i=PACK)
-        planes = [keep.tile([P, T], F32, name=f"plane{i}", tag=f"plane{i}", align_bytes=64) for i in range(PACK)]
+        planes = [keep.tile([P, T], F32, name=f"plane{i}") for i in range(PACK - 1)]
+        planes.append(shared.tile([P, T], F32, name="plane3", align_bytes=64, offset=PASSES * RAW_BYTES))
         nc.sync.dma_start(planes[0][:], x_rows[:, 0, :])
         nc.sync.dma_start(offsets[:], offs)
         for i in range(1, PACK):
             nc.sync.dma_start(planes[i][:], x_rows[:, i, :])
-
-        w2_plane = keep.tile([P, PASSES, M], U8, name="w2_plane", align_bytes=64)
-        nc.vector.memset(w2_plane[:].bitcast(I32), 0)
-        scale_rows = w2_scales.bitcast(I32).rearrange("a q n -> q a n")
-        for quad in range(P // QUAD):
-            nc.sync.dma_start(w2_plane[QUAD * quad : QUAD * quad + 4, :, :].bitcast(I32), scale_rows[4 * quad : 4 * quad + 4, :, :])
-
-        warm = keep.tile([P, 8], F32, name="warm")
-        nc.vector.memset(warm[:], 0.0)
-        nc.scalar.activation(warm[:, 0:1], warm[:, 1:2], RELU)
 
         turned = keep.tile([P, RUN // QUAD, QUAD], F32, name="turned", align_bytes=64)
         spread = keep.tile([P, S], F32, name="spread", align_bytes=64)
@@ -217,21 +208,26 @@ def tile_list_hmlp_tm_none_kernel(tc, xT, w1, w2_words, w2_scales, wgt, offs, ou
         round_w1(0, 0, False)
         gather_last_plane(CHUNKS - 1)
 
-        w2_codes = keep.tile([P, PASSES, 2 * M], U8, name="w2_codes", tag=f"plane{PACK - 1}", align_bytes=64)
+        w2_codes = shared.tile([P, PASSES, 2 * M], U8, name="w2_codes", align_bytes=64, offset=PASSES * RAW_BYTES)
         nc.sync.dma_start(w2_codes[:].bitcast(I32), w2_words.bitcast(I32).rearrange("a p n -> p a n"))
+        w2_plane = shared.tile([P, PASSES, M], U8, name="w2_plane", align_bytes=64, offset=PASSES * RAW_BYTES + PASSES * 2 * M)
+        scale_rows = w2_scales.bitcast(I32).rearrange("a q n -> q a n")
+        for quad in range(P // QUAD):
+            nc.sync.dma_start(w2_plane[QUAD * quad : QUAD * quad + 4, :, :].bitcast(I32), scale_rows[4 * quad : 4 * quad + 4, :, :])
 
-        for a in range(PASSES):
-            round_late(a + 1, True)
-            round_w1(a, PAIR, True)
-        round_late(CHUNKS - 1, True)
+        round_late(1, True)
+        round_w1(0, PAIR, True)
+        for c in range(2, CHUNKS):
+            round_late(c, True)
+        round_w1(1, PAIR, True)
         quantize_w1(0, 0)
         quantize_x(1)
         quantize_w1(0, PAIR)
         round_w1(1, 0, False)
         quantize_x(2)
         quantize_w1(1, 0)
-        quantize_w1(1, PAIR)
         quantize_x(CHUNKS - 1)
+        quantize_w1(1, PAIR)
 
         last = TILES - 1
         for a in range(PASSES):

@@ -33,7 +33,7 @@ RUN = S // GROUP
 HALF = S // 2
 RAW_BYTES = PACK * PASS * 4
 WARM_PASSES = 6
-SCALAR_TILES = range(1, 5)
+SCALAR_TILES = (range(1, 4), range(0, 5))
 
 
 def tile_list_hmlp_tm_none_kernel(tc, xT, w1, w2_words, w2_scales, wgt, offs, out):
@@ -78,8 +78,9 @@ def tile_list_hmlp_tm_none_kernel(tc, xT, w1, w2_words, w2_scales, wgt, offs, ou
         nc.vector.transpose(weights[:, HALF:S], spread[:, HALF:S])
 
         early_first = shared.tile([P, PAIR, CHUNK], F32, name="early_first", align_bytes=64, offset=RAW_BYTES - 64)
-        early_rest = keep.tile([P, PAIR, S - CHUNK], F32, name="early_rest")
-        late = keep.tile([P, PAIR, S], F32, name="late")
+        early_rest = keep.tile([P, PAIR, S - CHUNK], F32, name="early_rest", tag="rest")
+        late_first = keep.tile([P, PAIR, S - CHUNK], F32, name="late_first")
+        late = [late_first[:, :, c * CHUNK : (c + 1) * CHUNK] for c in range(CHUNKS - 1)]
         x_bf = keep.tile([P, S * PACK], BF16, name="x_bf", align_bytes=64)
         x_codes = keep.tile([P, S], U32, name="x_codes", align_bytes=64)
         x_scales = keep.tile([P, S], U8, name="x_scales", align_bytes=64)
@@ -106,10 +107,10 @@ def tile_list_hmlp_tm_none_kernel(tc, xT, w1, w2_words, w2_scales, wgt, offs, ou
             cast(dst, src.rearrange("p i n -> p n i"), on_scalar)
 
         def gather_last_plane(c):
-            gather(PACK - 1, c * CHUNK, CHUNK, late[:, PAIR - 1, c * CHUNK : (c + 1) * CHUNK])
+            gather(PACK - 1, c * CHUNK, CHUNK, late[c][:, PAIR - 1, :])
 
         def round_late(c, on_scalar):
-            round_x(late[:, :, c * CHUNK : (c + 1) * CHUNK], c * CHUNK, CHUNK, PAIR, on_scalar)
+            round_x(late[c], c * CHUNK, CHUNK, PAIR, on_scalar)
 
         def quantize_x(c):
             cols = slice(c * CHUNK, (c + 1) * CHUNK)
@@ -139,7 +140,7 @@ def tile_list_hmlp_tm_none_kernel(tc, xT, w1, w2_words, w2_scales, wgt, offs, ou
                 )
             dst = h_bf[b][:, a, :].rearrange("p (n t) -> p n t", t=PACK)
             src = acc[:].rearrange("p t n -> p n t")
-            if b in SCALAR_TILES:
+            if b in SCALAR_TILES[a]:
                 nc.scalar.activation(dst, src, RELU)
             else:
                 nc.vector.tensor_scalar(dst, src, 0.0, None, MAX)
@@ -187,7 +188,7 @@ def tile_list_hmlp_tm_none_kernel(tc, xT, w1, w2_words, w2_scales, wgt, offs, ou
         nc.scalar.dma_start(w1_raw[0][:], w1_rows[:, :, 0:PASS])
         round_x(early_rest[:], CHUNK, S - CHUNK, 0, True)
         nc.scalar.dma_start(w1_raw[1][:], w1_rows[:, :, PASS : 2 * PASS])
-        gather(PAIR, 0, S, late[:, 0, :])
+        gather(PAIR, 0, S - CHUNK, late_first[:, 0, :])
 
         gather_last_plane(0)
         gather_last_plane(1)
@@ -205,6 +206,9 @@ def tile_list_hmlp_tm_none_kernel(tc, xT, w1, w2_words, w2_scales, wgt, offs, ou
                 start=True,
                 stop=True,
             )
+        late_last = keep.tile([P, PAIR, CHUNK], F32, name="late_last", tag="rest")
+        late.append(late_last[:])
+        gather(PAIR, S - CHUNK, CHUNK, late_last[:, 0, :])
         round_w1(0, 0, False)
         gather_last_plane(CHUNKS - 1)
 

@@ -22,6 +22,7 @@ P = 128
 QUAD = 32
 GROUP = 16
 PACK = 4
+BLOCKS = 4
 PAIR = 2
 PASS = P * PACK
 PASSES = H // PASS
@@ -32,6 +33,7 @@ CHUNKS = S // CHUNK
 RUN = S // GROUP
 HALF = S // 2
 RAW_BYTES = PACK * PASS * 4
+ALIGN = 64
 WARM_PASSES = 6
 SCALAR_TILES = (range(1, 4), range(0, 5))
 
@@ -43,30 +45,36 @@ def tile_list_hmlp_tm_none_kernel(tc, xT, w1, w2_words, w2_scales, wgt, offs, ou
         shared = ctx.enter_context(tc.tile_pool(name="shared", bufs=1))
         psum = ctx.enter_context(tc.psum_pool(name="psum", bufs=8))
 
-        seeds = keep.tile([P, RUN], F32, name="seeds", align_bytes=64)
+        seeds = keep.tile([P, RUN], F32, name="seeds", align_bytes=ALIGN)
         wgt_flat = wgt.rearrange("p s -> (p s)")
         for quad in range(P // QUAD):
             first = (QUAD * quad + 1) * S
-            rows = wgt_flat[first : first + QUAD * (S - RUN)].rearrange("(r x) -> r x", x=S - RUN)
+            steps = wgt_flat[first : first + QUAD * (S - RUN)].rearrange("(p x) -> p x", x=S - RUN)
             queue = nc.sync if quad % 2 == 0 else nc.scalar
-            queue.dma_start(seeds[QUAD * quad : QUAD * (quad + 1), :], rows[:, 0:RUN])
+            queue.dma_start(seeds[QUAD * quad : QUAD * (quad + 1), :], steps[:, 0:RUN])
 
         offsets = keep.tile([P, S // GROUP], U16, name="offsets")
-        x_rows = xT.rearrange("(p i) t -> p i t", i=PACK)
-        planes = [keep.tile([P, T], F32, name=f"plane{i}") for i in range(PACK - 1)]
-        planes.append(shared.tile([P, T], F32, name="plane3", align_bytes=64, offset=PASSES * RAW_BYTES))
+        x_rows = xT.rearrange("(p i) c -> p i c", i=PACK)
+        planes = [keep.tile([P, T], F32, name=f"plane{i}", tag=f"plane{i}", align_bytes=ALIGN) for i in range(PACK)]
         nc.sync.dma_start(planes[0][:], x_rows[:, 0, :])
         nc.sync.dma_start(offsets[:], offs)
         for i in range(1, PACK):
             nc.sync.dma_start(planes[i][:], x_rows[:, i, :])
 
-        turned = keep.tile([P, RUN // QUAD, QUAD], F32, name="turned", align_bytes=64)
-        spread = keep.tile([P, S], F32, name="spread", align_bytes=64)
-        weights = keep.tile([P, S], F32, name="weights", align_bytes=64)
-        for b in range(RUN // QUAD):
-            nc.vector.transpose(turned[:, b, :], seeds[:, QUAD * b : QUAD * (b + 1)])
-        by_source = turned[:].rearrange("p b (g u) -> p u b g", u=GROUP)
-        by_run = spread[:].rearrange("p (v b g r) -> p v b g r", b=RUN // QUAD, g=QUAD // GROUP, r=GROUP)
+        w2_exps = keep.tile([P, PASSES, M], U8, name="w2_exps", align_bytes=ALIGN)
+        nc.vector.memset(w2_exps[:].bitcast(I32), 0)
+        scale_rows = w2_scales.bitcast(I32).rearrange("a q n -> q a n")
+        for quad in range(P // QUAD):
+            rows = slice(BLOCKS * quad, BLOCKS * (quad + 1))
+            nc.sync.dma_start(w2_exps[QUAD * quad : QUAD * quad + BLOCKS, :, :].bitcast(I32), scale_rows[rows, :, :])
+
+        turned = keep.tile([P, RUN // QUAD, QUAD], F32, name="turned", align_bytes=ALIGN)
+        spread = keep.tile([P, S], F32, name="spread", align_bytes=ALIGN)
+        weights = keep.tile([P, S], F32, name="weights", align_bytes=ALIGN)
+        for s in range(RUN // QUAD):
+            nc.vector.transpose(turned[:, s, :], seeds[:, QUAD * s : QUAD * (s + 1)])
+        by_source = turned[:].rearrange("p s (g u) -> p u s g", u=GROUP)
+        by_run = spread[:].rearrange("p (v s g e) -> p v s g e", s=RUN // QUAD, g=QUAD // GROUP, e=GROUP)
 
         def repeated(sources, count):
             return by_source[:, sources].unsqueeze(4).to_broadcast([P, count, RUN // QUAD, QUAD // GROUP, GROUP])
@@ -77,19 +85,19 @@ def tile_list_hmlp_tm_none_kernel(tc, xT, w1, w2_words, w2_scales, wgt, offs, ou
         nc.vector.transpose(weights[:, 0:HALF], spread[:, 0:HALF])
         nc.vector.transpose(weights[:, HALF:S], spread[:, HALF:S])
 
-        early_first = shared.tile([P, PAIR, CHUNK], F32, name="early_first", align_bytes=64, offset=RAW_BYTES - 64)
+        early_first = shared.tile([P, PAIR, CHUNK], F32, name="early_first", align_bytes=ALIGN, offset=RAW_BYTES - ALIGN)
         early_rest = keep.tile([P, PAIR, S - CHUNK], F32, name="early_rest", tag="rest")
         late_first = keep.tile([P, PAIR, S - CHUNK], F32, name="late_first")
         late = [late_first[:, :, c * CHUNK : (c + 1) * CHUNK] for c in range(CHUNKS - 1)]
-        x_bf = keep.tile([P, S * PACK], BF16, name="x_bf", align_bytes=64)
-        x_codes = keep.tile([P, S], U32, name="x_codes", align_bytes=64)
-        x_scales = keep.tile([P, S], U8, name="x_scales", align_bytes=64)
-        w1_bf = [keep.tile([P, PASS * PACK], BF16, name=f"w1_bf{a}", align_bytes=64) for a in range(PASSES)]
-        w1_codes = [keep.tile([P, PASS], U32, name=f"w1_codes{a}", align_bytes=64) for a in range(PASSES)]
-        w1_scales = [keep.tile([P, PASS], U8, name=f"w1_scales{a}", align_bytes=64) for a in range(PASSES)]
-        h_bf = [keep.tile([P, PASSES, TILE * PACK], BF16, name=f"h_bf{b}", align_bytes=64) for b in range(TILES)]
-        h_codes = [keep.tile([P, PASSES, TILE], U32, name=f"h_codes{b}", align_bytes=64) for b in range(TILES)]
-        h_scales = [keep.tile([P, PASSES, TILE], U8, name=f"h_scales{b}", align_bytes=64) for b in range(TILES)]
+        x_bf = keep.tile([P, S * PACK], BF16, name="x_bf", align_bytes=ALIGN)
+        x_codes = keep.tile([P, S], U32, name="x_codes", align_bytes=ALIGN)
+        x_scales = keep.tile([P, S], U8, name="x_scales", align_bytes=ALIGN)
+        w1_bf = [keep.tile([P, PASS * PACK], BF16, name=f"w1_bf{a}", align_bytes=ALIGN) for a in range(PASSES)]
+        w1_codes = [keep.tile([P, PASS], U32, name=f"w1_codes{a}", align_bytes=ALIGN) for a in range(PASSES)]
+        w1_scales = [keep.tile([P, PASS], U8, name=f"w1_scales{a}", align_bytes=ALIGN) for a in range(PASSES)]
+        h_bf = [keep.tile([P, PASSES, TILE * PACK], BF16, name=f"h_bf{b}", align_bytes=ALIGN) for b in range(TILES)]
+        h_codes = [keep.tile([P, PASSES, TILE], U32, name=f"h_codes{b}", align_bytes=ALIGN) for b in range(TILES)]
+        h_scales = [keep.tile([P, PASSES, TILE], U8, name=f"h_scales{b}", align_bytes=ALIGN) for b in range(TILES)]
         y = [keep.tile([P, M], F32, name=f"y{b}") for b in range(TILES)]
 
         def cast(dst, src, on_scalar):
@@ -160,7 +168,7 @@ def tile_list_hmlp_tm_none_kernel(tc, xT, w1, w2_words, w2_scales, wgt, offs, ou
                         lhsT=h_codes[b][:, a, :].bitcast(FP8X4),
                         lhsT_scale=h_scales[b][:, a, :],
                         rhs=w2_codes[:, a, 2 * (n0 + lo) : 2 * (n0 + lo + step)].bitcast(FP4X4),
-                        rhs_scale=w2_plane[:, a, n0 + lo : n0 + lo + step],
+                        rhs_scale=w2_exps[:, a, n0 + lo : n0 + lo + step],
                         start=(a == 0),
                         stop=(a == PASSES - 1),
                     )
@@ -184,7 +192,7 @@ def tile_list_hmlp_tm_none_kernel(tc, xT, w1, w2_words, w2_scales, wgt, offs, ou
             gather(i, CHUNK, S - CHUNK, early_rest[:, i, :])
         round_x(early_first[:], 0, CHUNK, 0, True)
         w1_rows = w1.rearrange("(p i) r -> p i r", i=PACK)
-        w1_raw = [shared.tile([P, PACK, PASS], F32, name=f"w1_raw{a}", align_bytes=64, offset=a * RAW_BYTES) for a in range(PASSES)]
+        w1_raw = [shared.tile([P, PACK, PASS], F32, name=f"w1_raw{a}", align_bytes=ALIGN, offset=a * RAW_BYTES) for a in range(PASSES)]
         nc.scalar.dma_start(w1_raw[0][:], w1_rows[:, :, 0:PASS])
         round_x(early_rest[:], CHUNK, S - CHUNK, 0, True)
         nc.scalar.dma_start(w1_raw[1][:], w1_rows[:, :, PASS : 2 * PASS])
@@ -196,7 +204,7 @@ def tile_list_hmlp_tm_none_kernel(tc, xT, w1, w2_words, w2_scales, wgt, offs, ou
         gather_last_plane(2)
         quantize_x(0)
         scratch = psum.tile([P, CHUNK], F32, name="scratch", tag="bank")
-        for r in range(WARM_PASSES):
+        for repeat in range(WARM_PASSES):
             nc.tensor.matmul_mx(
                 out=scratch[:],
                 lhsT=x_codes[:, 0:P].bitcast(FP8X4),
@@ -212,12 +220,8 @@ def tile_list_hmlp_tm_none_kernel(tc, xT, w1, w2_words, w2_scales, wgt, offs, ou
         round_w1(0, 0, False)
         gather_last_plane(CHUNKS - 1)
 
-        w2_codes = shared.tile([P, PASSES, 2 * M], U8, name="w2_codes", align_bytes=64, offset=PASSES * RAW_BYTES)
+        w2_codes = keep.tile([P, PASSES, 2 * M], U8, name="w2_codes", tag=f"plane{PACK - 1}", align_bytes=ALIGN)
         nc.sync.dma_start(w2_codes[:].bitcast(I32), w2_words.bitcast(I32).rearrange("a p n -> p a n"))
-        w2_plane = shared.tile([P, PASSES, M], U8, name="w2_plane", align_bytes=64, offset=PASSES * RAW_BYTES + PASSES * 2 * M)
-        scale_rows = w2_scales.bitcast(I32).rearrange("a q n -> q a n")
-        for quad in range(P // QUAD):
-            nc.sync.dma_start(w2_plane[QUAD * quad : QUAD * quad + 4, :, :].bitcast(I32), scale_rows[4 * quad : 4 * quad + 4, :, :])
 
         round_late(1, True)
         round_w1(0, PAIR, True)
@@ -243,7 +247,7 @@ def tile_list_hmlp_tm_none_kernel(tc, xT, w1, w2_words, w2_scales, wgt, offs, ou
 
         for b in range(1, last):
             output_tile(b, b < last - 1)
-        halves = [second_layer(last, u * M // 2, M // 2, P) for u in range(2)]
-        for u in range(2):
-            copy_out(y[last][:, u * M // 2 : (u + 1) * M // 2], halves[u], u == 1)
+        sides = [second_layer(last, side * M // 2, M // 2, P) for side in range(2)]
+        for side in range(2):
+            copy_out(y[last][:, side * M // 2 : (side + 1) * M // 2], sides[side], side == 1)
         store(last)

@@ -152,7 +152,9 @@ def tile_list_hmlp_tm_none_kernel(tc, xT, w1, w2_words, w2_scales, wgt, offs, ou
                 nc.scalar.activation(dst, src, RELU)
             else:
                 nc.vector.tensor_scalar(dst, src, 0.0, None, MAX)
-            if a == PASSES - 1:
+            if b == TILES - 1:
+                nc.vector.quantize_mx(h_codes[b][:, a, :].bitcast(FP8X4), h_scales[b][:, a, :], h_bf[b][:, a, :])
+            elif a == PASSES - 1:
                 nc.vector.quantize_mx(
                     h_codes[b][:].rearrange("p a n -> p (a n)").bitcast(FP8X4),
                     h_scales[b][:].rearrange("p a n -> p (a n)"),
@@ -247,7 +249,19 @@ def tile_list_hmlp_tm_none_kernel(tc, xT, w1, w2_words, w2_scales, wgt, offs, ou
 
         for b in range(1, last):
             output_tile(b, b < last - 1)
-        sides = [second_layer(last, side * M // 2, M // 2, P) for side in range(2)]
+        sides = [psum.tile([P, M // 2], F32, name="y_acc", tag="bank") for side in range(2)]
+        for a in range(PASSES):
+            for n0 in range(0, M, P):
+                side, lo = divmod(n0, M // 2)
+                nc.tensor.matmul_mx(
+                    out=sides[side][:, lo : lo + P],
+                    lhsT=h_codes[last][:, a, :].bitcast(FP8X4),
+                    lhsT_scale=h_scales[last][:, a, :],
+                    rhs=w2_codes[:, a, 2 * n0 : 2 * (n0 + P)].bitcast(FP4X4),
+                    rhs_scale=w2_exps[:, a, n0 : n0 + P],
+                    start=(a == 0 and lo == 0),
+                    stop=(a == PASSES - 1 and lo + P == M // 2),
+                )
         for side in range(2):
             copy_out(y[last][:, side * M // 2 : (side + 1) * M // 2], sides[side], side == 1)
         store(last)

@@ -37,6 +37,26 @@ ALIGN = 64
 WARM_PASSES = 6
 SCALAR_TILES = (range(1, 4), range(0, 5))
 
+MSPLIT = None
+WIDE = (0,)
+WC = 0
+ZERO = False
+SEEDS = False
+BFIRST = False
+EA = 256
+G2N = 3
+XH = ()
+XB = ()
+HH = ()
+LOADS = "123"
+GATE = "ef"
+W2 = "a"
+HOLD = "na"
+QA = "s"
+QB = "s"
+WB = "--"
+PLAN = (("G0",), ("G3", 0,), ("G3", 1,), ("RL", 0, 0,), ("G3", 2,), ("QX", 0,), ("WARM",), ("RW", 0, 0, 0,), ("RL", 1, 1,), ("RW", 0, 1, 1,), ("W2",), ("RL", 2, 1,), ("RW", 1, 1, 1,), ("QW", 0, 0,), ("QX", 1,), ("QW", 0, 1,), ("G2", 3,), ("RW", 1, 0, 0,), ("QX", 2,), ("QW", 1, 0,), ("QW", 1, 1,), ("G3", 3,), ("RL", 3, 0,), ("L1", 0, 0, 1,), ("L1", 0, 1, 1,), ("L1", 0, 2, 1,), ("L1", 0, 4, 1,), ("L1", 1, 4, 1,), ("L1", 1, 0, 0,), ("QH", 0, None,), ("QH", 4, None,), ("L1", 1, 2, 1,), ("L1", 1, 1, 1,), ("L1", 0, 3, 1,), ("QX", 3,), ("L1", 0, 5, 1,), ("L1", 1, 5, 1,), ("QH", 1, None,), ("L1", 1, 3, 0,), ("QH", 2, None,), ("QH", 3, None,), ("L1", 0, 6, 1,), ("Y", 0, 0,), ("Y", 4, 0,), ("Y", 2, 1,), ("Y", 1, 1,), ("L1", 1, 6, 0,), ("QH", 5, None,), ("L1", 0, 7, 1,), ("QH", 6, None,), ("Y", 3, 0,), ("L1", 1, 7, 1,), ("QH", 7, 1,), ("QH", 7, 0,), ("Y", 5, 1,), ("Y", 6, 1,), ("YA", 7,), ("YB", 7,),)
+
 
 def tile_list_hmlp_tm_none_kernel(tc, xT, w1, w2_words, w2_scales, wgt, offs, out):
     nc = tc.nc
@@ -50,23 +70,37 @@ def tile_list_hmlp_tm_none_kernel(tc, xT, w1, w2_words, w2_scales, wgt, offs, ou
         for quad in range(P // QUAD):
             first = (QUAD * quad + 1) * S
             steps = wgt_flat[first : first + QUAD * (S - RUN)].rearrange("(p x) -> p x", x=S - RUN)
-            queue = nc.sync if quad % 2 == 0 else nc.scalar
+            queue = nc.sync if (quad % 2 == 0 and not SEEDS) else nc.scalar
             queue.dma_start(seeds[QUAD * quad : QUAD * (quad + 1), :], steps[:, 0:RUN])
 
         offsets = keep.tile([P, S // GROUP], U16, name="offsets")
         x_rows = xT.rearrange("(p i) c -> p i c", i=PACK)
-        planes = [keep.tile([P, T], F32, name=f"plane{i}", tag=f"plane{i}", align_bytes=ALIGN) for i in range(PACK)]
+        planes = [keep.tile([P, T], F32, name=f"plane{i}", tag=f"plane{i}", align_bytes=ALIGN) if (i != 1 or GATE != "p1") else shared.tile([P, T], F32, name="plane1", align_bytes=ALIGN, offset=RAW_BYTES // 2) for i in range(PACK)]
         nc.sync.dma_start(planes[0][:], x_rows[:, 0, :])
         nc.sync.dma_start(offsets[:], offs)
-        for i in range(1, PACK):
-            nc.sync.dma_start(planes[i][:], x_rows[:, i, :])
+        w1_rows = w1.rearrange("(p i) r -> p i r", i=PACK)
+        w1_raw = [None, None]
+        def load_w1(a, q):
+            w1_raw[a] = shared.tile([P, PACK, PASS], F32, name=f"w1_raw{a}", align_bytes=ALIGN, offset=a * RAW_BYTES)
+            q.dma_start(w1_raw[a][:], w1_rows[:, :, a * PASS : (a + 1) * PASS])
+        for ch in LOADS:
+            if ch in "123":
+                nc.sync.dma_start(planes[int(ch)][:], x_rows[:, int(ch), :])
+            else:
+                load_w1("AB".index(ch), nc.sync)
 
-        w2_exps = keep.tile([P, PASSES, M], U8, name="w2_exps", align_bytes=ALIGN)
-        nc.vector.memset(w2_exps[:].bitcast(I32), 0)
-        scale_rows = w2_scales.bitcast(I32).rearrange("a q n -> q a n")
-        for quad in range(P // QUAD):
-            rows = slice(BLOCKS * quad, BLOCKS * (quad + 1))
-            nc.sync.dma_start(w2_exps[QUAD * quad : QUAD * quad + BLOCKS, :, :].bitcast(I32), scale_rows[rows, :, :])
+        def load_exps(w2_exps, zero):
+            if zero:
+                nc.vector.memset(w2_exps[:].bitcast(I32), 0)
+            scale_rows = w2_scales.bitcast(I32).rearrange("a q n -> q a n")
+            for quad in range(P // QUAD):
+                rows = slice(BLOCKS * quad, BLOCKS * (quad + 1))
+                nc.sync.dma_start(w2_exps[QUAD * quad : QUAD * quad + BLOCKS, :, :].bitcast(I32), scale_rows[rows, :, :])
+
+
+        if W2 != 'w1a':
+            w2_exps = keep.tile([P, PASSES, M], U8, name="w2_exps", align_bytes=ALIGN)
+            load_exps(w2_exps, True)
 
         turned = keep.tile([P, RUN // QUAD, QUAD], F32, name="turned", align_bytes=ALIGN)
         spread = keep.tile([P, S], F32, name="spread", align_bytes=ALIGN)
@@ -85,23 +119,25 @@ def tile_list_hmlp_tm_none_kernel(tc, xT, w1, w2_words, w2_scales, wgt, offs, ou
         nc.vector.transpose(weights[:, 0:HALF], spread[:, 0:HALF])
         nc.vector.transpose(weights[:, HALF:S], spread[:, HALF:S])
 
-        early_first = shared.tile([P, PAIR, CHUNK], F32, name="early_first", align_bytes=ALIGN, offset=RAW_BYTES - ALIGN)
-        early_rest = keep.tile([P, PAIR, S - CHUNK], F32, name="early_rest", tag="rest")
-        late_first = keep.tile([P, PAIR, S - CHUNK], F32, name="late_first")
-        late = [late_first[:, :, c * CHUNK : (c + 1) * CHUNK] for c in range(CHUNKS - 1)]
+        early_first = shared.tile([P, PAIR, EA], F32, name="early_first", align_bytes=ALIGN, offset=RAW_BYTES - ALIGN if 'A' not in LOADS else (RAW_BYTES if 'B' not in LOADS else 4 * RAW_BYTES))
+        early_rest = shared.tile([P, PAIR, S - EA], F32, name="early_rest", align_bytes=ALIGN, offset=2 * RAW_BYTES)
+        late_first = shared.tile([P, PAIR, G2N * CHUNK], F32, name="late_first", align_bytes=ALIGN, offset=7 * RAW_BYTES)
+        late = [late_first[:, :, c * CHUNK : (c + 1) * CHUNK] if c < G2N else None for c in range(CHUNKS)]
         x_bf = keep.tile([P, S * PACK], BF16, name="x_bf", align_bytes=ALIGN)
         x_codes = keep.tile([P, S], U32, name="x_codes", align_bytes=ALIGN)
-        x_scales = keep.tile([P, S], U8, name="x_scales", align_bytes=ALIGN)
-        w1_bf = [keep.tile([P, PASS * PACK], BF16, name=f"w1_bf{a}", align_bytes=ALIGN) for a in range(PASSES)]
+        x_sc = [None] * CHUNKS
+        w1_bf = {}
         w1_codes = [keep.tile([P, PASS], U32, name=f"w1_codes{a}", align_bytes=ALIGN) for a in range(PASSES)]
         w1_scales = [keep.tile([P, PASS], U8, name=f"w1_scales{a}", align_bytes=ALIGN) for a in range(PASSES)]
-        h_bf = [keep.tile([P, PASSES, TILE * PACK], BF16, name=f"h_bf{b}", align_bytes=ALIGN) for b in range(TILES)]
+        h_bf = [None] * TILES
         h_codes = [keep.tile([P, PASSES, TILE], U32, name=f"h_codes{b}", align_bytes=ALIGN) for b in range(TILES)]
         h_scales = [keep.tile([P, PASSES, TILE], U8, name=f"h_scales{b}", align_bytes=ALIGN) for b in range(TILES)]
         y = [keep.tile([P, M], F32, name=f"y{b}") for b in range(TILES)]
 
         def cast(dst, src, on_scalar):
-            if on_scalar:
+            if on_scalar == 2:
+                nc.gpsimd.tensor_copy(dst, src)
+            elif on_scalar:
                 nc.scalar.activation(dst, src, COPY)
             else:
                 nc.vector.tensor_copy(dst, src)
@@ -122,18 +158,36 @@ def tile_list_hmlp_tm_none_kernel(tc, xT, w1, w2_words, w2_scales, wgt, offs, ou
 
         def quantize_x(c):
             cols = slice(c * CHUNK, (c + 1) * CHUNK)
-            nc.vector.quantize_mx(x_codes[:, cols].bitcast(FP8X4), x_scales[:, cols], x_bf[:, c * CHUNK * PACK : (c + 1) * CHUNK * PACK])
+            if c in XH:
+                x_sc[c] = shared.tile([P, CHUNK], U8, name=f"x_sc{c}", align_bytes=ALIGN, offset=(4096 if c not in XB else RAW_BYTES + 7168) + c * CHUNK)
+            else:
+                x_sc[c] = keep.tile([P, CHUNK], U8, name=f"x_sc{c}", align_bytes=ALIGN)
+            nc.vector.quantize_mx(x_codes[:, cols].bitcast(FP8X4), x_sc[c][:], x_bf[:, c * CHUNK * PACK : (c + 1) * CHUNK * PACK])
 
         def round_w1(a, t0, on_scalar):
             src = w1_raw[a][:].rearrange("p i (m t) -> p m i t", t=PACK)[:, :, :, t0 : t0 + PAIR]
-            dst = w1_bf[a][:].rearrange("p (t m i) -> p m i t", t=PACK, i=PACK)[:, :, :, t0 : t0 + PAIR]
+            h = t0 // PAIR
+            slot = 2 * a + h
+            if a == 1 and WB[h] != "-":
+                slot = int(WB[h])
+            if a in WIDE:
+                if a not in w1_bf:
+                    w1_bf[a] = shared.tile([P, PACK * PASS], BF16, name=f"w1_bf{a}", align_bytes=ALIGN, offset=5 * RAW_BYTES + 4096 * a)
+                cast(w1_bf[a][:].rearrange("p (t m i) -> p m i t", t=PACK, i=PACK)[:, :, :, t0 : t0 + PAIR], src, on_scalar)
+                return
+            w1_bf[a, h] = shared.tile([P, PAIR * PASS], BF16, name=f"w1_bf{a}{h}", align_bytes=ALIGN, offset=5 * RAW_BYTES + 2048 * slot)
+            dst = w1_bf[a, h][:].rearrange("p (t m i) -> p m i t", t=PAIR, i=PACK)
             cast(dst, src, on_scalar)
 
         def quantize_w1(a, t0):
+            if a in WIDE:
+                if t0:
+                    nc.vector.quantize_mx(w1_codes[a][:].bitcast(FP8X4), w1_scales[a][:], w1_bf[a][:])
+                return
             cols = slice(t0 * P, (t0 + PAIR) * P)
-            nc.vector.quantize_mx(w1_codes[a][:, cols].bitcast(FP8X4), w1_scales[a][:, cols], w1_bf[a][:, t0 * PASS : (t0 + PAIR) * PASS])
+            nc.vector.quantize_mx(w1_codes[a][:, cols].bitcast(FP8X4), w1_scales[a][:, cols], w1_bf[a, t0 // PAIR][:])
 
-        def first_layer(a, b):
+        def first_layer(a, b, on_scalar):
             acc = psum.tile([P, PACK, TILE], F32, name="h_acc", tag="bank")
             tokens = slice(b * TILE, (b + 1) * TILE)
             for t in range(PACK):
@@ -142,24 +196,33 @@ def tile_list_hmlp_tm_none_kernel(tc, xT, w1, w2_words, w2_scales, wgt, offs, ou
                     lhsT=w1_codes[a][:, t * P : (t + 1) * P].bitcast(FP8X4),
                     lhsT_scale=w1_scales[a][:, t * P : (t + 1) * P],
                     rhs=x_codes[:, tokens].bitcast(FP8X4),
-                    rhs_scale=x_scales[:, tokens],
+                    rhs_scale=x_sc[b // 2][:, (b % 2) * TILE : (b % 2 + 1) * TILE],
                     start=True,
                     stop=True,
                 )
+            if h_bf[b] is None:
+                h_bf[b] = shared.tile([P, PASSES, TILE * PACK], BF16, name=f"h_bf{b}", align_bytes=ALIGN, offset=RAW_BYTES + 2048 * HH.index(b)) if b in HH else keep.tile([P, PASSES, TILE * PACK], BF16, name=f"h_bf{b}", align_bytes=ALIGN)
             dst = h_bf[b][:, a, :].rearrange("p (n t) -> p n t", t=PACK)
             src = acc[:].rearrange("p t n -> p n t")
-            if b in SCALAR_TILES[a]:
+            if on_scalar:
                 nc.scalar.activation(dst, src, RELU)
             else:
                 nc.vector.tensor_scalar(dst, src, 0.0, None, MAX)
-            if b == TILES - 1:
-                nc.vector.quantize_mx(h_codes[b][:, a, :].bitcast(FP8X4), h_scales[b][:, a, :], h_bf[b][:, a, :])
-            elif a == PASSES - 1:
+
+        def quantize_h(b, a):
+            if a is None:
                 nc.vector.quantize_mx(
                     h_codes[b][:].rearrange("p a n -> p (a n)").bitcast(FP8X4),
                     h_scales[b][:].rearrange("p a n -> p (a n)"),
                     h_bf[b][:].rearrange("p a n -> p (a n)"),
                 )
+            else:
+                nc.vector.quantize_mx(h_codes[b][:, a, :].bitcast(FP8X4), h_scales[b][:, a, :], h_bf[b][:, a, :])
+
+        def round_w1_m(a, m0, m1, on_scalar):
+            src = w1_raw[a][:].rearrange("p i (m t) -> p m i t", t=PACK)[:, m0:m1]
+            dst = w1_bf[a][:].rearrange("p (t m i) -> p m i t", t=PACK, i=PACK)[:, m0:m1]
+            cast(dst, src, on_scalar)
 
         def second_layer(b, n0, width, step):
             acc = psum.tile([P, width], F32, name="y_acc", tag="bank")
@@ -189,79 +252,79 @@ def tile_list_hmlp_tm_none_kernel(tc, xT, w1, w2_words, w2_scales, wgt, offs, ou
             copy_out(y[b][:], second_layer(b, 0, M, M), on_scalar)
             store(b)
 
-        for i in range(PAIR):
-            gather(i, 0, CHUNK, early_first[:, i, :])
-            gather(i, CHUNK, S - CHUNK, early_rest[:, i, :])
-        round_x(early_first[:], 0, CHUNK, 0, True)
-        w1_rows = w1.rearrange("(p i) r -> p i r", i=PACK)
-        w1_raw = [shared.tile([P, PACK, PASS], F32, name=f"w1_raw{a}", align_bytes=ALIGN, offset=a * RAW_BYTES) for a in range(PASSES)]
-        nc.scalar.dma_start(w1_raw[0][:], w1_rows[:, :, 0:PASS])
-        round_x(early_rest[:], CHUNK, S - CHUNK, 0, True)
-        nc.scalar.dma_start(w1_raw[1][:], w1_rows[:, :, PASS : 2 * PASS])
-        gather(PAIR, 0, S - CHUNK, late_first[:, 0, :])
-
-        gather_last_plane(0)
-        gather_last_plane(1)
-        round_late(0, False)
-        gather_last_plane(2)
-        quantize_x(0)
-        scratch = psum.tile([P, CHUNK], F32, name="scratch", tag="bank")
-        for repeat in range(WARM_PASSES):
-            nc.tensor.matmul_mx(
-                out=scratch[:],
-                lhsT=x_codes[:, 0:P].bitcast(FP8X4),
-                lhsT_scale=x_scales[:, 0:P],
-                rhs=x_codes[:, 0:CHUNK].bitcast(FP8X4),
-                rhs_scale=x_scales[:, 0:CHUNK],
-                start=True,
-                stop=True,
-            )
-        late_last = keep.tile([P, PAIR, CHUNK], F32, name="late_last", tag="rest")
-        late.append(late_last[:])
-        gather(PAIR, S - CHUNK, CHUNK, late_last[:, 0, :])
-        round_w1(0, 0, False)
-        gather_last_plane(CHUNKS - 1)
-
-        w2_codes = keep.tile([P, PASSES, 2 * M], U8, name="w2_codes", tag=f"plane{PACK - 1}", align_bytes=ALIGN)
-        nc.sync.dma_start(w2_codes[:].bitcast(I32), w2_words.bitcast(I32).rearrange("a p n -> p a n"))
-
-        round_late(1, True)
-        round_w1(0, PAIR, True)
-        for c in range(2, CHUNKS):
-            round_late(c, True)
-        round_w1(1, PAIR, True)
-        quantize_w1(0, 0)
-        quantize_x(1)
-        quantize_w1(0, PAIR)
-        round_w1(1, 0, False)
-        quantize_x(2)
-        quantize_w1(1, 0)
-        quantize_x(CHUNKS - 1)
-        quantize_w1(1, PAIR)
-
-        last = TILES - 1
-        for a in range(PASSES):
-            for b in range(last):
-                first_layer(a, b)
-        first_layer(0, last)
-        output_tile(0, True)
-        first_layer(1, last)
-
-        for b in range(1, last):
-            output_tile(b, b < last - 1)
-        sides = [psum.tile([P, M // 2], F32, name="y_acc", tag="bank") for side in range(2)]
-        for a in range(PASSES):
-            for n0 in range(0, M, P):
-                side, lo = divmod(n0, M // 2)
-                nc.tensor.matmul_mx(
-                    out=sides[side][:, lo : lo + P],
-                    lhsT=h_codes[last][:, a, :].bitcast(FP8X4),
-                    lhsT_scale=h_scales[last][:, a, :],
-                    rhs=w2_codes[:, a, 2 * n0 : 2 * (n0 + P)].bitcast(FP4X4),
-                    rhs_scale=w2_exps[:, a, n0 : n0 + P],
-                    start=(a == 0 and lo == 0),
-                    stop=(a == PASSES - 1 and lo + P == M // 2),
-                )
-        for side in range(2):
-            copy_out(y[last][:, side * M // 2 : (side + 1) * M // 2], sides[side], side == 1)
-        store(last)
+        st = {}
+        if W2 == "sync":
+            w2_codes = keep.tile([P, PASSES, 2 * M], U8, name="w2_codes", align_bytes=ALIGN)
+            nc.sync.dma_start(w2_codes[:].bitcast(I32), w2_words.bitcast(I32).rearrange("a p n -> p a n"))
+        for step in PLAN:
+            op = step[0]
+            if op == "G0":
+                for i in range(PAIR):
+                    gather(i, 0, EA, early_first[:, i, :])
+                    gather(i, EA, S - EA, early_rest[:, i, :])
+                round_x(early_first[:], 0, EA, 0, True)
+                if 'A' not in LOADS:
+                    load_w1(0, nc.gpsimd if QA == "g" else nc.scalar)
+                if 'B' not in LOADS and BFIRST:
+                    load_w1(1, nc.gpsimd if QB == "g" else nc.scalar)
+                round_x(early_rest[:], EA, S - EA, 0, True)
+                if 'B' not in LOADS and not BFIRST:
+                    load_w1(1, nc.gpsimd if QB == "g" else nc.scalar)
+                gather(PAIR, 0, G2N * CHUNK, late_first[:, 0, :])
+            elif op == "G2":
+                c = step[1]
+                lt = shared.tile([P, PAIR, CHUNK], F32, name=f"late{c}", align_bytes=ALIGN, offset={"R": 2 * RAW_BYTES, "a": 0, "b": RAW_BYTES + 4096, "0": 5 * RAW_BYTES, "1": 5 * RAW_BYTES + 2048, "2": 5 * RAW_BYTES + 4096, "3": 5 * RAW_BYTES + 6144, "n": 3 * RAW_BYTES, "L": 7 * RAW_BYTES}[HOLD[c - 2]] + (2048 * (c - 2) if HOLD[c - 2] in "RabnL" else 0))
+                late[c] = lt[:]
+                gather(PAIR, c * CHUNK, CHUNK, lt[:, 0, :])
+            elif op == "G3":
+                gather_last_plane(step[1])
+                if step[1] == CHUNKS - 1 and W2 == "p3":
+                    w2_codes = keep.tile([P, PASSES, 2 * M], U8, name="w2_codes", tag=f"plane{PACK - 1}", align_bytes=ALIGN)
+                    nc.sync.dma_start(w2_codes[:].bitcast(I32), w2_words.bitcast(I32).rearrange("a p n -> p a n"))
+            elif op == "RL":
+                round_late(step[1], step[2])
+            elif op == "QX":
+                quantize_x(step[1])
+            elif op == "RW":
+                if MSPLIT is None:
+                    round_w1(step[1], step[2] * PAIR, step[3])
+                else:
+                    ms = MSPLIT[step[1]]
+                    round_w1_m(step[1], (0, ms)[step[2]], (ms, P)[step[2]], step[3])
+            elif op == "W2":
+                w2_codes = shared.tile([P, PASSES, 2 * M], U8, name="w2_codes", align_bytes=ALIGN, offset=4096)
+                nc.sync.dma_start(w2_codes[:].bitcast(I32), w2_words.bitcast(I32).rearrange("a p n -> p a n"))
+            elif op == "QW":
+                quantize_w1(step[1], step[2] * PAIR)
+            elif op == "WARM":
+                scratch = psum.tile([P, CHUNK], F32, name="scratch", tag="bank")
+                for repeat in range(WARM_PASSES):
+                    nc.tensor.matmul_mx(out=scratch[:], lhsT=x_codes[:, WC * CHUNK : WC * CHUNK + P].bitcast(FP8X4), lhsT_scale=x_sc[WC][:, 0:P], rhs=x_codes[:, WC * CHUNK : (WC + 1) * CHUNK].bitcast(FP8X4), rhs_scale=x_sc[WC][:], start=True, stop=True)
+            elif op == "L1":
+                first_layer(step[1], step[2], step[3])
+            elif op == "QH":
+                quantize_h(step[1], step[2])
+            elif op == "Y":
+                output_tile(step[1], step[2])
+            elif op == "YA":
+                b = step[1]
+                st[b] = [psum.tile([P, M // 2], F32, name="y_acc", tag="bank") for side in range(2)]
+                for side in range(2):
+                    for g in range(2):
+                        n0 = side * 256 + g * P
+                        nc.tensor.matmul_mx(out=st[b][side][:, g * P : (g + 1) * P], lhsT=h_codes[b][:, 0, :].bitcast(FP8X4), lhsT_scale=h_scales[b][:, 0, :], rhs=w2_codes[:, 0, 2 * n0 : 2 * (n0 + P)].bitcast(FP4X4), rhs_scale=w2_exps[:, 0, n0 : n0 + P], start=(g == 0), stop=False)
+            elif op == "YB":
+                b = step[1]
+                for side in range(2):
+                    for g in range(2):
+                        n0 = side * 256 + g * P
+                        nc.tensor.matmul_mx(out=st[b][side][:, g * P : (g + 1) * P], lhsT=h_codes[b][:, 1, :].bitcast(FP8X4), lhsT_scale=h_scales[b][:, 1, :], rhs=w2_codes[:, 1, 2 * n0 : 2 * (n0 + P)].bitcast(FP4X4), rhs_scale=w2_exps[:, 1, n0 : n0 + P], start=False, stop=(g == 1))
+                for side in range(2):
+                    copy_out(y[b][:, side * M // 2 : (side + 1) * M // 2], st[b][side], side == 1)
+                store(b)
+            elif op == "YS":
+                b = step[1]
+                sides = [second_layer(b, side * M // 2, M // 2, P) for side in range(2)]
+                for side in range(2):
+                    copy_out(y[b][:, side * M // 2 : (side + 1) * M // 2], sides[side], side == 1)
+                store(b)

@@ -55,7 +55,7 @@ HOLD = "na"
 QA = "s"
 QB = "s"
 WB = "--"
-PLAN = (("G0",), ("G3", 0,), ("G3", 1,), ("RL", 0, 0,), ("G3", 2,), ("QX", 0,), ("WARM",), ("RW", 0, 0, 0,), ("RL", 1, 1,), ("RW", 0, 1, 1,), ("W2",), ("RL", 2, 1,), ("RW", 1, 1, 1,), ("QW", 0, 0,), ("QX", 1,), ("QW", 0, 1,), ("G2", 3,), ("RW", 1, 0, 0,), ("QX", 2,), ("QW", 1, 0,), ("QW", 1, 1,), ("G3", 3,), ("RL", 3, 0,), ("L1", 0, 0, 1,), ("L1", 0, 1, 1,), ("L1", 0, 2, 1,), ("L1", 0, 4, 1,), ("L1", 1, 4, 1,), ("L1", 1, 0, 0,), ("QH", 0, None,), ("QH", 4, None,), ("L1", 1, 2, 1,), ("L1", 1, 1, 1,), ("L1", 0, 3, 1,), ("QX", 3,), ("L1", 0, 5, 1,), ("L1", 1, 5, 1,), ("QH", 1, None,), ("L1", 1, 3, 0,), ("QH", 2, None,), ("QH", 3, None,), ("L1", 0, 6, 1,), ("Y", 0, 0,), ("Y", 4, 0,), ("Y", 2, 1,), ("Y", 1, 1,), ("L1", 1, 6, 0,), ("QH", 5, None,), ("L1", 0, 7, 1,), ("QH", 6, None,), ("Y", 3, 0,), ("L1", 1, 7, 1,), ("QH", 7, 1,), ("QH", 7, 0,), ("Y", 5, 1,), ("Y", 6, 1,), ("YA", 7,), ("YB", 7,),)
+PLAN = (("G0",), ("G3", 0,), ("G3", 1,), ("RL", 0, 0,), ("G3", 2,), ("QX", 0,), ("WARM",), ("RW", 0, 0, 0,), ("RL", 1, 1,), ("RW", 0, 1, 1,), ("W2",), ("RL", 2, 1,), ("RW", 1, 1, 1,), ("QW", 0, 0,), ("QX", 1,), ("QW", 0, 1,), ("G2", 3,), ("RW", 1, 0, 0,), ("QX", 2,), ("QW", 1, 0,), ("QW", 1, 1,), ("G3", 3,), ("RL", 3, 0,), ("QX", 3,), ("L1", 0, 0, 1,), ("L1", 0, 1, 1,), ("L1", 0, 2, 1,), ("L1", 0, 3, 1,), ("L1", 0, 4, 1,), ("L1", 0, 5, 0,), ("L1", 1, 0, 0,), ("QH", 0, None,), ("L1", 1, 1, 1,), ("QH", 1, None,), ("L1", 1, 2, 1,), ("QH", 2, None,), ("L1", 1, 3, 1,), ("QH", 3, None,), ("L1", 1, 4, 1,), ("QH", 4, None,), ("L1", 1, 5, 1,), ("QH", 5, None,), ("L1", 0, 6, 0,), ("L1", 1, 6, 0,), ("QH", 6, None,), ("L1", 0, 7, 0,), ("QH", 7, 0,), ("Y", 0, 1,), ("L1", 1, 7, 0,), ("QH", 7, 1,), ("Y", 1, 1,), ("Y", 2, 1,), ("Y", 3, 1,), ("Y", 4, 1,), ("Y", 5, 1,), ("Y", 6, 0,), ("YA", 7,), ("YB", 7,),)
 
 
 def tile_list_hmlp_tm_none_kernel(tc, xT, w1, w2_words, w2_scales, wgt, offs, out):

@@ -33,7 +33,7 @@ CHUNKS = S // CHUNK
 RUN = S // GROUP
 HALF = S // 2
 RAW_BYTES = PACK * PASS * 4
-ALIGN = 64
+ALIGN = 256
 WARM_PASSES = 6
 SCALAR_TILES = (range(1, 4), range(0, 5))
 
@@ -132,7 +132,7 @@ def tile_list_hmlp_tm_none_kernel(tc, xT, w1, w2_words, w2_scales, wgt, offs, ou
         h_bf = [None] * TILES
         h_codes = [keep.tile([P, PASSES, TILE], U32, name=f"h_codes{b}", align_bytes=ALIGN) for b in range(TILES)]
         h_scales = [keep.tile([P, PASSES, TILE], U8, name=f"h_scales{b}", align_bytes=ALIGN) for b in range(TILES)]
-        y = [keep.tile([P, M], F32, name=f"y{b}") for b in range(TILES)]
+        y = [keep.tile([P, M], F32, name=f"y{b}", align_bytes=ALIGN) for b in range(TILES)]
 
         def cast(dst, src, on_scalar):
             if on_scalar == 2:

@@ -33,29 +33,11 @@ CHUNKS = S // CHUNK
 RUN = S // GROUP
 HALF = S // 2
 RAW_BYTES = PACK * PASS * 4
+LATE_BYTES = PAIR * CHUNK * 4
 ALIGN = 256
 WARM_PASSES = 6
-SCALAR_TILES = (range(1, 4), range(0, 5))
-
-MSPLIT = None
-WIDE = (0,)
-WC = 0
-ZERO = False
-SEEDS = False
-BFIRST = False
-EA = 256
-G2N = 3
-XH = ()
-XB = ()
-HH = ()
-LOADS = "123"
-GATE = "ef"
-W2 = "a"
-HOLD = "na"
-QA = "s"
-QB = "s"
-WB = "--"
-PLAN = (("G0",), ("G3", 0,), ("G3", 1,), ("RL", 0, 0,), ("G3", 2,), ("QX", 0,), ("WARM",), ("RW", 0, 0, 0,), ("RL", 1, 1,), ("RW", 0, 1, 1,), ("W2",), ("RL", 2, 1,), ("RW", 1, 1, 1,), ("QW", 0, 0,), ("QX", 1,), ("QW", 0, 1,), ("G2", 3,), ("RW", 1, 0, 0,), ("QX", 2,), ("QW", 1, 0,), ("QW", 1, 1,), ("G3", 3,), ("RL", 3, 0,), ("QX", 3,), ("L1", 0, 0, 1,), ("L1", 0, 1, 1,), ("L1", 0, 2, 1,), ("L1", 0, 3, 1,), ("L1", 0, 4, 1,), ("L1", 0, 5, 0,), ("L1", 1, 0, 0,), ("QH", 0, None,), ("L1", 1, 1, 1,), ("QH", 1, None,), ("L1", 1, 2, 1,), ("QH", 2, None,), ("L1", 1, 3, 1,), ("QH", 3, None,), ("L1", 1, 4, 1,), ("QH", 4, None,), ("L1", 1, 5, 1,), ("QH", 5, None,), ("L1", 0, 6, 0,), ("L1", 1, 6, 0,), ("QH", 6, None,), ("L1", 0, 7, 0,), ("QH", 7, 0,), ("Y", 0, 1,), ("L1", 1, 7, 0,), ("QH", 7, 1,), ("Y", 1, 1,), ("Y", 2, 1,), ("Y", 3, 1,), ("Y", 4, 1,), ("Y", 5, 1,), ("Y", 6, 0,), ("YA", 7,), ("YB", 7,),)
+EARLY_TILES = TILES - CHUNK // TILE
+VECTOR_JOINS = 3
 
 
 def tile_list_hmlp_tm_none_kernel(tc, xT, w1, w2_words, w2_scales, wgt, offs, out):
@@ -70,37 +52,23 @@ def tile_list_hmlp_tm_none_kernel(tc, xT, w1, w2_words, w2_scales, wgt, offs, ou
         for quad in range(P // QUAD):
             first = (QUAD * quad + 1) * S
             steps = wgt_flat[first : first + QUAD * (S - RUN)].rearrange("(p x) -> p x", x=S - RUN)
-            queue = nc.sync if (quad % 2 == 0 and not SEEDS) else nc.scalar
+            queue = nc.sync if quad % 2 == 0 else nc.scalar
             queue.dma_start(seeds[QUAD * quad : QUAD * (quad + 1), :], steps[:, 0:RUN])
 
         offsets = keep.tile([P, S // GROUP], U16, name="offsets")
         x_rows = xT.rearrange("(p i) c -> p i c", i=PACK)
-        planes = [keep.tile([P, T], F32, name=f"plane{i}", tag=f"plane{i}", align_bytes=ALIGN) if (i != 1 or GATE != "p1") else shared.tile([P, T], F32, name="plane1", align_bytes=ALIGN, offset=RAW_BYTES // 2) for i in range(PACK)]
+        planes = [keep.tile([P, T], F32, name=f"plane{i}", tag=f"plane{i}", align_bytes=ALIGN) for i in range(PACK)]
         nc.sync.dma_start(planes[0][:], x_rows[:, 0, :])
         nc.sync.dma_start(offsets[:], offs)
-        w1_rows = w1.rearrange("(p i) r -> p i r", i=PACK)
-        w1_raw = [None, None]
-        def load_w1(a, q):
-            w1_raw[a] = shared.tile([P, PACK, PASS], F32, name=f"w1_raw{a}", align_bytes=ALIGN, offset=a * RAW_BYTES)
-            q.dma_start(w1_raw[a][:], w1_rows[:, :, a * PASS : (a + 1) * PASS])
-        for ch in LOADS:
-            if ch in "123":
-                nc.sync.dma_start(planes[int(ch)][:], x_rows[:, int(ch), :])
-            else:
-                load_w1("AB".index(ch), nc.sync)
+        for i in range(1, PACK):
+            nc.sync.dma_start(planes[i][:], x_rows[:, i, :])
 
-        def load_exps(w2_exps, zero):
-            if zero:
-                nc.vector.memset(w2_exps[:].bitcast(I32), 0)
-            scale_rows = w2_scales.bitcast(I32).rearrange("a q n -> q a n")
-            for quad in range(P // QUAD):
-                rows = slice(BLOCKS * quad, BLOCKS * (quad + 1))
-                nc.sync.dma_start(w2_exps[QUAD * quad : QUAD * quad + BLOCKS, :, :].bitcast(I32), scale_rows[rows, :, :])
-
-
-        if W2 != 'w1a':
-            w2_exps = keep.tile([P, PASSES, M], U8, name="w2_exps", align_bytes=ALIGN)
-            load_exps(w2_exps, True)
+        w2_exps = keep.tile([P, PASSES, M], U8, name="w2_exps", align_bytes=ALIGN)
+        nc.vector.memset(w2_exps[:].bitcast(I32), 0)
+        scale_rows = w2_scales.bitcast(I32).rearrange("a q n -> q a n")
+        for quad in range(P // QUAD):
+            rows = slice(BLOCKS * quad, BLOCKS * (quad + 1))
+            nc.sync.dma_start(w2_exps[QUAD * quad : QUAD * quad + BLOCKS, :, :].bitcast(I32), scale_rows[rows, :, :])
 
         turned = keep.tile([P, RUN // QUAD, QUAD], F32, name="turned", align_bytes=ALIGN)
         spread = keep.tile([P, S], F32, name="spread", align_bytes=ALIGN)
@@ -119,25 +87,23 @@ def tile_list_hmlp_tm_none_kernel(tc, xT, w1, w2_words, w2_scales, wgt, offs, ou
         nc.vector.transpose(weights[:, 0:HALF], spread[:, 0:HALF])
         nc.vector.transpose(weights[:, HALF:S], spread[:, HALF:S])
 
-        early_first = shared.tile([P, PAIR, EA], F32, name="early_first", align_bytes=ALIGN, offset=RAW_BYTES - ALIGN if 'A' not in LOADS else (RAW_BYTES if 'B' not in LOADS else 4 * RAW_BYTES))
-        early_rest = shared.tile([P, PAIR, S - EA], F32, name="early_rest", align_bytes=ALIGN, offset=2 * RAW_BYTES)
-        late_first = shared.tile([P, PAIR, G2N * CHUNK], F32, name="late_first", align_bytes=ALIGN, offset=7 * RAW_BYTES)
-        late = [late_first[:, :, c * CHUNK : (c + 1) * CHUNK] if c < G2N else None for c in range(CHUNKS)]
+        early_first = shared.tile([P, PAIR, CHUNK], F32, name="early_first", align_bytes=ALIGN, offset=RAW_BYTES - ALIGN)
+        early_rest = keep.tile([P, PAIR, S - CHUNK], F32, name="early_rest")
+        late_first = keep.tile([P, PAIR, S - CHUNK], F32, name="late_first")
+        late = [late_first[:, :, c * CHUNK : (c + 1) * CHUNK] for c in range(CHUNKS - 1)]
         x_bf = keep.tile([P, S * PACK], BF16, name="x_bf", align_bytes=ALIGN)
         x_codes = keep.tile([P, S], U32, name="x_codes", align_bytes=ALIGN)
-        x_sc = [None] * CHUNKS
-        w1_bf = {}
+        x_scales = keep.tile([P, S], U8, name="x_scales", align_bytes=ALIGN)
+        w1_bf = [keep.tile([P, PASS * PACK], BF16, name=f"w1_bf{a}", align_bytes=ALIGN) for a in range(PASSES)]
         w1_codes = [keep.tile([P, PASS], U32, name=f"w1_codes{a}", align_bytes=ALIGN) for a in range(PASSES)]
         w1_scales = [keep.tile([P, PASS], U8, name=f"w1_scales{a}", align_bytes=ALIGN) for a in range(PASSES)]
-        h_bf = [None] * TILES
+        h_bf = [keep.tile([P, PASSES, TILE * PACK], BF16, name=f"h_bf{b}", align_bytes=ALIGN) for b in range(TILES)]
         h_codes = [keep.tile([P, PASSES, TILE], U32, name=f"h_codes{b}", align_bytes=ALIGN) for b in range(TILES)]
         h_scales = [keep.tile([P, PASSES, TILE], U8, name=f"h_scales{b}", align_bytes=ALIGN) for b in range(TILES)]
         y = [keep.tile([P, M], F32, name=f"y{b}", align_bytes=ALIGN) for b in range(TILES)]
 
         def cast(dst, src, on_scalar):
-            if on_scalar == 2:
-                nc.gpsimd.tensor_copy(dst, src)
-            elif on_scalar:
+            if on_scalar:
                 nc.scalar.activation(dst, src, COPY)
             else:
                 nc.vector.tensor_copy(dst, src)
@@ -158,34 +124,16 @@ def tile_list_hmlp_tm_none_kernel(tc, xT, w1, w2_words, w2_scales, wgt, offs, ou
 
         def quantize_x(c):
             cols = slice(c * CHUNK, (c + 1) * CHUNK)
-            if c in XH:
-                x_sc[c] = shared.tile([P, CHUNK], U8, name=f"x_sc{c}", align_bytes=ALIGN, offset=(4096 if c not in XB else RAW_BYTES + 7168) + c * CHUNK)
-            else:
-                x_sc[c] = keep.tile([P, CHUNK], U8, name=f"x_sc{c}", align_bytes=ALIGN)
-            nc.vector.quantize_mx(x_codes[:, cols].bitcast(FP8X4), x_sc[c][:], x_bf[:, c * CHUNK * PACK : (c + 1) * CHUNK * PACK])
+            nc.vector.quantize_mx(x_codes[:, cols].bitcast(FP8X4), x_scales[:, cols], x_bf[:, c * CHUNK * PACK : (c + 1) * CHUNK * PACK])
 
         def round_w1(a, t0, on_scalar):
             src = w1_raw[a][:].rearrange("p i (m t) -> p m i t", t=PACK)[:, :, :, t0 : t0 + PAIR]
-            h = t0 // PAIR
-            slot = 2 * a + h
-            if a == 1 and WB[h] != "-":
-                slot = int(WB[h])
-            if a in WIDE:
-                if a not in w1_bf:
-                    w1_bf[a] = shared.tile([P, PACK * PASS], BF16, name=f"w1_bf{a}", align_bytes=ALIGN, offset=5 * RAW_BYTES + 4096 * a)
-                cast(w1_bf[a][:].rearrange("p (t m i) -> p m i t", t=PACK, i=PACK)[:, :, :, t0 : t0 + PAIR], src, on_scalar)
-                return
-            w1_bf[a, h] = shared.tile([P, PAIR * PASS], BF16, name=f"w1_bf{a}{h}", align_bytes=ALIGN, offset=5 * RAW_BYTES + 2048 * slot)
-            dst = w1_bf[a, h][:].rearrange("p (t m i) -> p m i t", t=PAIR, i=PACK)
+            dst = w1_bf[a][:].rearrange("p (t m i) -> p m i t", t=PACK, i=PACK)[:, :, :, t0 : t0 + PAIR]
             cast(dst, src, on_scalar)
 
-        def quantize_w1(a, t0):
-            if a in WIDE:
-                if t0:
-                    nc.vector.quantize_mx(w1_codes[a][:].bitcast(FP8X4), w1_scales[a][:], w1_bf[a][:])
-                return
-            cols = slice(t0 * P, (t0 + PAIR) * P)
-            nc.vector.quantize_mx(w1_codes[a][:, cols].bitcast(FP8X4), w1_scales[a][:, cols], w1_bf[a, t0 // PAIR][:])
+        def quantize_w1(a, t0, count):
+            cols = slice(t0 * P, (t0 + count) * P)
+            nc.vector.quantize_mx(w1_codes[a][:, cols].bitcast(FP8X4), w1_scales[a][:, cols], w1_bf[a][:, t0 * PASS : (t0 + count) * PASS])
 
         def first_layer(a, b, on_scalar):
             acc = psum.tile([P, PACK, TILE], F32, name="h_acc", tag="bank")
@@ -196,12 +144,10 @@ def tile_list_hmlp_tm_none_kernel(tc, xT, w1, w2_words, w2_scales, wgt, offs, ou
                     lhsT=w1_codes[a][:, t * P : (t + 1) * P].bitcast(FP8X4),
                     lhsT_scale=w1_scales[a][:, t * P : (t + 1) * P],
                     rhs=x_codes[:, tokens].bitcast(FP8X4),
-                    rhs_scale=x_sc[b // 2][:, (b % 2) * TILE : (b % 2 + 1) * TILE],
+                    rhs_scale=x_scales[:, tokens],
                     start=True,
                     stop=True,
                 )
-            if h_bf[b] is None:
-                h_bf[b] = shared.tile([P, PASSES, TILE * PACK], BF16, name=f"h_bf{b}", align_bytes=ALIGN, offset=RAW_BYTES + 2048 * HH.index(b)) if b in HH else keep.tile([P, PASSES, TILE * PACK], BF16, name=f"h_bf{b}", align_bytes=ALIGN)
             dst = h_bf[b][:, a, :].rearrange("p (n t) -> p n t", t=PACK)
             src = acc[:].rearrange("p t n -> p n t")
             if on_scalar:
@@ -209,35 +155,24 @@ def tile_list_hmlp_tm_none_kernel(tc, xT, w1, w2_words, w2_scales, wgt, offs, ou
             else:
                 nc.vector.tensor_scalar(dst, src, 0.0, None, MAX)
 
-        def quantize_h(b, a):
-            if a is None:
-                nc.vector.quantize_mx(
-                    h_codes[b][:].rearrange("p a n -> p (a n)").bitcast(FP8X4),
-                    h_scales[b][:].rearrange("p a n -> p (a n)"),
-                    h_bf[b][:].rearrange("p a n -> p (a n)"),
-                )
-            else:
-                nc.vector.quantize_mx(h_codes[b][:, a, :].bitcast(FP8X4), h_scales[b][:, a, :], h_bf[b][:, a, :])
+        def quantize_h(b, a0, count):
+            passes = slice(a0, a0 + count)
+            nc.vector.quantize_mx(
+                h_codes[b][:, passes, :].rearrange("p a n -> p (a n)").bitcast(FP8X4),
+                h_scales[b][:, passes, :].rearrange("p a n -> p (a n)"),
+                h_bf[b][:, passes, :].rearrange("p a n -> p (a n)"),
+            )
 
-        def round_w1_m(a, m0, m1, on_scalar):
-            src = w1_raw[a][:].rearrange("p i (m t) -> p m i t", t=PACK)[:, m0:m1]
-            dst = w1_bf[a][:].rearrange("p (t m i) -> p m i t", t=PACK, i=PACK)[:, m0:m1]
-            cast(dst, src, on_scalar)
-
-        def second_layer(b, n0, width, step):
-            acc = psum.tile([P, width], F32, name="y_acc", tag="bank")
-            for lo in range(0, width, step):
-                for a in range(PASSES):
-                    nc.tensor.matmul_mx(
-                        out=acc[:, lo : lo + step],
-                        lhsT=h_codes[b][:, a, :].bitcast(FP8X4),
-                        lhsT_scale=h_scales[b][:, a, :],
-                        rhs=w2_codes[:, a, 2 * (n0 + lo) : 2 * (n0 + lo + step)].bitcast(FP4X4),
-                        rhs_scale=w2_exps[:, a, n0 + lo : n0 + lo + step],
-                        start=(a == 0),
-                        stop=(a == PASSES - 1),
-                    )
-            return acc
+        def second_layer_pass(acc, b, a, n0, width, start, stop):
+            nc.tensor.matmul_mx(
+                out=acc,
+                lhsT=h_codes[b][:, a, :].bitcast(FP8X4),
+                lhsT_scale=h_scales[b][:, a, :],
+                rhs=w2_codes[:, a, 2 * n0 : 2 * (n0 + width)].bitcast(FP4X4),
+                rhs_scale=w2_exps[:, a, n0 : n0 + width],
+                start=start,
+                stop=stop,
+            )
 
         def copy_out(dst, acc, on_scalar):
             if on_scalar:
@@ -249,82 +184,87 @@ def tile_list_hmlp_tm_none_kernel(tc, xT, w1, w2_words, w2_scales, wgt, offs, ou
             nc.sync.dma_start(out[b * TILE : (b + 1) * TILE, :], y[b][:])
 
         def output_tile(b, on_scalar):
-            copy_out(y[b][:], second_layer(b, 0, M, M), on_scalar)
+            acc = psum.tile([P, M], F32, name="y_acc", tag="bank")
+            for a in range(PASSES):
+                second_layer_pass(acc[:], b, a, 0, M, a == 0, a == PASSES - 1)
+            copy_out(y[b][:], acc, on_scalar)
             store(b)
 
-        st = {}
-        if W2 == "sync":
-            w2_codes = keep.tile([P, PASSES, 2 * M], U8, name="w2_codes", align_bytes=ALIGN)
-            nc.sync.dma_start(w2_codes[:].bitcast(I32), w2_words.bitcast(I32).rearrange("a p n -> p a n"))
-        for step in PLAN:
-            op = step[0]
-            if op == "G0":
-                for i in range(PAIR):
-                    gather(i, 0, EA, early_first[:, i, :])
-                    gather(i, EA, S - EA, early_rest[:, i, :])
-                round_x(early_first[:], 0, EA, 0, True)
-                if 'A' not in LOADS:
-                    load_w1(0, nc.gpsimd if QA == "g" else nc.scalar)
-                if 'B' not in LOADS and BFIRST:
-                    load_w1(1, nc.gpsimd if QB == "g" else nc.scalar)
-                round_x(early_rest[:], EA, S - EA, 0, True)
-                if 'B' not in LOADS and not BFIRST:
-                    load_w1(1, nc.gpsimd if QB == "g" else nc.scalar)
-                gather(PAIR, 0, G2N * CHUNK, late_first[:, 0, :])
-            elif op == "G2":
-                c = step[1]
-                lt = shared.tile([P, PAIR, CHUNK], F32, name=f"late{c}", align_bytes=ALIGN, offset={"R": 2 * RAW_BYTES, "a": 0, "b": RAW_BYTES + 4096, "0": 5 * RAW_BYTES, "1": 5 * RAW_BYTES + 2048, "2": 5 * RAW_BYTES + 4096, "3": 5 * RAW_BYTES + 6144, "n": 3 * RAW_BYTES, "L": 7 * RAW_BYTES}[HOLD[c - 2]] + (2048 * (c - 2) if HOLD[c - 2] in "RabnL" else 0))
-                late[c] = lt[:]
-                gather(PAIR, c * CHUNK, CHUNK, lt[:, 0, :])
-            elif op == "G3":
-                gather_last_plane(step[1])
-                if step[1] == CHUNKS - 1 and W2 == "p3":
-                    w2_codes = keep.tile([P, PASSES, 2 * M], U8, name="w2_codes", tag=f"plane{PACK - 1}", align_bytes=ALIGN)
-                    nc.sync.dma_start(w2_codes[:].bitcast(I32), w2_words.bitcast(I32).rearrange("a p n -> p a n"))
-            elif op == "RL":
-                round_late(step[1], step[2])
-            elif op == "QX":
-                quantize_x(step[1])
-            elif op == "RW":
-                if MSPLIT is None:
-                    round_w1(step[1], step[2] * PAIR, step[3])
-                else:
-                    ms = MSPLIT[step[1]]
-                    round_w1_m(step[1], (0, ms)[step[2]], (ms, P)[step[2]], step[3])
-            elif op == "W2":
-                w2_codes = shared.tile([P, PASSES, 2 * M], U8, name="w2_codes", align_bytes=ALIGN, offset=4096)
-                nc.sync.dma_start(w2_codes[:].bitcast(I32), w2_words.bitcast(I32).rearrange("a p n -> p a n"))
-            elif op == "QW":
-                quantize_w1(step[1], step[2] * PAIR)
-            elif op == "WARM":
-                scratch = psum.tile([P, CHUNK], F32, name="scratch", tag="bank")
-                for repeat in range(WARM_PASSES):
-                    nc.tensor.matmul_mx(out=scratch[:], lhsT=x_codes[:, WC * CHUNK : WC * CHUNK + P].bitcast(FP8X4), lhsT_scale=x_sc[WC][:, 0:P], rhs=x_codes[:, WC * CHUNK : (WC + 1) * CHUNK].bitcast(FP8X4), rhs_scale=x_sc[WC][:], start=True, stop=True)
-            elif op == "L1":
-                first_layer(step[1], step[2], step[3])
-            elif op == "QH":
-                quantize_h(step[1], step[2])
-            elif op == "Y":
-                output_tile(step[1], step[2])
-            elif op == "YA":
-                b = step[1]
-                st[b] = [psum.tile([P, M // 2], F32, name="y_acc", tag="bank") for side in range(2)]
-                for side in range(2):
-                    for g in range(2):
-                        n0 = side * 256 + g * P
-                        nc.tensor.matmul_mx(out=st[b][side][:, g * P : (g + 1) * P], lhsT=h_codes[b][:, 0, :].bitcast(FP8X4), lhsT_scale=h_scales[b][:, 0, :], rhs=w2_codes[:, 0, 2 * n0 : 2 * (n0 + P)].bitcast(FP4X4), rhs_scale=w2_exps[:, 0, n0 : n0 + P], start=(g == 0), stop=False)
-            elif op == "YB":
-                b = step[1]
-                for side in range(2):
-                    for g in range(2):
-                        n0 = side * 256 + g * P
-                        nc.tensor.matmul_mx(out=st[b][side][:, g * P : (g + 1) * P], lhsT=h_codes[b][:, 1, :].bitcast(FP8X4), lhsT_scale=h_scales[b][:, 1, :], rhs=w2_codes[:, 1, 2 * n0 : 2 * (n0 + P)].bitcast(FP4X4), rhs_scale=w2_exps[:, 1, n0 : n0 + P], start=False, stop=(g == 1))
-                for side in range(2):
-                    copy_out(y[b][:, side * M // 2 : (side + 1) * M // 2], st[b][side], side == 1)
-                store(b)
-            elif op == "YS":
-                b = step[1]
-                sides = [second_layer(b, side * M // 2, M // 2, P) for side in range(2)]
-                for side in range(2):
-                    copy_out(y[b][:, side * M // 2 : (side + 1) * M // 2], sides[side], side == 1)
-                store(b)
+        for i in range(PAIR):
+            gather(i, 0, CHUNK, early_first[:, i, :])
+            gather(i, CHUNK, S - CHUNK, early_rest[:, i, :])
+        round_x(early_first[:], 0, CHUNK, 0, True)
+        w1_rows = w1.rearrange("(p i) r -> p i r", i=PACK)
+        w1_raw = [shared.tile([P, PACK, PASS], F32, name=f"w1_raw{a}", align_bytes=ALIGN, offset=a * RAW_BYTES) for a in range(PASSES)]
+        nc.scalar.dma_start(w1_raw[0][:], w1_rows[:, :, 0:PASS])
+        round_x(early_rest[:], CHUNK, S - CHUNK, 0, True)
+        nc.scalar.dma_start(w1_raw[1][:], w1_rows[:, :, PASS : 2 * PASS])
+        gather(PAIR, 0, S - CHUNK, late_first[:, 0, :])
+
+        gather_last_plane(0)
+        gather_last_plane(1)
+        round_late(0, False)
+        gather_last_plane(2)
+        quantize_x(0)
+        scratch = psum.tile([P, CHUNK], F32, name="scratch", tag="bank")
+        for repeat in range(WARM_PASSES):
+            nc.tensor.matmul_mx(
+                out=scratch[:],
+                lhsT=x_codes[:, 0:P].bitcast(FP8X4),
+                lhsT_scale=x_scales[:, 0:P],
+                rhs=x_codes[:, 0:CHUNK].bitcast(FP8X4),
+                rhs_scale=x_scales[:, 0:CHUNK],
+                start=True,
+                stop=True,
+            )
+
+        round_w1(0, 0, False)
+        round_late(1, True)
+        round_w1(0, PAIR, True)
+        w2_codes = shared.tile([P, PASSES, 2 * M], U8, name="w2_codes", align_bytes=ALIGN, offset=LATE_BYTES)
+        nc.sync.dma_start(w2_codes[:].bitcast(I32), w2_words.bitcast(I32).rearrange("a p n -> p a n"))
+        round_late(2, True)
+        round_w1(1, PAIR, True)
+        quantize_x(1)
+        quantize_w1(0, 0, PACK)
+
+        late_last = shared.tile([P, PAIR, CHUNK], F32, name="late_last", align_bytes=ALIGN, offset=0)
+        late.append(late_last[:])
+        gather(PAIR, S - CHUNK, CHUNK, late_last[:, 0, :])
+        round_w1(1, 0, False)
+        quantize_x(2)
+        quantize_w1(1, 0, PAIR)
+        quantize_w1(1, PAIR, PAIR)
+        gather_last_plane(CHUNKS - 1)
+        round_late(CHUNKS - 1, False)
+        quantize_x(CHUNKS - 1)
+
+        for b in range(EARLY_TILES - 1):
+            first_layer(0, b, True)
+        for b in range(EARLY_TILES):
+            if b == VECTOR_JOINS:
+                first_layer(0, EARLY_TILES - 1, False)
+            first_layer(1, b, b > 0)
+            quantize_h(b, 0, PASSES)
+
+        last = TILES - 1
+        output_tile(0, True)
+        for a in range(PASSES):
+            first_layer(a, last - 1, False)
+        quantize_h(last - 1, 0, PASSES)
+        first_layer(0, last, False)
+        quantize_h(last, 0, 1)
+        output_tile(1, True)
+        first_layer(1, last, False)
+        quantize_h(last, 1, 1)
+        for b in range(2, last):
+            output_tile(b, b < EARLY_TILES)
+
+        sides = [psum.tile([P, M // 2], F32, name="y_acc", tag="bank") for side in range(2)]
+        for a in range(PASSES):
+            for n0 in range(0, M, P):
+                side, lo = divmod(n0, M // 2)
+                second_layer_pass(sides[side][:, lo : lo + P], last, a, n0, P, a == 0 and lo == 0, a == PASSES - 1 and lo > 0)
+        for side in range(2):
+            copy_out(y[last][:, side * M // 2 : (side + 1) * M // 2], sides[side], side == 1)
+        store(last)

@@ -94,7 +94,7 @@ def tile_list_hmlp_tm_none_kernel(tc, xT, w1, w2_words, w2_scales, wgt, offs, ou
         x_bf = keep.tile([P, S * PACK], BF16, name="x_bf", align_bytes=ALIGN)
         x_codes = keep.tile([P, S], U32, name="x_codes", align_bytes=ALIGN)
         x_scales = keep.tile([P, S], U8, name="x_scales", align_bytes=ALIGN)
-        w1_bf = [keep.tile([P, PASS * PACK], BF16, name=f"w1_bf{a}", align_bytes=ALIGN) for a in range(PASSES)]
+        w1_bf = [keep.tile([P, PASS * PACK], BF16, name="w1_bf0", align_bytes=ALIGN)]
         w1_codes = [keep.tile([P, PASS], U32, name=f"w1_codes{a}", align_bytes=ALIGN) for a in range(PASSES)]
         w1_scales = [keep.tile([P, PASS], U8, name=f"w1_scales{a}", align_bytes=ALIGN) for a in range(PASSES)]
         h_bf = [keep.tile([P, PASSES, TILE * PACK], BF16, name=f"h_bf{b}", align_bytes=ALIGN) for b in range(TILES)]
@@ -197,8 +197,8 @@ def tile_list_hmlp_tm_none_kernel(tc, xT, w1, w2_words, w2_scales, wgt, offs, ou
         w1_rows = w1.rearrange("(p i) r -> p i r", i=PACK)
         w1_raw = [shared.tile([P, PACK, PASS], F32, name=f"w1_raw{a}", align_bytes=ALIGN, offset=a * RAW_BYTES) for a in range(PASSES)]
         nc.scalar.dma_start(w1_raw[0][:], w1_rows[:, :, 0:PASS])
-        round_x(early_rest[:], CHUNK, S - CHUNK, 0, True)
         nc.scalar.dma_start(w1_raw[1][:], w1_rows[:, :, PASS : 2 * PASS])
+        round_x(early_rest[:], CHUNK, S - CHUNK, 0, True)
         gather(PAIR, 0, S - CHUNK, late_first[:, 0, :])
 
         gather_last_plane(0)
@@ -224,6 +224,7 @@ def tile_list_hmlp_tm_none_kernel(tc, xT, w1, w2_words, w2_scales, wgt, offs, ou
         w2_codes = shared.tile([P, PASSES, 2 * M], U8, name="w2_codes", align_bytes=ALIGN, offset=LATE_BYTES)
         nc.sync.dma_start(w2_codes[:].bitcast(I32), w2_words.bitcast(I32).rearrange("a p n -> p a n"))
         round_late(2, True)
+        w1_bf.append(shared.tile([P, PASS * PACK], BF16, name="w1_bf1", align_bytes=ALIGN, offset=RAW_BYTES // 2))
         round_w1(1, PAIR, True)
         quantize_x(1)
         quantize_w1(0, 0, PACK)

@@ -30,12 +30,16 @@ TILE = 128
 TILES = S // TILE
 CHUNK = 256
 CHUNKS = S // CHUNK
-RUN = S // GROUP
+RUN = 128
+RUNS = S // RUN
+SEED_START = 7 * S - RUN
 HALF = S // 2
 RAW_BYTES = PACK * PASS * 4
 LATE_BYTES = PAIR * CHUNK * 4
 ALIGN = 256
-WARM_PASSES = 6
+SCALAR_M = 96
+RAW_AT = LATE_BYTES
+WARM_PASSES = 2
 EARLY_TILES = TILES - CHUNK // TILE
 VECTOR_JOINS = 3
 
@@ -49,11 +53,10 @@ def tile_list_hmlp_tm_none_kernel(tc, xT, w1, w2_words, w2_scales, wgt, offs, ou
 
         seeds = keep.tile([P, RUN], F32, name="seeds", align_bytes=ALIGN)
         wgt_flat = wgt.rearrange("p s -> (p s)")
-        for quad in range(P // QUAD):
-            first = (QUAD * quad + 1) * S
-            steps = wgt_flat[first : first + QUAD * (S - RUN)].rearrange("(p x) -> p x", x=S - RUN)
-            queue = nc.sync if quad % 2 == 0 else nc.scalar
-            queue.dma_start(seeds[QUAD * quad : QUAD * (quad + 1), :], steps[:, 0:RUN])
+        for side, queue in enumerate((nc.sync, nc.scalar)):
+            first = side * (P // 2) * S + SEED_START
+            steps = wgt_flat[first : first + (P // 2) * (S - RUN)].rearrange("(p x) -> p x", x=S - RUN)
+            queue.dma_start(seeds[side * P // 2 : (side + 1) * P // 2, :], steps[:, 0:RUN])
 
         offsets = keep.tile([P, S // GROUP], U16, name="offsets")
         x_rows = xT.rearrange("(p i) c -> p i c", i=PACK)
@@ -63,37 +66,28 @@ def tile_list_hmlp_tm_none_kernel(tc, xT, w1, w2_words, w2_scales, wgt, offs, ou
         for i in range(1, PACK):
             nc.sync.dma_start(planes[i][:], x_rows[:, i, :])
 
-        w2_exps = keep.tile([P, PASSES, M], U8, name="w2_exps", align_bytes=ALIGN)
-        nc.vector.memset(w2_exps[:].bitcast(I32), 0)
-        scale_rows = w2_scales.bitcast(I32).rearrange("a q n -> q a n")
-        for quad in range(P // QUAD):
-            rows = slice(BLOCKS * quad, BLOCKS * (quad + 1))
-            nc.sync.dma_start(w2_exps[QUAD * quad : QUAD * quad + BLOCKS, :, :].bitcast(I32), scale_rows[rows, :, :])
-
         turned = keep.tile([P, RUN // QUAD, QUAD], F32, name="turned", align_bytes=ALIGN)
         spread = keep.tile([P, S], F32, name="spread", align_bytes=ALIGN)
         weights = keep.tile([P, S], F32, name="weights", align_bytes=ALIGN)
-        for s in range(RUN // QUAD):
-            nc.vector.transpose(turned[:, s, :], seeds[:, QUAD * s : QUAD * (s + 1)])
+        nc.vector.transpose(turned[:].rearrange("p s u -> p (s u)"), seeds[:])
         by_source = turned[:].rearrange("p s (g u) -> p u s g", u=GROUP)
         by_run = spread[:].rearrange("p (v s g e) -> p v s g e", s=RUN // QUAD, g=QUAD // GROUP, e=GROUP)
 
         def repeated(sources, count):
             return by_source[:, sources].unsqueeze(4).to_broadcast([P, count, RUN // QUAD, QUAD // GROUP, GROUP])
 
-        nc.vector.tensor_copy(by_run[:, 0:1], repeated(slice(0, 1), 1))
-        nc.vector.tensor_copy(by_run[:, 1:8], repeated(slice(15, 8, -1), 7))
-        nc.scalar.copy(by_run[:, 8:16], repeated(slice(8, 0, -1), 8))
+        nc.vector.tensor_copy(by_run[:, 0:4], repeated(slice(7, 3, -1), 4))
+        nc.scalar.copy(by_run[:, 4:8], repeated(slice(3, None, -1), 4))
         nc.vector.transpose(weights[:, 0:HALF], spread[:, 0:HALF])
         nc.vector.transpose(weights[:, HALF:S], spread[:, HALF:S])
 
-        early_first = shared.tile([P, PAIR, CHUNK], F32, name="early_first", align_bytes=ALIGN, offset=RAW_BYTES - ALIGN)
+        early_first = shared.tile([P, PAIR, CHUNK], F32, name="early_first", align_bytes=ALIGN, offset=RAW_AT + RAW_BYTES - ALIGN)
         early_rest = keep.tile([P, PAIR, S - CHUNK], F32, name="early_rest")
         late_first = keep.tile([P, PAIR, S - CHUNK], F32, name="late_first")
         late = [late_first[:, :, c * CHUNK : (c + 1) * CHUNK] for c in range(CHUNKS - 1)]
         x_bf = keep.tile([P, S * PACK], BF16, name="x_bf", align_bytes=ALIGN)
         x_codes = keep.tile([P, S], U32, name="x_codes", align_bytes=ALIGN)
-        x_scales = keep.tile([P, S], U8, name="x_scales", align_bytes=ALIGN)
+        x_scales = {c: keep.tile([P, CHUNK], U8, name=f"x_scales{c}", align_bytes=ALIGN) for c in range(CHUNKS) if c != 1}
         w1_bf = [keep.tile([P, PASS * PACK], BF16, name="w1_bf0", align_bytes=ALIGN)]
         w1_codes = [keep.tile([P, PASS], U32, name=f"w1_codes{a}", align_bytes=ALIGN) for a in range(PASSES)]
         w1_scales = [keep.tile([P, PASS], U8, name=f"w1_scales{a}", align_bytes=ALIGN) for a in range(PASSES)]
@@ -124,11 +118,11 @@ def tile_list_hmlp_tm_none_kernel(tc, xT, w1, w2_words, w2_scales, wgt, offs, ou
 
         def quantize_x(c):
             cols = slice(c * CHUNK, (c + 1) * CHUNK)
-            nc.vector.quantize_mx(x_codes[:, cols].bitcast(FP8X4), x_scales[:, cols], x_bf[:, c * CHUNK * PACK : (c + 1) * CHUNK * PACK])
+            nc.vector.quantize_mx(x_codes[:, cols].bitcast(FP8X4), x_scales[c][:], x_bf[:, c * CHUNK * PACK : (c + 1) * CHUNK * PACK])
 
-        def round_w1(a, t0, on_scalar):
-            src = w1_raw[a][:].rearrange("p i (m t) -> p m i t", t=PACK)[:, :, :, t0 : t0 + PAIR]
-            dst = w1_bf[a][:].rearrange("p (t m i) -> p m i t", t=PACK, i=PACK)[:, :, :, t0 : t0 + PAIR]
+        def round_w1(a, t0, on_scalar, ms=slice(0, P)):
+            src = w1_raw[a][:].rearrange("p i (m t) -> p m i t", t=PACK)[:, ms, :, t0 : t0 + PAIR]
+            dst = w1_bf[a][:].rearrange("p (t m i) -> p m i t", t=PACK, i=PACK)[:, ms, :, t0 : t0 + PAIR]
             cast(dst, src, on_scalar)
 
         def quantize_w1(a, t0, count):
@@ -144,7 +138,7 @@ def tile_list_hmlp_tm_none_kernel(tc, xT, w1, w2_words, w2_scales, wgt, offs, ou
                     lhsT=w1_codes[a][:, t * P : (t + 1) * P].bitcast(FP8X4),
                     lhsT_scale=w1_scales[a][:, t * P : (t + 1) * P],
                     rhs=x_codes[:, tokens].bitcast(FP8X4),
-                    rhs_scale=x_scales[:, tokens],
+                    rhs_scale=x_scales[b // 2][:, b % 2 * TILE : (b % 2 + 1) * TILE],
                     start=True,
                     stop=True,
                 )
@@ -195,25 +189,31 @@ def tile_list_hmlp_tm_none_kernel(tc, xT, w1, w2_words, w2_scales, wgt, offs, ou
             gather(i, CHUNK, S - CHUNK, early_rest[:, i, :])
         round_x(early_first[:], 0, CHUNK, 0, True)
         w1_rows = w1.rearrange("(p i) r -> p i r", i=PACK)
-        w1_raw = [shared.tile([P, PACK, PASS], F32, name=f"w1_raw{a}", align_bytes=ALIGN, offset=a * RAW_BYTES) for a in range(PASSES)]
+        w1_raw = [shared.tile([P, PACK, PASS], F32, name=f"w1_raw{a}", align_bytes=ALIGN, offset=RAW_AT + a * (RAW_BYTES + PASSES * M)) for a in range(PASSES)]
         nc.scalar.dma_start(w1_raw[0][:], w1_rows[:, :, 0:PASS])
         nc.scalar.dma_start(w1_raw[1][:], w1_rows[:, :, PASS : 2 * PASS])
+        w2_exps = shared.tile([P, PASSES, M], U8, name="w2_exps", align_bytes=ALIGN, offset=RAW_AT + RAW_BYTES)
+        scale_rows = w2_scales.bitcast(I32).rearrange("a q n -> q a n")
+        for quad in range(P // QUAD):
+            rows = slice(BLOCKS * quad, BLOCKS * (quad + 1))
+            nc.scalar.dma_start(w2_exps[QUAD * quad : QUAD * quad + BLOCKS, :, :].bitcast(I32), scale_rows[rows, :, :])
+
         round_x(early_rest[:], CHUNK, S - CHUNK, 0, True)
         gather(PAIR, 0, S - CHUNK, late_first[:, 0, :])
 
-        gather_last_plane(0)
         gather_last_plane(1)
-        round_late(0, False)
+        gather_last_plane(0)
         gather_last_plane(2)
+        round_late(0, False)
         quantize_x(0)
         scratch = psum.tile([P, CHUNK], F32, name="scratch", tag="bank")
         for repeat in range(WARM_PASSES):
             nc.tensor.matmul_mx(
                 out=scratch[:],
                 lhsT=x_codes[:, 0:P].bitcast(FP8X4),
-                lhsT_scale=x_scales[:, 0:P],
+                lhsT_scale=x_scales[0][:, 0:P],
                 rhs=x_codes[:, 0:CHUNK].bitcast(FP8X4),
-                rhs_scale=x_scales[:, 0:CHUNK],
+                rhs_scale=x_scales[0][:],
                 start=True,
                 stop=True,
             )
@@ -221,18 +221,21 @@ def tile_list_hmlp_tm_none_kernel(tc, xT, w1, w2_words, w2_scales, wgt, offs, ou
         round_w1(0, 0, False)
         round_late(1, True)
         round_w1(0, PAIR, True)
-        w2_codes = shared.tile([P, PASSES, 2 * M], U8, name="w2_codes", align_bytes=ALIGN, offset=LATE_BYTES)
+        w2_codes = shared.tile([P, PASSES, 2 * M], U8, name="w2_codes", align_bytes=ALIGN, offset=ALIGN + LATE_BYTES)
         nc.sync.dma_start(w2_codes[:].bitcast(I32), w2_words.bitcast(I32).rearrange("a p n -> p a n"))
         round_late(2, True)
-        w1_bf.append(shared.tile([P, PASS * PACK], BF16, name="w1_bf1", align_bytes=ALIGN, offset=RAW_BYTES // 2))
-        round_w1(1, PAIR, True)
+        w1_bf.append(shared.tile([P, PASS * PACK], BF16, name="w1_bf1", align_bytes=ALIGN, offset=2 * ALIGN + 2 * LATE_BYTES))
+        round_w1(1, PAIR, True, slice(0, SCALAR_M))
+        x_scales[1] = shared.tile([P, CHUNK], U8, name="x_scales1", align_bytes=ALIGN, offset=ALIGN + 2 * LATE_BYTES)
+        quantize_w1(0, 0, PAIR)
+        quantize_w1(0, PAIR, PAIR)
         quantize_x(1)
-        quantize_w1(0, 0, PACK)
 
-        late_last = shared.tile([P, PAIR, CHUNK], F32, name="late_last", align_bytes=ALIGN, offset=0)
+        late_last = shared.tile([P, PAIR, CHUNK], F32, name="late_last", align_bytes=ALIGN, offset=ALIGN)
         late.append(late_last[:])
         gather(PAIR, S - CHUNK, CHUNK, late_last[:, 0, :])
         round_w1(1, 0, False)
+        round_w1(1, PAIR, False, slice(SCALAR_M, P))
         quantize_x(2)
         quantize_w1(1, 0, PAIR)
         quantize_w1(1, PAIR, PAIR)

@@ -30,15 +30,18 @@ TILE = 128
 TILES = S // TILE
 CHUNK = 256
 CHUNKS = S // CHUNK
-RUN = 128
-RUNS = S // RUN
-SEED_START = 7 * S - RUN
+RUN = S // GROUP
 HALF = S // 2
 RAW_BYTES = PACK * PASS * 4
 LATE_BYTES = PAIR * CHUNK * 4
 ALIGN = 256
-SCALAR_M = 96
 RAW_AT = LATE_BYTES
+LATE_LAST_AT = ALIGN
+W2_CODES_AT = LATE_LAST_AT + LATE_BYTES
+X_SCALES_AT = W2_CODES_AT + PASSES * 2 * M
+W1_ROUNDED_AT = X_SCALES_AT + CHUNK
+HELD_CHUNK = 1
+SCALAR_M = 96
 WARM_PASSES = 2
 EARLY_TILES = TILES - CHUNK // TILE
 VECTOR_JOINS = 3
@@ -53,10 +56,11 @@ def tile_list_hmlp_tm_none_kernel(tc, xT, w1, w2_words, w2_scales, wgt, offs, ou
 
         seeds = keep.tile([P, RUN], F32, name="seeds", align_bytes=ALIGN)
         wgt_flat = wgt.rearrange("p s -> (p s)")
-        for side, queue in enumerate((nc.sync, nc.scalar)):
-            first = side * (P // 2) * S + SEED_START
-            steps = wgt_flat[first : first + (P // 2) * (S - RUN)].rearrange("(p x) -> p x", x=S - RUN)
-            queue.dma_start(seeds[side * P // 2 : (side + 1) * P // 2, :], steps[:, 0:RUN])
+        for quad in range(P // QUAD):
+            start = (QUAD * quad + 1) * S
+            steps = wgt_flat[start : start + QUAD * (S - RUN)].rearrange("(p x) -> p x", x=S - RUN)
+            queue = nc.sync if quad % 2 == 0 else nc.scalar
+            queue.dma_start(seeds[QUAD * quad : QUAD * (quad + 1), :], steps[:, 0:RUN])
 
         offsets = keep.tile([P, S // GROUP], U16, name="offsets")
         x_rows = xT.rearrange("(p i) c -> p i c", i=PACK)
@@ -66,18 +70,27 @@ def tile_list_hmlp_tm_none_kernel(tc, xT, w1, w2_words, w2_scales, wgt, offs, ou
         for i in range(1, PACK):
             nc.sync.dma_start(planes[i][:], x_rows[:, i, :])
 
+        w2_exps = keep.tile([P, PASSES, M], U8, name="w2_exps", align_bytes=ALIGN)
+        nc.vector.memset(w2_exps[:].bitcast(I32), 0)
+        scale_rows = w2_scales.bitcast(I32).rearrange("a q n -> q a n")
+        for quad in range(P // QUAD):
+            rows = slice(BLOCKS * quad, BLOCKS * (quad + 1))
+            nc.sync.dma_start(w2_exps[QUAD * quad : QUAD * quad + BLOCKS, :, :].bitcast(I32), scale_rows[rows, :, :])
+
         turned = keep.tile([P, RUN // QUAD, QUAD], F32, name="turned", align_bytes=ALIGN)
         spread = keep.tile([P, S], F32, name="spread", align_bytes=ALIGN)
         weights = keep.tile([P, S], F32, name="weights", align_bytes=ALIGN)
-        nc.vector.transpose(turned[:].rearrange("p s u -> p (s u)"), seeds[:])
+        for s in range(RUN // QUAD):
+            nc.vector.transpose(turned[:, s, :], seeds[:, QUAD * s : QUAD * (s + 1)])
         by_source = turned[:].rearrange("p s (g u) -> p u s g", u=GROUP)
         by_run = spread[:].rearrange("p (v s g e) -> p v s g e", s=RUN // QUAD, g=QUAD // GROUP, e=GROUP)
 
         def repeated(sources, count):
             return by_source[:, sources].unsqueeze(4).to_broadcast([P, count, RUN // QUAD, QUAD // GROUP, GROUP])
 
-        nc.vector.tensor_copy(by_run[:, 0:4], repeated(slice(7, 3, -1), 4))
-        nc.scalar.copy(by_run[:, 4:8], repeated(slice(3, None, -1), 4))
+        nc.vector.tensor_copy(by_run[:, 0:1], repeated(slice(0, 1), 1))
+        nc.vector.tensor_copy(by_run[:, 1:8], repeated(slice(15, 8, -1), 7))
+        nc.scalar.copy(by_run[:, 8:16], repeated(slice(8, 0, -1), 8))
         nc.vector.transpose(weights[:, 0:HALF], spread[:, 0:HALF])
         nc.vector.transpose(weights[:, HALF:S], spread[:, HALF:S])
 
@@ -87,7 +100,7 @@ def tile_list_hmlp_tm_none_kernel(tc, xT, w1, w2_words, w2_scales, wgt, offs, ou
         late = [late_first[:, :, c * CHUNK : (c + 1) * CHUNK] for c in range(CHUNKS - 1)]
         x_bf = keep.tile([P, S * PACK], BF16, name="x_bf", align_bytes=ALIGN)
         x_codes = keep.tile([P, S], U32, name="x_codes", align_bytes=ALIGN)
-        x_scales = {c: keep.tile([P, CHUNK], U8, name=f"x_scales{c}", align_bytes=ALIGN) for c in range(CHUNKS) if c != 1}
+        x_scales = {c: keep.tile([P, CHUNK], U8, name=f"x_scales{c}", align_bytes=ALIGN) for c in range(CHUNKS) if c != HELD_CHUNK}
         w1_bf = [keep.tile([P, PASS * PACK], BF16, name="w1_bf0", align_bytes=ALIGN)]
         w1_codes = [keep.tile([P, PASS], U32, name=f"w1_codes{a}", align_bytes=ALIGN) for a in range(PASSES)]
         w1_scales = [keep.tile([P, PASS], U8, name=f"w1_scales{a}", align_bytes=ALIGN) for a in range(PASSES)]
@@ -132,13 +145,14 @@ def tile_list_hmlp_tm_none_kernel(tc, xT, w1, w2_words, w2_scales, wgt, offs, ou
         def first_layer(a, b, on_scalar):
             acc = psum.tile([P, PACK, TILE], F32, name="h_acc", tag="bank")
             tokens = slice(b * TILE, (b + 1) * TILE)
+            chunk, first = divmod(b * TILE, CHUNK)
             for t in range(PACK):
                 nc.tensor.matmul_mx(
                     out=acc[:, t, :],
                     lhsT=w1_codes[a][:, t * P : (t + 1) * P].bitcast(FP8X4),
                     lhsT_scale=w1_scales[a][:, t * P : (t + 1) * P],
                     rhs=x_codes[:, tokens].bitcast(FP8X4),
-                    rhs_scale=x_scales[b // 2][:, b % 2 * TILE : (b % 2 + 1) * TILE],
+                    rhs_scale=x_scales[chunk][:, first : first + TILE],
                     start=True,
                     stop=True,
                 )
@@ -189,21 +203,14 @@ def tile_list_hmlp_tm_none_kernel(tc, xT, w1, w2_words, w2_scales, wgt, offs, ou
             gather(i, CHUNK, S - CHUNK, early_rest[:, i, :])
         round_x(early_first[:], 0, CHUNK, 0, True)
         w1_rows = w1.rearrange("(p i) r -> p i r", i=PACK)
-        w1_raw = [shared.tile([P, PACK, PASS], F32, name=f"w1_raw{a}", align_bytes=ALIGN, offset=RAW_AT + a * (RAW_BYTES + PASSES * M)) for a in range(PASSES)]
+        w1_raw = [shared.tile([P, PACK, PASS], F32, name=f"w1_raw{a}", align_bytes=ALIGN, offset=RAW_AT + a * RAW_BYTES) for a in range(PASSES)]
         nc.scalar.dma_start(w1_raw[0][:], w1_rows[:, :, 0:PASS])
         nc.scalar.dma_start(w1_raw[1][:], w1_rows[:, :, PASS : 2 * PASS])
-        w2_exps = shared.tile([P, PASSES, M], U8, name="w2_exps", align_bytes=ALIGN, offset=RAW_AT + RAW_BYTES)
-        scale_rows = w2_scales.bitcast(I32).rearrange("a q n -> q a n")
-        for quad in range(P // QUAD):
-            rows = slice(BLOCKS * quad, BLOCKS * (quad + 1))
-            nc.scalar.dma_start(w2_exps[QUAD * quad : QUAD * quad + BLOCKS, :, :].bitcast(I32), scale_rows[rows, :, :])
-
         round_x(early_rest[:], CHUNK, S - CHUNK, 0, True)
         gather(PAIR, 0, S - CHUNK, late_first[:, 0, :])
 
-        gather_last_plane(1)
-        gather_last_plane(0)
-        gather_last_plane(2)
+        for c in (1, 0, 2):
+            gather_last_plane(c)
         round_late(0, False)
         quantize_x(0)
         scratch = psum.tile([P, CHUNK], F32, name="scratch", tag="bank")
@@ -221,17 +228,17 @@ def tile_list_hmlp_tm_none_kernel(tc, xT, w1, w2_words, w2_scales, wgt, offs, ou
         round_w1(0, 0, False)
         round_late(1, True)
         round_w1(0, PAIR, True)
-        w2_codes = shared.tile([P, PASSES, 2 * M], U8, name="w2_codes", align_bytes=ALIGN, offset=ALIGN + LATE_BYTES)
+        w2_codes = shared.tile([P, PASSES, 2 * M], U8, name="w2_codes", align_bytes=ALIGN, offset=W2_CODES_AT)
         nc.sync.dma_start(w2_codes[:].bitcast(I32), w2_words.bitcast(I32).rearrange("a p n -> p a n"))
         round_late(2, True)
-        w1_bf.append(shared.tile([P, PASS * PACK], BF16, name="w1_bf1", align_bytes=ALIGN, offset=2 * ALIGN + 2 * LATE_BYTES))
+        w1_bf.append(shared.tile([P, PASS * PACK], BF16, name="w1_bf1", align_bytes=ALIGN, offset=W1_ROUNDED_AT))
         round_w1(1, PAIR, True, slice(0, SCALAR_M))
-        x_scales[1] = shared.tile([P, CHUNK], U8, name="x_scales1", align_bytes=ALIGN, offset=ALIGN + 2 * LATE_BYTES)
+        x_scales[HELD_CHUNK] = shared.tile([P, CHUNK], U8, name=f"x_scales{HELD_CHUNK}", align_bytes=ALIGN, offset=X_SCALES_AT)
         quantize_w1(0, 0, PAIR)
         quantize_w1(0, PAIR, PAIR)
-        quantize_x(1)
+        quantize_x(HELD_CHUNK)
 
-        late_last = shared.tile([P, PAIR, CHUNK], F32, name="late_last", align_bytes=ALIGN, offset=ALIGN)
+        late_last = shared.tile([P, PAIR, CHUNK], F32, name="late_last", align_bytes=ALIGN, offset=LATE_LAST_AT)
         late.append(late_last[:])
         gather(PAIR, S - CHUNK, CHUNK, late_last[:, 0, :])
         round_w1(1, 0, False)

@@ -42,7 +42,6 @@ X_SCALES_AT = W2_CODES_AT + PASSES * 2 * M
 W1_ROUNDED_AT = X_SCALES_AT + CHUNK
 HELD_CHUNK = 1
 SCALAR_M = 96
-WARM_PASSES = 2
 EARLY_TILES = TILES - CHUNK // TILE
 VECTOR_JOINS = 3
 
@@ -213,17 +212,6 @@ def tile_list_hmlp_tm_none_kernel(tc, xT, w1, w2_words, w2_scales, wgt, offs, ou
             gather_last_plane(c)
         round_late(0, False)
         quantize_x(0)
-        scratch = psum.tile([P, CHUNK], F32, name="scratch", tag="bank")
-        for repeat in range(WARM_PASSES):
-            nc.tensor.matmul_mx(
-                out=scratch[:],
-                lhsT=x_codes[:, 0:P].bitcast(FP8X4),
-                lhsT_scale=x_scales[0][:, 0:P],
-                rhs=x_codes[:, 0:CHUNK].bitcast(FP8X4),
-                rhs_scale=x_scales[0][:],
-                start=True,
-                stop=True,
-            )
 
         round_w1(0, 0, False)
         round_late(1, True)

@@ -17,6 +17,7 @@ MULT = mybir.AluOpType.mult
 MAX = mybir.AluOpType.max
 RELU = mybir.ActivationFunctionType.Relu
 COPY = mybir.ActivationFunctionType.Copy
+IDENTITY = mybir.ActivationFunctionType.Identity
 
 P = 128
 QUAD = 32
@@ -71,10 +72,7 @@ def tile_list_hmlp_tm_none_kernel(tc, xT, w1, w2_words, w2_scales, wgt, offs, ou
 
         w2_exps = keep.tile([P, PASSES, M], U8, name="w2_exps", align_bytes=ALIGN)
         nc.vector.memset(w2_exps[:].bitcast(I32), 0)
-        scale_rows = w2_scales.bitcast(I32).rearrange("a q n -> q a n")
-        for quad in range(P // QUAD):
-            rows = slice(BLOCKS * quad, BLOCKS * (quad + 1))
-            nc.sync.dma_start(w2_exps[QUAD * quad : QUAD * quad + BLOCKS, :, :].bitcast(I32), scale_rows[rows, :, :])
+        zero = w2_exps[:, 0, 0:4].bitcast(F32)
 
         turned = keep.tile([P, RUN // QUAD, QUAD], F32, name="turned", align_bytes=ALIGN)
         spread = keep.tile([P, S], F32, name="spread", align_bytes=ALIGN)
@@ -205,7 +203,12 @@ def tile_list_hmlp_tm_none_kernel(tc, xT, w1, w2_words, w2_scales, wgt, offs, ou
         w1_raw = [shared.tile([P, PACK, PASS], F32, name=f"w1_raw{a}", align_bytes=ALIGN, offset=RAW_AT + a * RAW_BYTES) for a in range(PASSES)]
         nc.scalar.dma_start(w1_raw[0][:], w1_rows[:, :, 0:PASS])
         nc.scalar.dma_start(w1_raw[1][:], w1_rows[:, :, PASS : 2 * PASS])
-        round_x(early_rest[:], CHUNK, S - CHUNK, 0, True)
+        early_dst = x_bf[:].rearrange("p (n i) -> p n i", i=PACK)[:, CHUNK:S, 0:PAIR]
+        nc.scalar.activation(early_dst, early_rest[:].rearrange("p i n -> p n i"), IDENTITY, bias=zero)
+        scale_rows = w2_scales.bitcast(I32).rearrange("a q n -> q a n")
+        for quad in range(P // QUAD):
+            rows = slice(BLOCKS * quad, BLOCKS * (quad + 1))
+            nc.sync.dma_start(w2_exps[QUAD * quad : QUAD * quad + BLOCKS, :, :].bitcast(I32), scale_rows[rows, :, :])
         gather(PAIR, 0, S - CHUNK, late_first[:, 0, :])
 
         for c in (1, 0, 2):

from contextlib import ExitStack

import concourse.mybir as mybir

K, H, M, T, S = 512, 1024, 512, 2048, 1024
FLOPS = 2 * K * H * S + 2 * H * M * S

F32 = mybir.dt.float32
BF16 = mybir.dt.bfloat16
I32 = mybir.dt.int32
U32 = mybir.dt.uint32
U16 = mybir.dt.uint16
U8 = mybir.dt.uint8
FP8X4 = mybir.dt.float8_e4m3fn_x4
FP4X4 = mybir.dt.float4_e2m1fn_x4
MULT = mybir.AluOpType.mult
MAX = mybir.AluOpType.max
RELU = mybir.ActivationFunctionType.Relu
COPY = mybir.ActivationFunctionType.Copy
IDENTITY = mybir.ActivationFunctionType.Identity

P = 128
QUAD = 32
GROUP = 16
PACK = 4
BLOCKS = 4
PAIR = 2
PASS = P * PACK
PASSES = H // PASS
TILE = 128
TILES = S // TILE
CHUNK = 256
CHUNKS = S // CHUNK
RUN = S // GROUP
HALF = S // 2
RAW_BYTES = PACK * PASS * 4
LATE_BYTES = PAIR * CHUNK * 4
ALIGN = 256
RAW_AT = LATE_BYTES
LATE_LAST_AT = ALIGN
W2_CODES_AT = LATE_LAST_AT + LATE_BYTES
X_SCALES_AT = W2_CODES_AT + PASSES * 2 * M
W1_ROUNDED_AT = X_SCALES_AT + CHUNK
HELD_CHUNK = 1
SCALAR_M = 96
EARLY_TILES = TILES - CHUNK // TILE
VECTOR_JOINS = 3


def tile_list_hmlp_tm_none_kernel(tc, xT, w1, w2_words, w2_scales, wgt, offs, out):
    nc = tc.nc
    with ExitStack() as ctx:
        keep = ctx.enter_context(tc.tile_pool(name="keep", bufs=1))
        shared = ctx.enter_context(tc.tile_pool(name="shared", bufs=1))
        psum = ctx.enter_context(tc.psum_pool(name="psum", bufs=8))

        seeds = keep.tile([P, RUN], F32, name="seeds", align_bytes=ALIGN)
        wgt_flat = wgt.rearrange("p s -> (p s)")
        for quad in range(P // QUAD):
            start = (QUAD * quad + 1) * S
            steps = wgt_flat[start : start + QUAD * (S - RUN)].rearrange("(p x) -> p x", x=S - RUN)
            queue = nc.sync if quad % 2 == 0 else nc.scalar
            queue.dma_start(seeds[QUAD * quad : QUAD * (quad + 1), :], steps[:, 0:RUN])

        offsets = keep.tile([P, S // GROUP], U16, name="offsets")
        x_rows = xT.rearrange("(p i) c -> p i c", i=PACK)
        planes = [keep.tile([P, T], F32, name=f"plane{i}", tag=f"plane{i}", align_bytes=ALIGN) for i in range(PACK)]
        nc.sync.dma_start(planes[0][:], x_rows[:, 0, :])
        nc.sync.dma_start(offsets[:], offs)
        for i in range(1, PACK):
            nc.sync.dma_start(planes[i][:], x_rows[:, i, :])

        w2_exps = keep.tile([P, PASSES, M], U8, name="w2_exps", align_bytes=ALIGN)
        nc.vector.memset(w2_exps[:].bitcast(I32), 0)
        zero = w2_exps[:, 0, 0:4].bitcast(F32)

        turned = keep.tile([P, RUN // QUAD, QUAD], F32, name="turned", align_bytes=ALIGN)
        spread = keep.tile([P, S], F32, name="spread", align_bytes=ALIGN)
        weights = keep.tile([P, S], F32, name="weights", align_bytes=ALIGN)
        for s in range(RUN // QUAD):
            nc.vector.transpose(turned[:, s, :], seeds[:, QUAD * s : QUAD * (s + 1)])
        by_source = turned[:].rearrange("p s (g u) -> p u s g", u=GROUP)
        by_run = spread[:].rearrange("p (v s g e) -> p v s g e", s=RUN // QUAD, g=QUAD // GROUP, e=GROUP)

        def repeated(sources, count):
            return by_source[:, sources].unsqueeze(4).to_broadcast([P, count, RUN // QUAD, QUAD // GROUP, GROUP])

        nc.vector.tensor_copy(by_run[:, 0:1], repeated(slice(0, 1), 1))
        nc.vector.tensor_copy(by_run[:, 1:8], repeated(slice(15, 8, -1), 7))
        nc.scalar.copy(by_run[:, 8:16], repeated(slice(8, 0, -1), 8))
        nc.vector.transpose(weights[:, 0:HALF], spread[:, 0:HALF])
        nc.vector.transpose(weights[:, HALF:S], spread[:, HALF:S])

        early_first = shared.tile([P, PAIR, CHUNK], F32, name="early_first", align_bytes=ALIGN, offset=RAW_AT + RAW_BYTES - ALIGN)
        early_rest = keep.tile([P, PAIR, S - CHUNK], F32, name="early_rest")
        late_first = keep.tile([P, PAIR, S - CHUNK], F32, name="late_first")
        late = [late_first[:, :, c * CHUNK : (c + 1) * CHUNK] for c in range(CHUNKS - 1)]
        x_bf = keep.tile([P, S * PACK], BF16, name="x_bf", align_bytes=ALIGN)
        x_codes = keep.tile([P, S], U32, name="x_codes", align_bytes=ALIGN)
        x_scales = {c: keep.tile([P, CHUNK], U8, name=f"x_scales{c}", align_bytes=ALIGN) for c in range(CHUNKS) if c != HELD_CHUNK}
        w1_bf = [keep.tile([P, PASS * PACK], BF16, name="w1_bf0", align_bytes=ALIGN)]
        w1_codes = [keep.tile([P, PASS], U32, name=f"w1_codes{a}", align_bytes=ALIGN) for a in range(PASSES)]
        w1_scales = [keep.tile([P, PASS], U8, name=f"w1_scales{a}", align_bytes=ALIGN) for a in range(PASSES)]
        h_bf = [keep.tile([P, PASSES, TILE * PACK], BF16, name=f"h_bf{b}", align_bytes=ALIGN) for b in range(TILES)]
        h_codes = [keep.tile([P, PASSES, TILE], U32, name=f"h_codes{b}", align_bytes=ALIGN) for b in range(TILES)]
        h_scales = [keep.tile([P, PASSES, TILE], U8, name=f"h_scales{b}", align_bytes=ALIGN) for b in range(TILES)]
        y = [keep.tile([P, M], F32, name=f"y{b}", align_bytes=ALIGN) for b in range(TILES)]

        def cast(dst, src, on_scalar):
            if on_scalar:
                nc.scalar.activation(dst, src, COPY)
            else:
                nc.vector.tensor_copy(dst, src)

        def gather(i, j0, n, dst):
            window = planes[i][:].indirect(offsets[:, j0 // GROUP : (j0 + n) // GROUP])
            nc.vector.tensor_tensor(dst, window, weights[:, j0 : j0 + n], MULT)

        def round_x(src, j0, n, i0, on_scalar):
            dst = x_bf[:].rearrange("p (n i) -> p n i", i=PACK)[:, j0 : j0 + n, i0 : i0 + PAIR]
            cast(dst, src.rearrange("p i n -> p n i"), on_scalar)

        def gather_last_plane(c):
            gather(PACK - 1, c * CHUNK, CHUNK, late[c][:, PAIR - 1, :])

        def round_late(c, on_scalar):
            round_x(late[c], c * CHUNK, CHUNK, PAIR, on_scalar)

        def quantize_x(c):
            cols = slice(c * CHUNK, (c + 1) * CHUNK)
            nc.vector.quantize_mx(x_codes[:, cols].bitcast(FP8X4), x_scales[c][:], x_bf[:, c * CHUNK * PACK : (c + 1) * CHUNK * PACK])

        def round_w1(a, t0, on_scalar, ms=slice(0, P)):
            src = w1_raw[a][:].rearrange("p i (m t) -> p m i t", t=PACK)[:, ms, :, t0 : t0 + PAIR]
            dst = w1_bf[a][:].rearrange("p (t m i) -> p m i t", t=PACK, i=PACK)[:, ms, :, t0 : t0 + PAIR]
            cast(dst, src, on_scalar)

        def quantize_w1(a, t0, count):
            cols = slice(t0 * P, (t0 + count) * P)
            nc.vector.quantize_mx(w1_codes[a][:, cols].bitcast(FP8X4), w1_scales[a][:, cols], w1_bf[a][:, t0 * PASS : (t0 + count) * PASS])

        def first_layer(a, b, on_scalar):
            acc = psum.tile([P, PACK, TILE], F32, name="h_acc", tag="bank")
            tokens = slice(b * TILE, (b + 1) * TILE)
            chunk, first = divmod(b * TILE, CHUNK)
            for t in range(PACK):
                nc.tensor.matmul_mx(
                    out=acc[:, t, :],
                    lhsT=w1_codes[a][:, t * P : (t + 1) * P].bitcast(FP8X4),
                    lhsT_scale=w1_scales[a][:, t * P : (t + 1) * P],
                    rhs=x_codes[:, tokens].bitcast(FP8X4),
                    rhs_scale=x_scales[chunk][:, first : first + TILE],
                    start=True,
                    stop=True,
                )
            dst = h_bf[b][:, a, :].rearrange("p (n t) -> p n t", t=PACK)
            src = acc[:].rearrange("p t n -> p n t")
            if on_scalar:
                nc.scalar.activation(dst, src, RELU)
            else:
                nc.vector.tensor_scalar(dst, src, 0.0, None, MAX)

        def quantize_h(b, a0, count):
            passes = slice(a0, a0 + count)
            nc.vector.quantize_mx(
                h_codes[b][:, passes, :].rearrange("p a n -> p (a n)").bitcast(FP8X4),
                h_scales[b][:, passes, :].rearrange("p a n -> p (a n)"),
                h_bf[b][:, passes, :].rearrange("p a n -> p (a n)"),
            )

        def second_layer_pass(acc, b, a, n0, width, start, stop):
            nc.tensor.matmul_mx(
                out=acc,
                lhsT=h_codes[b][:, a, :].bitcast(FP8X4),
                lhsT_scale=h_scales[b][:, a, :],
                rhs=w2_codes[:, a, 2 * n0 : 2 * (n0 + width)].bitcast(FP4X4),
                rhs_scale=w2_exps[:, a, n0 : n0 + width],
                start=start,
                stop=stop,
            )

        def copy_out(dst, acc, on_scalar):
            if on_scalar:
                nc.scalar.copy(dst, acc[:])
            else:
                nc.vector.tensor_copy(dst, acc[:])

        def store(b):
            nc.sync.dma_start(out[b * TILE : (b + 1) * TILE, :], y[b][:])

        def output_tile(b, on_scalar):
            acc = psum.tile([P, M], F32, name="y_acc", tag="bank")
            for a in range(PASSES):
                second_layer_pass(acc[:], b, a, 0, M, a == 0, a == PASSES - 1)
            copy_out(y[b][:], acc, on_scalar)
            store(b)

        for i in range(PAIR):
            gather(i, 0, CHUNK, early_first[:, i, :])
            gather(i, CHUNK, S - CHUNK, early_rest[:, i, :])
        round_x(early_first[:], 0, CHUNK, 0, True)
        w1_rows = w1.rearrange("(p i) r -> p i r", i=PACK)
        w1_raw = [shared.tile([P, PACK, PASS], F32, name=f"w1_raw{a}", align_bytes=ALIGN, offset=RAW_AT + a * RAW_BYTES) for a in range(PASSES)]
        nc.scalar.dma_start(w1_raw[0][:], w1_rows[:, :, 0:PASS])
        nc.scalar.dma_start(w1_raw[1][:], w1_rows[:, :, PASS : 2 * PASS])
        early_dst = x_bf[:].rearrange("p (n i) -> p n i", i=PACK)[:, CHUNK:S, 0:PAIR]
        nc.scalar.activation(early_dst, early_rest[:].rearrange("p i n -> p n i"), IDENTITY, bias=zero)
        scale_rows = w2_scales.bitcast(I32).rearrange("a q n -> q a n")
        for quad in range(P // QUAD):
            rows = slice(BLOCKS * quad, BLOCKS * (quad + 1))
            nc.sync.dma_start(w2_exps[QUAD * quad : QUAD * quad + BLOCKS, :, :].bitcast(I32), scale_rows[rows, :, :])
        gather(PAIR, 0, S - CHUNK, late_first[:, 0, :])

        for c in (1, 0, 2):
            gather_last_plane(c)
        round_late(0, False)
        quantize_x(0)

        round_w1(0, 0, False)
        round_late(1, True)
        round_w1(0, PAIR, True)
        w2_codes = shared.tile([P, PASSES, 2 * M], U8, name="w2_codes", align_bytes=ALIGN, offset=W2_CODES_AT)
        nc.sync.dma_start(w2_codes[:].bitcast(I32), w2_words.bitcast(I32).rearrange("a p n -> p a n"))
        round_late(2, True)
        w1_bf.append(shared.tile([P, PASS * PACK], BF16, name="w1_bf1", align_bytes=ALIGN, offset=W1_ROUNDED_AT))
        round_w1(1, PAIR, True, slice(0, SCALAR_M))
        x_scales[HELD_CHUNK] = shared.tile([P, CHUNK], U8, name=f"x_scales{HELD_CHUNK}", align_bytes=ALIGN, offset=X_SCALES_AT)
        quantize_w1(0, 0, PAIR)
        quantize_w1(0, PAIR, PAIR)
        quantize_x(HELD_CHUNK)

        late_last = shared.tile([P, PAIR, CHUNK], F32, name="late_last", align_bytes=ALIGN, offset=LATE_LAST_AT)
        late.append(late_last[:])
        gather(PAIR, S - CHUNK, CHUNK, late_last[:, 0, :])
        round_w1(1, 0, False)
        round_w1(1, PAIR, False, slice(SCALAR_M, P))
        quantize_x(2)
        quantize_w1(1, 0, PAIR)
        quantize_w1(1, PAIR, PAIR)
        gather_last_plane(CHUNKS - 1)
        round_late(CHUNKS - 1, False)
        quantize_x(CHUNKS - 1)

        for b in range(EARLY_TILES - 1):
            first_layer(0, b, True)
        for b in range(EARLY_TILES):
            if b == VECTOR_JOINS:
                first_layer(0, EARLY_TILES - 1, False)
            first_layer(1, b, b > 0)
            quantize_h(b, 0, PASSES)

        last = TILES - 1
        output_tile(0, True)
        for a in range(PASSES):
            first_layer(a, last - 1, False)
        quantize_h(last - 1, 0, PASSES)
        first_layer(0, last, False)
        quantize_h(last, 0, 1)
        output_tile(1, True)
        first_layer(1, last, False)
        quantize_h(last, 1, 1)
        for b in range(2, last):
            output_tile(b, b < EARLY_TILES)

        sides = [psum.tile([P, M // 2], F32, name="y_acc", tag="bank") for side in range(2)]
        for a in range(PASSES):
            for n0 in range(0, M, P):
                side, lo = divmod(n0, M // 2)
                second_layer_pass(sides[side][:, lo : lo + P], last, a, n0, P, a == 0 and lo == 0, a == PASSES - 1 and lo > 0)
        for side in range(2):
            copy_out(y[last][:, side * M // 2 : (side + 1) * M // 2], sides[side], side == 1)
        store(last)
